import numpy as np, ml_dtypes
CORES = [10,34,74,98]
N = 4
BF = ml_dtypes.bfloat16
P, BK, W, SH, NB, EV = 256, 8192, 8, 3, 4096, 4
LV, AR, LIVE = 48, 64, 448
def group():
    return np.arange(8)[None, :, None]
def event(bm, cs, ls, e, sd, t):
    q = e >> 16; u = e & 65535; g = group()
    m = bm[q, g, u >> SH]; b = (m >> 5) + ((u & (W - 1)) >= (m & 31))
    c = cs.reshape(N, 8, 16, NB)[q, g, :, b]
    k = np.sum(c <= ((sd >> (4 * t)) & 4095)[..., None], axis=-1)
    return c, np.maximum(e - ls.reshape(N, 8, 16, NB)[q, g, k, b].astype(np.float32).astype(np.int64), 0)
def first(rng, key, on, cap):
    k = np.where(on, key, 9999); o = np.lexsort((rng.random(k.size), k)); s = k[o]; r = np.empty_like(o)
    r[o] = np.arange(s.size) - np.searchsorted(s, s); return on & (r < cap)
def plant(rng, d, u, sd):
    e = u + 65536 * np.arange(N)[:, None, None]; d["en"] = e.astype(np.int32); g = np.broadcast_to(group(), e.shape).ravel()
    for t in range(EV - 1):
        s = sd + (rng.integers(0, 16, sd.shape) << (8 + 4 * t)); v = event(d["bm"], d["cs"], d["ls"], e, s, t)[1]
        a = (e >> 16).ravel(); z = (v >> 16).ravel()
        ok = first(rng, z * 8 + g, first(rng, (a * N + z) * 8 + g, a != z, LV), AR)
        no = ((a != z) & ~ok).reshape(e.shape); sd = np.where(no, sd, s); e = np.where(no, e, v)
    d["sd"] = sd.astype(np.int32); return d
def sections(c):
    return c.reshape(N, 128, NB).astype(np.int32)
def losses(v):
    v[:, :, 0] = 0; return v.reshape(N, 128, NB).astype(np.float32).astype(BF)
def setup_inputs(rng):
    h = np.zeros((N, 8, BK), np.int64); h[:, :, -1] = 1
    np.put_along_axis(h[..., :-1], np.argsort(rng.random((N, 8, BK - 1)), axis=-1)[..., :NB - 2], 1, -1)
    bm = (np.cumsum(h, axis=-1) - h) * 32 + np.where(h == 1, rng.integers(0, W, h.shape), W)
    c = np.sort(rng.integers(256, 4097, (N, 8, 16, NB)), axis=2); c[:, :, 15] = rng.integers(4096, 8192, (N, 8, NB))
    v = rng.integers(0, 256, c.shape) << rng.integers(0, 10 + 1, c.shape)
    d = {"bm": bm.astype(np.int32), "cs": sections(c), "ls": losses(v), "en": None, "sd": None}
    return plant(rng, d, rng.integers(0, 65536, (N, 8, P)), rng.integers(0, 256, (N, 8, P)))
def setup_inputs_full(rng):
    d = setup_inputs(rng); v = losses(rng.integers(64, 256, (N, 8, 16, NB)) * 512); d["ls"][1:] = v[1:]
    return plant(rng, d, rng.integers(0, 65536, (N, 8, P)), rng.integers(0, 256, (N, 8, P)))
def setup_inputs_ends(rng):
    d = setup_inputs(rng); m = d["bm"]; n = (N, 8, P)
    d["bm"] = np.where((m & 31) < W, (m >> 5) * 32 + rng.choice(np.array([0, 1, W - 1]), m.shape), m).astype(np.int32)
    c = 256 * np.sort(rng.integers(1, 17, (N, 8, 16, NB)), axis=2); c[:, :, 15] = rng.choice(np.array([4096, 8191]), (N, 8, NB)); d["cs"] = sections(c)
    d["ls"] = losses(rng.choice(np.array([0, 1, 1, 2, 255, 32768, 65280, 65536, 131072, 65536 * N]), c.shape))
    u = W * rng.integers(0, BK, n) + rng.choice(np.array([0, 1, W - 1]), n)
    u = np.where(rng.random(n) < 0.25, rng.choice(np.array([0, 1, 65534, 65535]), n), u)
    return plant(rng, d, u, np.zeros(n, np.int64))
def setup_inputs_still(rng):
    d = setup_inputs(rng); w = (N, 8, 16, NB)
    c = np.sort(rng.integers(0, 4097, w), axis=2); c[:, :, 15] = rng.integers(4096, 8192, (N, 8, NB)); d["cs"] = sections(c)
    d["ls"] = rng.integers(1, 256, w).reshape(N, 128, NB).astype(np.float32).astype(BF)
    return plant(rng, d, rng.integers(4096, 65536, (N, 8, P)), rng.integers(0, 256, (N, 8, P)))
def setup_inputs_spread(rng):
    d = setup_inputs(rng); w = (N, 8, 16, NB)
    d["bm"] = ((rng.random((N, 8, BK)) ** 4 * (NB - 1)).astype(np.int64) * 32 + rng.integers(0, W + 1, (N, 8, BK))).astype(np.int32)
    c = 256 + (rng.random(w) ** 3 * 7936).astype(np.int64); c[:, :, 15] = np.maximum(c[:, :, 15], 4096); d["cs"] = sections(c)
    d["ls"] = losses((rng.random(w) ** 4 * 256).astype(np.int64) << rng.integers(0, 10 + 1, w))
    return plant(rng, d, (rng.random((N, 8, P)) ** 4 * 65536).astype(np.int64), rng.integers(0, 256, (N, 8, P)))
def check_inputs(d):
    bad = []; m = d["bm"]; c = d["cs"].reshape(N, 8, 16, NB); v = d["ls"].astype(np.float32); e = d["en"].astype(np.int64); s = d["sd"].astype(np.int64)
    if not ((m >= 0) & ((m >> 5) <= NB - 2) & ((m & 31) <= W)).all(): bad.append("buckets")
    if not ((c >= 0) & (c <= 8191)).all() or not (c[:, :, 15] >= 4096).all(): bad.append("sections")
    if not ((v >= 0) & (v <= 65536 * N) & (v == np.floor(v))).all(): bad.append("losses")
    if not ((e >> 16) == np.arange(N)[:, None, None]).all(): bad.append("energies")
    if not ((s >= 0) & (s < 16 ** (EV + 1))).all(): bad.append("seeds")
    if bad: return bad
    for t in range(EV - 1):
        a = e >> 16; e = event(m, d["cs"], d["ls"], e, s, t)[1]; z = e >> 16
        n = np.bincount(((a * N + z) * 8 + group()).ravel(), minlength=N * N * 8).reshape(N, N, 8)
        if (n[~np.eye(N, dtype=bool)] > LV).any(): bad.append("leavers")
        if (np.sum(n, axis=0) > LIVE).any(): bad.append("live")
    return sorted(set(bad))
def reference(bm, cs, ls, en, sd):
    e = en.astype(np.int64); s = sd.astype(np.int64); tally = np.zeros((N, 8, P, 16), np.int64)
    for t in range(EV):
        c, e = event(bm, cs, ls, e, s, t)
        tally += c
    return {"y": tally.transpose(0, 1, 3, 2).reshape(N, 128, P).astype(np.float32)}

@@ -1,0 +1,555 @@
+from concourse.bass import DstId, RemoteDMATransfer
+from concourse.mybir import AluOpType as A, ActivationFunctionType as AF
+
+N, CAP, EV, RES = 4, 48, 4, 16
+BIG = 131072.0
+TRW = 1456
+
+SCRATCH = {}
+for _n, _w, _t in (
+        ("bmr", 512, "int32"), ("bmh", 512, "int32"), ("kt", 512, "int32"), ("hi", 512, "bfloat16"), ("lo", 512, "bfloat16"),
+        ("bmp", 1024, "bfloat16"), ("win", 8192, "bfloat16"), ("one", 128, "bfloat16"), ("s8", 128, "bfloat16"), ("s9", 128, "bfloat16"),
+        ("sel", 512, "bfloat16"), ("csb", 4112, "int32"), ("lsb", 4112, "bfloat16"), ("lbi", 2048, "bfloat16"), ("lb", 2048, "bfloat16"),
+        ("lid", 2048, "bfloat16"), ("raw", 256, "int32"), ("rawp", 256, "int32"), ("rsd", 256, "int32"), ("rsp", 256, "int32"),
+        ("a0", 256, "int32"), ("a1", 256, "int32"), ("a2", 256, "int32"), ("f1", 256, "float32"), ("f2", 256, "float32"),
+        ("f3", 256, "float32"), ("h0", 256, "bfloat16"), ("h1", 256, "bfloat16"), ("enw", 16, "int32"), ("pi", 4, "int32"),
+        ("ci", 16, "int32"), ("prm", 16, "uint16"), ("j16", 16, "float32"), ("oh", 16, "float32"), ("oz", 16, "float32"),
+        ("dl", 8, "float32"), ("cc", 64, "float32"), ("mi", 128, "bfloat16"), ("mg", 128, "bfloat16"), ("mo", 128, "bfloat16"),
+        ("bk", 128, "bfloat16"), ("idf", 128, "float32"), ("idb", 128, "bfloat16"), ("nu", 384, "bfloat16"), ("nt", 128, "bfloat16"),
+        ("nv", 384, "bfloat16"), ("bv", 384, "bfloat16"), ("br", 384, "bfloat16"), ("be", 128, "bfloat16"), ("jm", 144, "float32"),
+        ("dm", 144, "float32"), ("r16", 144, "float32"), ("dg", 144, "float32"), ("ds", 144, "float32"), ("bw", 16, "float32"),
+        ("b2", 16, "float32"), ("trn", 64, "float32"), ("trd", 32, "float32"), ("rm", 64, "float32"), ("z", 704, "bfloat16"),
+        ("tal", 704, "float32"), ("bl", 64, "float32"), ("le0", 288, "uint16"), ("le1", 192, "uint16"), ("le2", 96, "uint16"),
+        ("li0", 18, "uint16"), ("li1", 12, "uint16"), ("li2", 6, "uint16"), ("ll0", 154, "uint16"), ("ll1", 102, "uint16"),
+        ("ll2", 52, "uint16"), ("er", 288, "uint16"), ("il", 18, "uint16"), ("lr", 154, "uint16"), ("ert", 32, "float32"),
+        ("lrt", 32, "float32"), ("ye0", TRW, "float32"), ("ye1", TRW, "float32"), ("ye2", TRW, "float32"), ("yl", TRW, "float32"),
+        ("ac", 256, "float32"), ("yo", 256, "float32"), ("xs", 64, "bfloat16"), ("af", 64, "bfloat16"), ("dd", 64, "float32"),
+        ("lf", 64, "float32"), ("sw0", 768, "bfloat16"), ("sw1", 768, "bfloat16"), ("sw2", 768, "bfloat16"),
+        ("ft0", 64, "bfloat16"), ("ft1", 64, "bfloat16"), ("ft2", 64, "bfloat16")):
+    SCRATCH[_n] = ("sbuf", [128, _w], _t)
+for _k in "EA":
+    for _n, _w, _t in (("of", 64, "uint16"), ("bn", 64, "uint16"), ("lt", 64, "uint16"), ("yy", 704, "bfloat16"),
+                       ("in", 512, "bfloat16"), ("mk", 512, "bfloat16"), ("xx", 512, "bfloat16"), ("vr", 512, "float32")):
+        SCRATCH[_n + _k] = ("sbuf", [128, _w], _t)
+PS = ("psV", "psK", "psZ", "psW", "psB", "psU", "psP", "psI")
+for _k in PS:
+    SCRATCH[_k] = ("psum", [128, 512], "float32")
+
+SEMAPHORES = (["cV", "cP", "cS", "cG", "snt", "rx0", "rx1", "rx2"] + [a + str(s) for a in ("ri", "re", "rl") for s in range(3)]
+              + ["d%d" % i for i in range(16)])
+
+
+def tracker(g, T):
+    qs = {"V": g.vector, "P": g.tensor, "S": g.scalar, "Y": g.sync, "G": g}
+    cnt, acc, nd = {}, {}, [0]
+    know = {q: {} for q in qs}
+
+    def clean(regs):
+        return [(r[0], 0, 512) if r[0] in PS else tuple(r[:3]) for r in regs]
+
+    def need(q, reads, writes):
+        out = []
+        for kind, regs in (("r", clean(reads)), ("w", clean(writes))):
+            for b, lo, hi in regs:
+                for e in acc.get(b, []):
+                    if e[0] < hi and lo < e[1]:
+                        same = e[3] == q
+                        if b in PS:
+                            if same and q == "P":
+                                continue
+                            if not same or e[2] == "w":
+                                out.append(e)
+                        elif e[2] == "w" or kind == "w":
+                            if same and e[2] == "r" and q in "VPS":
+                                continue
+                            out.append(e)
+        return out
+
+    def wait(q, deps):
+        k = know[q]
+        top, imp = {}, {}
+        for e in deps:
+            top[e[4]] = max(top.get(e[4], 0), e[5])
+            for s, v in e[6].items():
+                if s != e[4]:
+                    imp[s] = max(imp.get(s, 0), v)
+        for s, v in top.items():
+            if k.get(s, 0) >= v or imp.get(s, 0) >= v:
+                continue
+            qs[q].wait_ge(T.sem[s], v)
+        for e in deps:
+            k[e[4]] = max(k.get(e[4], 0), e[5])
+            for s, v in e[6].items():
+                k[s] = max(k.get(s, 0), v)
+
+    def note(q, reads, writes, sem, val, snap):
+        for kind, regs in (("r", clean(reads)), ("w", clean(writes))):
+            for b, lo, hi in regs:
+                l = acc.setdefault(b, [])
+                if kind == "w":
+                    l[:] = [e for e in l if not (lo <= e[0] and e[1] <= hi)]
+                l.append((lo, hi, kind, q, sem, val, snap))
+
+    def op(q, fns, reads, writes):
+        wait(q, need(q, reads, writes))
+        for f in fns[:-1]:
+            f()
+        s = "c" + q
+        fns[-1]().then_inc(T.sem[s], 1)
+        cnt[s] = cnt.get(s, 0) + 1
+        note(q, reads, writes, s, cnt[s], dict(know[q]))
+
+    def dmas(lst, reads, writes):
+        s = "d%d" % nd[0]
+        nd[0] += 1
+        for e, o, i in lst:
+            wait(e, need(e, reads, []))
+            (g.sync if e == "Y" else g.scalar).dma_start(o, i).then_inc(T.sem[s], 16)
+        cnt[s] = 16 * len(lst)
+        note("D", reads, writes, s, cnt[s], {})
+
+    def landed(sem, val, regs):
+        note("R", [], regs, sem, val, {})
+        cnt[sem] = val
+
+    def sent(val):
+        cnt["snt"] = cnt.get("snt", 0) + val
+
+    def finish():
+        for s, v in cnt.items():
+            g.wait_ge(T.sem[s], v)
+
+    return op, dmas, landed, sent, finish, wait, need
+
+
+def rank_program(g, core, T, topo):
+    q = T.rank_of(core)
+    if q is None:
+        return
+    op, dmas, landed, sent, finish, wait, need = tracker(g, T)
+    V, P, S = g.vector, g.tensor, g.scalar
+    NA = N - 1 - q
+    AC = 3 * NA
+    CT = RES + AC * 2
+    OFF = BIG - 8192.0 * q
+    cols = {}
+
+    def B(n, lo=0, hi=None, step=1):
+        return (n, lo, SCRATCH[n][1][1] if hi is None else hi, step)
+
+    def ap(r):
+        return T[r[0]][:, r[1]:r[2]] if r[3] == 1 else T[r[0]][:, r[1]:r[2]:r[3]]
+
+    def ts(o, i, s1, s2, op0, op1=None):
+        rd = [i] + [s for s in (s1, s2) if isinstance(s, tuple)]
+        a1 = ap(s1) if isinstance(s1, tuple) else s1
+        a2 = ap(s2) if isinstance(s2, tuple) else s2
+        if op1 is None:
+            op("V", [lambda: V.tensor_scalar(ap(o), ap(i), a1, None, op0)], rd, [o])
+        else:
+            op("V", [lambda: V.tensor_scalar(ap(o), ap(i), a1, a2, op0, op1)], rd, [o])
+
+    def tt(o, a, b, f):
+        op("V", [lambda: V.tensor_tensor(ap(o), ap(a), ap(b), f)], [a, b], [o])
+
+    def ttg(o, w, l, b, f):
+        op("V", [lambda: V.tensor_tensor(ap(o), ap(w).indirect(ap(l)), ap(b), f)], [w, l, b], [o])
+
+    def cp(o, i):
+        op("V", [lambda: V.tensor_copy(ap(o), ap(i))], [i], [o])
+
+    def cpg(o, w, l, eng="V"):
+        if eng == "V":
+            op("V", [lambda: V.tensor_copy(ap(o), ap(w).indirect(ap(l)))], [w, l], [o])
+        else:
+            op("S", [lambda: S.activation(ap(o), ap(w).indirect(ap(l)), AF.Copy)], [w, l], [o])
+
+    def sca(w, l, i):
+        op("V", [lambda: V.tensor_copy(ap(w).indirect(ap(l)), ap(i))], [l, i], [w])
+
+    def scan(o, m, i):
+        op("V", [lambda: V.tensor_tensor_scan(ap(o), ap(m), ap(i), 0.0, A.mult, A.add)], [m, i], [o])
+
+    def fill(o, c):
+        op("V", [lambda: V.memset(ap(o), c)], [], [o])
+
+    def act(o, i, scale=None):
+        if scale is None:
+            op("S", [lambda: S.activation(ap(o), ap(i), AF.Copy)], [i], [o])
+        else:
+            op("S", [lambda: S.activation(ap(o), ap(i), AF.Identity, scale=ap(scale))], [i, scale], [o])
+
+    def iota(o, pat, base, ch):
+        if SCRATCH[o[0]][2] == "int32":
+            op("G", [lambda: g.iota(ap(o), pat, base, ch)], [], [o])
+        else:
+            op("G", [lambda: g.iota(ap(o), pat, base, ch, allow_small_or_imprecise_dtypes=True)], [], [o])
+
+    def aff(o, i, pat, cmp, base, ch):
+        op("G", [lambda: g.affine_select(ap(o), ap(i), pat, cmp, 0.0, base, ch)], [i], [o])
+
+    def mm(o, lst, a=0, b=None):
+        n = len(lst)
+        part = list(enumerate(lst))[a:b]
+        fns = [lambda k=k, l=l, r=r: P.matmul(ap(o), ap(l), ap(r), k == 0, k == n - 1) for k, (l, r) in part]
+        op("P", fns, [x for _, p in part for x in p], [o])
+
+    def wrapmm(lname, src, s0, s1):
+        return [(B(lname, 128 * r, 128 * r + 128), (src, s0 + r, s1, 16)) for r in range(16)]
+
+    def col(name):
+        if name not in cols:
+            cols[name] = len(cols)
+        k = cols[name]
+        return B("cc", k, k + 1)
+
+    def oh(k):
+        return B("oh", k, k + 1)
+
+    def M3(n, k):
+        return B(n, 128 * k, 128 * k + 128)
+
+    iota(B("raw"), [[1, 256]], 0, 0)
+    iota(B("pi", 0, 1), [[0, 1]], 0, 1)
+    dmas([("Y", T.bmr[:, :], T.bm[:, :])], [], [B("bmr")])
+    dmas([("Y", T.enw[:, :], T.en[:, :])], [], [B("enw")])
+    dmas([("YS"[o % 2], T.rsd[o::16, :], T.sd[:, :]) for o in range(16)], [], [B("rsd")])
+    dmas([("Y", T.raw[o::16, :], T.en[:, :]) for o in range(3)], [B("raw")], [B("raw")])
+    dmas([("Y", T.csb[:, 0:4096], T.cs[:, :])], [], [B("csb", 0, 4096)])
+    dmas([("Y", T.lsb[:, 0:4096], T.ls[:, :])], [], [B("lsb", 0, 4096)])
+    fill(B("one"), 1.0)
+    iota(B("j16"), [[1, 16]], 0, 0)
+    iota(B("kt"), [[-32, 512]], 0, 0)
+    aff(B("s8"), B("one"), [[0, 8], [-1, 16]], A.is_ge, 7, 0)
+    aff(B("s9"), B("one"), [[0, 8], [1, 16]], A.is_ge, -8, 0)
+    for k in range(2):
+        aff(M3("sel", k), B("s8"), [[-16, 8], [-2, 16]], A.is_equal, -k, 1)
+        aff(M3("sel", 2 + k), B("s9"), [[-16, 8], [-2, 16]], A.is_equal, 16 - k, 1)
+    iota(B("mg"), [[16, 8], [0, 16]], 0, 0)
+    iota(B("mi"), [[1, 128]], 0, 0)
+    iota(B("ci"), [[1, 16]], 0, 0)
+    if q:
+        iota(B("mo"), [[0, 8], [1, 16]], 0, 0)
+    iota(B("lbi"), [[-1, 16], [1, 128]], 0, 0)
+    if q:
+        iota(B("trn", 0, CT), [[16, CT]], CAP * q - 2047, 1)
+    if NA:
+        iota(B("trd"), [[16, 32]], -1024, 1)
+        iota(B("jm"), [[0, 9], [1, 16]], 0, 0)
+
+    fill(B("csb", 4096, 4112), 0)
+    fill(B("lsb", 4096, 4112), 0.0)
+    ts(B("pi", 1, 2), B("pi", 0, 1), 15, None, A.bitwise_and)
+    cp(col("p"), B("pi", 0, 1))
+    cp(col("o"), B("pi", 1, 2))
+    ts(col("bb"), col("o"), -16384.0, 32.0, A.mult, A.add)
+    tt(col("g16"), col("p"), col("o"), A.subtract)
+    ts(B("oh"), B("j16"), col("o"), None, A.is_equal)
+    ts(B("oz"), B("j16"), col("o"), 0.03125, A.is_equal, A.mult)
+    tt(B("dl"), B("oz", 0, 8), B("oz", 8, 16), A.add)
+    ts(col("o16"), col("o"), 16.0, None, A.mult)
+    tt(col("m1"), oh(9), oh(10), A.add)
+    tt(col("m2"), oh(11), oh(12), A.add)
+    ts(col("e3"), col("o"), 2.0, None, A.is_le)
+    ts(col("mA"), col("e3"), 0.125, oh(7), A.mult, A.add)
+    ts(col("t4"), col("e3"), -0.4375, oh(6), A.mult, A.add)
+    ts(col("bA"), oh(8), float(q), col("t4"), A.mult, A.add)
+    tt(col("t5"), oh(1), oh(2), A.add)
+    tt(col("t6"), oh(10), oh(12), A.add)
+    tt(col("cM"), col("t5"), col("t6"), A.add)
+    if q:
+        fill(B("rm", 0, q * CT), 1.0)
+        for t in range(3):
+            fill(B("ft%d" % t, 0, q * CT), 0.0)
+            fill(B("sw%d" % t, 0, CAP * q), 0.0)
+        for d in range(1, q):
+            fill(B("rm", d * CT, d * CT + 1), 0.0)
+    ts(B("bmh"), B("bmr"), 31, None, A.bitwise_and)
+    ts(B("psV"), B("bmh"), -5.0, col("bb"), A.mult, A.add)
+    tt(B("psK"), B("psV"), B("kt"), A.add)
+    tt(B("psZ"), B("psK"), B("bmr"), A.add)
+    act(B("hi"), B("psZ"))
+    ts(B("bk"), B("mg"), col("g16"), None, A.is_equal)
+    ts(B("idf"), B("mi"), col("p"), None, A.is_equal)
+    tt(B("lo"), B("psZ"), B("hi"), A.subtract)
+    for k, b in enumerate(("psW", "psB")):
+        mm(B(b), [(M3("sel", k), B("hi")), (M3("sel", 2 + k), B("lo"))])
+    ts(B("prm"), B("ci"), col("o16"), None, A.add)
+    ts(B("bl", 0, 16), B("enw"), 0.125, -0.4375 - 8192.0 * q, A.mult, A.add)
+    ts(B("ofE", 0, 16), B("bl", 0, 16), 8191.0, 0.0, A.min, A.max)
+    cpg(B("rsp"), B("rsd"), B("prm"))
+    ts(B("a0"), B("rsp"), 4095, None, A.bitwise_and)
+    cp(B("bmp", 0, 512), B("psW"))
+    act(B("bmp", 512, 1024), B("psB"))
+    if q:
+        ts(B("idb"), B("mi"), col("p"), None, A.is_equal)
+        ts(B("nt"), B("mi"), col("p"), -1.0, A.is_le, A.mult)
+        tt(B("nt"), B("nt"), B("bk"), A.mult)
+        tt(B("nt"), B("nt"), B("idb"), A.add)
+    for s in range(8):
+        o = B("win", 1024 * s, 1024 * s + 1024)
+        d = B("dl", s, s + 1)
+        if s in (1, 4, 7):
+            act(o, B("bmp"), d)
+        else:
+            ts(o, B("bmp"), d, None, A.mult)
+    ts(B("lb"), B("lbi"), col("g16"), None, A.is_equal)
+
+    def early():
+        if q:
+            for d in range(q):
+                ts(M3("nv", d), B("idb"), -2048.0 + CAP * d, None, A.mult)
+            for d in range(q):
+                tt(M3("nu", d), M3("nv", d), B("nt"), A.add)
+
+    def rows():
+        ts(B("a1"), B("rsp"), 4, 4095, A.arith_shift_right, A.bitwise_and)
+        ts(B("a2"), B("rsp"), 8, 4095, A.arith_shift_right, A.bitwise_and)
+        cpg(B("rawp"), B("raw"), B("prm"))
+
+    def later():
+        ts(B("f1"), B("a1"), col("m1"), None, A.mult)
+        ts(B("psU", 0, 256), B("rawp"), col("mA"), col("bA"), A.mult, A.add)
+        ts(B("f2"), B("a2"), col("m2"), None, A.mult)
+        tt(B("psP", 0, 256), B("psU", 0, 256), B("f1"), A.add)
+        tt(B("psI", 0, 256), B("psP", 0, 256), B("f2"), A.add)
+        act(B("h0"), B("psI", 0, 256), col("cM"))
+        for t in (1, 2):
+            ts(M3("bv", t), B("bk"), col("m%d" % t), None, A.mult)
+        if q:
+            for t in range(3):
+                ts(M3("nv", t), B("mo"), float(3 + t), None, A.is_equal)
+        tt(B("f3"), B("psI", 0, 256), B("h0"), A.subtract)
+        act(B("h1"), B("f3"), oh(2))
+        if q:
+            for t in range(3):
+                tt(M3("br", t), M3("nv", t), B("bk"), A.mult)
+        tt(B("z", 0, 256), B("f3"), B("h1"), A.subtract)
+
+    def last():
+        if NA:
+            ts(col("u1"), col("o"), 5.0, None, A.is_le)
+            ts(B("dm"), B("jm"), col("o"), None, A.is_equal)
+            ts(col("cb"), oh(6), -BIG, col("u1"), A.mult, A.add)
+            ts(B("r16"), B("jm"), 0.0, None, A.is_gt)
+            ts(B("be"), B("bk"), col("cb"), None, A.mult)
+            ts(col("u3"), oh(8), 256.0, oh(7), A.mult, A.add)
+            ts(col("cid"), oh(6), -2048.0, col("u3"), A.mult, A.add)
+            ts(B("lid"), B("lb"), col("cid"), None, A.mult)
+        if q:
+            for s in range(q):
+                fill(B("ye%d" % s, 256 * q, 256 * q + 256), 0.0)
+            fill(B("yl", 256 * q, 256 * q + 256), 0.0)
+
+    def vrep(x, t, s0, s1):
+        mm(B("psV", 0, s1 - s0), [(M3("bv", t), B("z", s0, s1))])
+        act(B("vr" + x, 0, s1 - s0), B("psV", 0, s1 - s0))
+
+    def diag(ps, n):
+        tt(B("dg", 0, n), B(ps, 0, n), B("dm", 0, n), A.mult)
+        scan(B("ds", 0, n), B("r16", 0, n), B("dg", 0, n))
+        return B("ds", 15, n, 16)
+
+    def buckets(c0, c1):
+        ts(B("ofE", 0, c1 - c0), B("bl", c0, c1), 8191.0, 0.0, A.min, A.max)
+
+    def bins(x, c0, c1, mid=None):
+        n = c1 - c0
+        yy = B("yy" + x, 0, 16 * n)
+        if x == "E":
+            L = [(B("idf"), B("bl", c0, c1))] + wrapmm("lb", "yyE", 0, 16 * n)
+            mm(B("psW", 0, n), L, 0, 1)
+            cpg(yy, B("win"), B("ofE", 0, n), "S")
+            mm(B("psW", 0, n), L, 1)
+            if mid:
+                mid()
+            ts(B("bnE", 0, n), B("psW", 0, n), 4096.0, 0.0, A.min, A.max)
+            return
+        cpg(yy, B("win"), B("ofA", 0, n))
+        if mid:
+            mid()
+        if q:
+            mm(B("psW", 0, 16 * n), [(B("be"), B("z", 16 * c0, 16 * c1)), (B("bk"), yy)])
+            ts(B("bnA", 0, n), diag("psW", 16 * n), OFF, 4096.0, A.add, A.min)
+        else:
+            mm(B("psW", 0, 16 * n), [(B("bk"), yy)])
+            tt(B("bw", 0, n), diag("psW", 16 * n), B("bl", c0, c1), A.add)
+            ts(B("bnA", 0, n), B("bw", 0, n), 4096.0, 0.0, A.min, A.max)
+
+    def tally(x, c0, c1, first):
+        o = B("tal", 16 * c0, 16 * c1)
+        if first:
+            cpg(o, B("csb"), B("bn" + x, 0, c1 - c0))
+        else:
+            ttg(o, B("csb"), B("bn" + x, 0, c1 - c0), o, A.add)
+
+    def event(x, t, c0, c1, first):
+        n, s0, s1 = c1 - c0, 16 * c0, 16 * c1
+        S_ = 16 * n
+        row, zr = B("xx" + x, 0, S_), B("z", s0, s1)
+        ttg(B("in" + x, 0, S_), B("csb"), B("bn" + x, 0, n), B("a0") if t == 0 else B("vr" + x, 0, S_), A.is_le)
+        mm(B("psK", 0, S_), [(B("bk"), B("in" + x, 0, S_))])
+        L = [(B("idf"), B("bl", c0, c1))] + wrapmm("lb", "xxE", 0, S_)
+        if x == "E":
+            mm(B("psB", 0, n), L, 0, 1)
+        elif q:
+            L = [(B("be"), zr), (B("bk"), row)]
+        else:
+            L = [(B("bk"), row)]
+        tally(x, c0, c1, first)
+        if t == 0:
+            later()
+        ts(B("mk" + x, 0, S_), B("psK", 0, S_), col("o"), -0.125, A.is_equal, A.mult)
+        ttg(row, B("lsb"), B("bn" + x, 0, n), B("mk" + x, 0, S_), A.mult)
+        off = 0.0
+        if x == "E":
+            mm(B("psB", 0, n), L, 1)
+            en = B("psB", 0, n)
+        else:
+            mm(B("psB", 0, S_), L)
+        if q:
+            mm(B("psZ", 0, S_), [(B("idb"), zr), (M3("br", t), row)])
+            act(zr, B("psZ", 0, S_))
+        if x == "A":
+            en = diag("psB", S_)
+            off = OFF
+        if q == 0:
+            if x == "A":
+                tt(B("b2", 0, n), en, B("bl", c0, c1), A.add)
+                en = B("b2", 0, n)
+            ts(B("bl", c0, c1), en, -0.4375, 0.0, A.max, A.add)
+            return
+        ft = "ft%d" % t
+        W = q * CT
+
+        def thr(s):
+            return 8192.0 * (s + 1 - q) - 0.5 - off
+        ts(B(ft, c0, c1), en, thr(0), None, A.is_lt)
+        for s in range(1, q):
+            ts(B("af", s * CT + c0, s * CT + c1), en, thr(s), None, A.is_lt)
+        for s in range(1, q):
+            prev = B(ft, c0, c1) if s == 1 else B("af", (s - 1) * CT + c0, (s - 1) * CT + c1)
+            tt(B(ft, s * CT + c0, s * CT + c1), B("af", s * CT + c0, s * CT + c1), prev, A.subtract)
+        scan(B("xs", 0, W), B("rm", 0, W), B(ft, 0, W))
+        for d in range(q):
+            blk = (d * CT, d * CT + CT)
+            mm(B("psP", *blk), [(B("bk"), B("xs", *blk)), (M3("nu", d), B(ft, *blk))])
+        ts(B("dd", c0, c1), en, thr(q - 1), BIG, A.is_lt, A.mult)
+        if x == "A":
+            ts(B("b2", 0, n), en, off, None, A.add)
+            en = B("b2", 0, n)
+        tt(B("bl", c0, c1), en, B("dd", c0, c1), A.add)
+        for d in range(q):
+            tt(B("lf", 0, n), B("psP", d * CT + c0, d * CT + c1), B("trn", c0, c1) if d == 0 else B("lf", 0, n), A.min)
+        ts(B("lt" + x, 0, n), B("lf", 0, n), 2047.0, None, A.add)
+        sca(B("sw%d" % t, 0, CAP * q + 16 * CT + 128), B("lt" + x, 0, n), zr)
+
+    def calls(dests):
+        two = dests[-2:]
+        out = [[(d, 8 // len(two)) for d in two]]
+        return out + [[(d, 8)] for d in dests[:-2]]
+
+    def fused(dests, src, dst, rsem):
+        wait("G", need("G", [src(d) for d in dests], []))
+        for call in calls(dests):
+            e = topo.engines(core, T.cores[call[0][0]])
+            tr, pos = [], 0
+            for d, w in call:
+                m = 0
+                for k in e[pos:pos + w]:
+                    m |= 1 << k
+                pos += w
+                rid, pid, _ = topo.addr(T.cores[d])
+                tr.append(RemoteDMATransfer(dst_ids=[DstId(rid=rid, pnc=pid)], dma_engine_mask=m, remote_sem=T.sem[rsem], src=ap(src(d)), dst=ap(dst(d))))
+            g.remote_dma_fused(tr, local_sem=T.sem.snt)
+            sent(pos)
+
+    def width(dests, d):
+        return [w for c in calls(dests) for x, w in c if x == d][0]
+
+    def zcol(s, t, r):
+        return 16 * (RES + 3 * (N - 1 - s) * t) + CAP * (r - s - 1)
+
+    def idfin(n, tile, outbuf, off, c=0):
+        tt(B(tile, 0, n), B("psI", 0, n), B("trd", c, c + n), A.min)
+        ts(B(outbuf, off, off + n), B(tile, 0, n), 2048.0, None, A.add)
+
+    def lists(t, s):
+        k = 3 * (N - 1 - s)
+        return ({1: (0, k), 2: (k, 2 * k)} if s == 0 else {2: (0, 2 * k)}).get(t)
+
+    up, down = list(range(q + 1, N)), list(range(q))
+    for t in range(EV):
+        ce = RES + AC * max(0, t - 1)
+        if t < 3:
+            if t:
+                buckets(0, ce)
+                vrep("E", t, 0, 16 * ce)
+            bins("E", 0, ce, early if t == 0 else None)
+            if t == 0:
+                rows()
+            event("E", t, 0, ce, t == 0)
+        elif NA:
+            buckets(RES, ce)
+            bins("E", RES, ce)
+            tally("E", RES, ce, False)
+            cp(B("er", 0, 32 * AC), B("tal", 256, 256 + 32 * AC))
+            fused(up, lambda d: B("er", 0, 32 * AC), lambda d: B("le%d" % q, 0, 32 * AC), "re%d" % q)
+        if t and NA:
+            c0 = RES + AC * (t - 1)
+            c1 = c0 + AC
+            zr = B("z", 16 * c0, 16 * c1)
+            n = 16 * AC
+            landed("rx%d" % (t - 1), sum(width(list(range(r)), q) for r in range(q + 1, N)), [zr])
+            mm(B("psU", 0, n), [(B("be"), zr)])
+            if t < 3:
+                vrep("A", t, 16 * c0, 16 * c1)
+            ts(B("ofA", 0, AC), diag("psU", n), OFF, 8191.0, A.add, A.min)
+            if q == 0:
+                ts(B("bl", c0, c1), B("ds", 15, n, 16), OFF, -0.4375, A.add, A.max)
+            if t < 3:
+                bins("A", c0, c1)
+                event("A", t, c0, c1, True)
+            else:
+                L = wrapmm("lid", "z", 16 * c0, 16 * c1)
+                bins("A", c0, c1, lambda: mm(B("psI", 0, AC), L, 0, 8))
+                mm(B("psI", 0, AC), L, 8)
+                cpg(B("lr", 0, n), B("csb"), B("bnA", 0, AC))
+                idfin(AC, "lrt", "lr", n)
+                fused(up, lambda d: B("lr", 0, 17 * AC), lambda d: B("ll%d" % q, 0, 17 * AC), "rl%d" % q)
+        if t < 3 and q:
+            fused(down, lambda d: B("sw%d" % t, CAP * d, CAP * d + CAP), lambda d: B("z", zcol(d, t, q), zcol(d, t, q) + CAP), "rx%d" % t)
+        if t == 0:
+            last()
+        if NA and lists(t, q):
+            a, b = lists(t, q)
+            mm(B("psI", 0, b - a), wrapmm("lid", "z", 256 + 16 * a, 256 + 16 * b))
+            idfin(b - a, "ert", "il", a, a)
+            fused(up, lambda d: B("il", a, b), lambda d: B("li%d" % q, a, b), "ri%d" % q)
+
+    buckets(0, RES)
+    bins("E", 0, RES)
+    tally("E", 0, RES, False)
+    own = 256 * q
+    if q == 0:
+        cpg(B("yo"), B("tal", 0, 256), B("prm"))
+        for h in range(2):
+            dmas([("YS"[h], T.y[:, 128 * h:128 * h + 128], T.yo[:, 128 * h:128 * h + 128])], [B("yo")], [])
+    else:
+        cpg(B("ac"), B("tal", 0, 256), B("prm"))
+        for s in range(q - 1, -1, -1):
+            n = 6 * (N - 1 - s)
+            w = width(list(range(s + 1, N)), q)
+            landed("ri%d" % s, w * len([t for t in range(EV) if lists(t, s)]), [B("li%d" % s)])
+            landed("re%d" % s, w, [B("le%d" % s)])
+            sca(B("ye%d" % s), B("li%d" % s, 0, n), B("le%d" % s, 0, 16 * n))
+            tt(B("ac"), B("ac"), B("ye%d" % s, own, own + 256), A.add)
+        for s in range(q - 1, -1, -1):
+            n = 3 * (N - 1 - s)
+            landed("rl%d" % s, width(list(range(s + 1, N)), q), [B("ll%d" % s)])
+            sca(B("yl"), B("ll%d" % s, 16 * n, 17 * n), B("ll%d" % s, 0, 16 * n))
+        for h in range(2):
+            lo, hi = 128 * h, 128 * h + 128
+            tt(B("yo", lo, hi), B("ac", lo, hi), B("yl", own + lo, own + hi), A.add)
+            dmas([("YS"[h], T.y[:, lo:hi], T.yo[:, lo:hi])], [B("yo", lo, hi)], [])
+    finish()

@@ -3,29 +3,36 @@ from concourse.mybir import AluOpType as A, ActivationFunctionType as AF
 
 N, CAP, EV, RES = 4, 48, 4, 16
 BIG = 131072.0
+LOW = -524288.0
 TRW = 1456
 
 SCRATCH = {}
 for _n, _w, _t in (
-        ("bmr", 512, "int32"), ("bmh", 512, "int32"), ("kt", 512, "int32"), ("hi", 512, "bfloat16"), ("lo", 512, "bfloat16"),
-        ("bmp", 1024, "bfloat16"), ("win", 8192, "bfloat16"), ("one", 128, "bfloat16"), ("s8", 128, "bfloat16"), ("s9", 128, "bfloat16"),
-        ("sel", 512, "bfloat16"), ("csb", 4112, "int32"), ("lsb", 4112, "bfloat16"), ("lbi", 2048, "bfloat16"), ("lb", 2048, "bfloat16"),
-        ("lid", 2048, "bfloat16"), ("raw", 256, "int32"), ("rawp", 256, "int32"), ("rsd", 256, "int32"), ("rsp", 256, "int32"),
-        ("a0", 256, "int32"), ("a1", 256, "int32"), ("a2", 256, "int32"), ("f1", 256, "float32"), ("f2", 256, "float32"),
-        ("f3", 256, "float32"), ("h0", 256, "bfloat16"), ("h1", 256, "bfloat16"), ("enw", 16, "int32"), ("pi", 4, "int32"),
-        ("ci", 16, "int32"), ("prm", 16, "uint16"), ("j16", 16, "float32"), ("oh", 16, "float32"), ("oz", 16, "float32"),
-        ("dl", 8, "float32"), ("cc", 64, "float32"), ("mi", 128, "bfloat16"), ("mg", 128, "bfloat16"), ("mo", 128, "bfloat16"),
-        ("bk", 128, "bfloat16"), ("idf", 128, "float32"), ("idb", 128, "bfloat16"), ("nu", 384, "bfloat16"), ("nt", 128, "bfloat16"),
-        ("nv", 384, "bfloat16"), ("bv", 384, "bfloat16"), ("br", 384, "bfloat16"), ("be", 128, "bfloat16"), ("jm", 144, "float32"),
-        ("dm", 144, "float32"), ("r16", 144, "float32"), ("dg", 144, "float32"), ("ds", 144, "float32"), ("bw", 16, "float32"),
-        ("b2", 16, "float32"), ("trn", 64, "float32"), ("trd", 32, "float32"), ("rm", 64, "float32"), ("z", 704, "bfloat16"),
-        ("tal", 704, "float32"), ("bl", 64, "float32"), ("le0", 288, "uint16"), ("le1", 192, "uint16"), ("le2", 96, "uint16"),
-        ("li0", 18, "uint16"), ("li1", 12, "uint16"), ("li2", 6, "uint16"), ("ll0", 154, "uint16"), ("ll1", 102, "uint16"),
-        ("ll2", 52, "uint16"), ("er", 288, "uint16"), ("il", 18, "uint16"), ("lr", 154, "uint16"), ("ert", 32, "float32"),
-        ("lrt", 32, "float32"), ("ye0", TRW, "float32"), ("ye1", TRW, "float32"), ("ye2", TRW, "float32"), ("yl", TRW, "float32"),
-        ("ac", 256, "float32"), ("yo", 256, "float32"), ("xs", 64, "bfloat16"), ("af", 64, "bfloat16"), ("dd", 64, "float32"),
-        ("lf", 64, "float32"), ("sw0", 768, "bfloat16"), ("sw1", 768, "bfloat16"), ("sw2", 768, "bfloat16"),
-        ("ft0", 64, "bfloat16"), ("ft1", 64, "bfloat16"), ("ft2", 64, "bfloat16")):
+        ("bmr", 512, "int32"), ("bmh", 512, "int32"), ("kt", 512, "float32"), ("t5", 512, "float32"), ("hi", 512, "bfloat16"),
+        ("lo", 512, "bfloat16"), ("bmp", 1024, "bfloat16"), ("win", 8192, "bfloat16"), ("one", 128, "bfloat16"),
+        ("s8", 128, "bfloat16"), ("s9", 128, "bfloat16"), ("sel", 512, "bfloat16"), ("csb", 4112, "int32"),
+        ("lsb", 4112, "bfloat16"), ("mg4", 512, "bfloat16"), ("bk4", 512, "bfloat16"), ("lb4", 512, "bfloat16"),
+        ("lb4f", 512, "float32"), ("lid", 512, "bfloat16"), ("bkf", 128, "float32"), ("fz", 384, "float32"),
+        ("nm", 112, "bfloat16"), ("rq", 112, "float32"), ("m4", 112, "float32"), ("dq", 112, "float32"),
+        ("nma", 144, "bfloat16"), ("jm", 256, "float32"), ("dm", 256, "float32"), ("r16", 144, "float32"),
+        ("ds", 144, "float32"), ("enw", 16, "int32"), ("sdw", 16, "int32"), ("wi", 64, "int32"), ("mi0", 16, "int32"),
+        ("mi1", 16, "int32"), ("mh0", 16, "int32"), ("mb0", 16, "int32"), ("e7", 16, "int32"), ("ge", 256, "float32"),
+        ("gv0", 256, "float32"), ("gv1", 256, "float32"), ("gv2", 256, "float32"), ("gs", 256, "bfloat16"),
+        ("gm", 256, "float32"), ("ms", 256, "bfloat16"), ("pl", 256, "bfloat16"), ("ki", 256, "bfloat16"),
+        ("a0", 256, "float32"), ("f3", 256, "float32"), ("h0", 256, "bfloat16"), ("h1", 256, "bfloat16"),
+        ("pi", 4, "int32"), ("ci", 16, "int32"), ("jcl", 16, "uint16"), ("prm", 16, "uint16"), ("j16", 16, "float32"),
+        ("oh", 16, "float32"), ("cc", 64, "float32"), ("mi", 128, "bfloat16"), ("idb", 128, "bfloat16"),
+        ("nu", 128, "bfloat16"), ("k48", 64, "bfloat16"), ("nt", 128, "bfloat16"), ("bv", 384, "bfloat16"),
+        ("br", 384, "bfloat16"), ("be", 128, "bfloat16"), ("bw", 32, "float32"), ("b2", 32, "float32"),
+        ("eb", 32, "float32"), ("trn", 64, "float32"), ("trd", 32, "float32"), ("rm", 64, "float32"),
+        ("z", 704, "bfloat16"), ("tal", 704, "float32"), ("bl", 64, "float32"), ("le0", 192, "uint16"),
+        ("le1", 144, "uint16"), ("le2", 96, "uint16"), ("li0", 12, "uint16"), ("li1", 10, "uint16"), ("li2", 6, "uint16"),
+        ("ll0", 154, "uint16"), ("ll1", 102, "uint16"), ("ll2", 52, "uint16"), ("er", 288, "uint16"), ("il", 18, "uint16"),
+        ("lr", 154, "uint16"), ("ert", 32, "float32"), ("ye0", TRW, "float32"), ("ye1", TRW, "float32"),
+        ("ye2", TRW, "float32"), ("yl", TRW, "float32"), ("ac", 256, "float32"), ("yo", 256, "float32"),
+        ("xs", 64, "bfloat16"), ("af", 64, "bfloat16"), ("dd", 64, "float32"), ("lf", 64, "float32"),
+        ("sw0", 768, "bfloat16"), ("sw1", 768, "bfloat16"), ("sw2", 768, "bfloat16"), ("ft0", 64, "bfloat16"),
+        ("ft1", 64, "bfloat16"), ("ft2", 64, "bfloat16")):
     SCRATCH[_n] = ("sbuf", [128, _w], _t)
 for _k in "EA":
     for _n, _w, _t in (("of", 64, "uint16"), ("bn", 64, "uint16"), ("lt", 64, "uint16"), ("yy", 704, "bfloat16"),
@@ -167,15 +174,17 @@ def rank_program(g, core, T, topo):
     def sca(w, l, i):
         op("V", [lambda: V.tensor_copy(ap(w).indirect(ap(l)), ap(i))], [l, i], [w])
 
-    def scan(o, m, i):
-        op("V", [lambda: V.tensor_tensor_scan(ap(o), ap(m), ap(i), 0.0, A.mult, A.add)], [m, i], [o])
+    def scan(o, m, i, op0=A.mult, op1=A.add):
+        op("V", [lambda: V.tensor_tensor_scan(ap(o), ap(m), ap(i), 0.0, op0, op1)], [m, i], [o])
 
     def fill(o, c):
         op("V", [lambda: V.memset(ap(o), c)], [], [o])
 
-    def act(o, i, scale=None):
-        if scale is None:
-            op("S", [lambda: S.activation(ap(o), ap(i), AF.Copy)], [i], [o])
+    def act(o, i, scale=1.0, bias=None):
+        if bias:
+            op("S", [lambda: S.activation(ap(o), ap(i), AF.Identity, bias=ap(bias))], [i, bias], [o])
+        elif isinstance(scale, float):
+            op("S", [lambda: S.activation(ap(o), ap(i), AF.Copy, scale=scale)], [i], [o])
         else:
             op("S", [lambda: S.activation(ap(o), ap(i), AF.Identity, scale=ap(scale))], [i, scale], [o])
 
@@ -194,9 +203,6 @@ def rank_program(g, core, T, topo):
         fns = [lambda k=k, l=l, r=r: P.matmul(ap(o), ap(l), ap(r), k == 0, k == n - 1) for k, (l, r) in part]
         op("P", fns, [x for _, p in part for x in p], [o])
 
-    def wrapmm(lname, src, s0, s1):
-        return [(B(lname, 128 * r, 128 * r + 128), (src, s0 + r, s1, 16)) for r in range(16)]
-
     def col(name):
         if name not in cols:
             cols[name] = len(cols)
@@ -209,54 +215,135 @@ def rank_program(g, core, T, topo):
     def M3(n, k):
         return B(n, 128 * k, 128 * k + 128)
 
-    iota(B("raw"), [[1, 256]], 0, 0)
-    iota(B("pi", 0, 1), [[0, 1]], 0, 1)
-    dmas([("Y", T.bmr[:, :], T.bm[:, :])], [], [B("bmr")])
+    bk, idb = B("bk4", 0, 128), B("idb")
+
+    def quad(lname, src, s0, s1):
+        return ([(idb, B("nm", 0, (s1 - s0) // 4))]
+                + [(M3(lname, r), (src, s0 + r, s1, 4)) for r in range(4)])
+
+    def unquad(ps, n):
+        scan(B("dq", 0, 4 * n), B("rq", 0, 4 * n), B(ps, 0, 4 * n), A.add, A.max)
+        return B("dq", 3, 4 * n, 4)
+
+    def low(n):
+        return (idb, B("nma", 0, n))
+
+    def diag(ps, n):
+        scan(B("ds", 0, n), B("r16", 0, n), B(ps, 0, n), A.add, A.max)
+        return B("ds", 15, n, 16)
+
     dmas([("Y", T.enw[:, :], T.en[:, :])], [], [B("enw")])
-    dmas([("YS"[o % 2], T.rsd[o::16, :], T.sd[:, :]) for o in range(16)], [], [B("rsd")])
-    dmas([("Y", T.raw[o::16, :], T.en[:, :]) for o in range(3)], [B("raw")], [B("raw")])
+    dmas([("S", T.bmr[:, :], T.bm[:, :])], [], [B("bmr")])
+    dmas([("Y", T.sdw[:, :], T.sd[:, :])], [], [B("sdw")])
     dmas([("Y", T.csb[:, 0:4096], T.cs[:, :])], [], [B("csb", 0, 4096)])
     dmas([("Y", T.lsb[:, 0:4096], T.ls[:, :])], [], [B("lsb", 0, 4096)])
-    fill(B("one"), 1.0)
+    iota(B("pi", 0, 1), [[0, 1]], 0, 1)
     iota(B("j16"), [[1, 16]], 0, 0)
+    iota(B("jm"), [[0, 16], [1, 16]], 0, 0)
+    iota(B("ci"), [[1, 16]], 0, 0)
+    iota(B("mg4"), [[0, 4], [16, 8], [0, 16]], 0, 0)
+    iota(B("mi"), [[1, 128]], 0, 0)
+    iota(B("m4"), [[0, 28], [1, 4]], 0, 0)
+    fill(B("win", 0, 1024), 0.0)
+    fill(B("one"), 1.0)
+    for k in (1, 2, 3):
+        act(B("win", 1024 * k, 1024 * k + 1024), B("win", 0, 1024))
+    ts(B("pi", 1, 2), B("pi", 0, 1), 15, None, A.bitwise_and)
+    ts(B("pi", 2, 3), B("pi", 0, 1), 2, 3, A.arith_shift_right, A.bitwise_and)
+    cp(col("p"), B("pi", 0, 1))
+    cp(col("o"), B("pi", 1, 2))
+    cp(col("o4"), B("pi", 2, 3))
+    tt(col("g16"), col("p"), col("o"), A.subtract)
+    ts(B("oh"), B("j16"), col("o"), None, A.is_equal)
+    ts(B("dm"), B("jm"), col("o"), None, A.is_equal)
+    cp(B("jcl"), B("ci"))
+    ts(col("e3"), col("o"), 2.0, None, A.is_le)
+    tt(col("t5"), oh(1), oh(2), A.add)
+    tt(col("m1"), oh(3), oh(4), A.add)
+    tt(col("m2"), oh(6), oh(7), A.add)
+    tt(col("t6"), oh(4), oh(5), A.add)
+    tt(col("t7"), oh(7), oh(8), A.add)
+    tt(col("t8"), oh(2), oh(5), A.add)
+    ts(col("t4"), col("e3"), -0.4375, oh(12), A.mult, A.add)
+    tt(col("t6"), col("t5"), col("t6"), A.add)
+    tt(col("c2"), col("t8"), oh(8), A.add)
+    tt(col("cM"), col("t6"), col("t7"), A.add)
+    ts(col("bA"), oh(14), float(q), col("t4"), A.mult, A.add)
+    ts(col("bb"), col("o"), -16384.0, 32.0, A.mult, A.add)
+    ts(B("bk4"), B("mg4"), col("g16"), None, A.is_equal)
+    ts(idb, B("mi"), col("p"), None, A.is_equal)
+    if q:
+        ts(B("nt"), B("mi"), col("p"), -1.0, A.is_lt, A.mult)
+        ts(B("nu"), idb, -2048.0, None, A.mult)
+        tt(B("nt"), B("nt"), bk, A.mult)
+        tt(B("nu"), B("nt"), B("nu"), A.add)
+    aff(B("lb4"), B("bk4"), [[-1, 4], [0, 32], [1, 4]], A.is_equal, 0, 0)
+    act(B("bkf"), bk)
+    act(M3("fz", 0), bk, 0.125)
+    act(B("fz", 128, 384), B("bk4", 0, 256))
+    act(B("lb4f"), B("lb4"))
+    aff(B("fz"), B("fz"), [[-3, 3], [0, 8], [1, 16]], A.is_ge, 0, 0)
+    aff(B("fz"), B("fz"), [[3, 3], [0, 8], [-1, 16]], A.is_ge, 2, 0)
     iota(B("kt"), [[-32, 512]], 0, 0)
+    iota(B("pl"), [[1, 16], [16, 16]], 0, 0)
     aff(B("s8"), B("one"), [[0, 8], [-1, 16]], A.is_ge, 7, 0)
     aff(B("s9"), B("one"), [[0, 8], [1, 16]], A.is_ge, -8, 0)
     for k in range(2):
         aff(M3("sel", k), B("s8"), [[-16, 8], [-2, 16]], A.is_equal, -k, 1)
         aff(M3("sel", 2 + k), B("s9"), [[-16, 8], [-2, 16]], A.is_equal, 16 - k, 1)
-    iota(B("mg"), [[16, 8], [0, 16]], 0, 0)
-    iota(B("mi"), [[1, 128]], 0, 0)
-    iota(B("ci"), [[1, 16]], 0, 0)
-    if q:
-        iota(B("mo"), [[0, 8], [1, 16]], 0, 0)
-    iota(B("lbi"), [[-1, 16], [1, 128]], 0, 0)
     if q:
         iota(B("trn", 0, CT), [[16, CT]], CAP * q - 2047, 1)
+        iota(B("k48", 0, q * CT), [[CAP, q], [0, CT]], 0, 0)
+        aff(B("br"), B("bk4", 0, 384), [[-1, 3], [0, 8], [1, 16]], A.is_equal, -9, 0)
     if NA:
         iota(B("trd"), [[16, 32]], -1024, 1)
-        iota(B("jm"), [[0, 9], [1, 16]], 0, 0)
-
+    ts(B("nm"), B("m4"), col("o4"), LOW, A.not_equal, A.mult)
+    ts(B("rq"), B("m4"), 0.0, 2 * LOW, A.is_equal, A.mult)
+    ts(B("wi", 0, 16), B("enw"), 12, 15, A.arith_shift_right, A.bitwise_and)
+    ttg(B("gs"), B("wi", 0, 16), B("jcl"), B("dm"), A.mult)
+    mm(B("psU", 0, 256), [(bk, B("gs"))])
+    ts(B("mi0"), B("enw"), 3, 511, A.arith_shift_right, A.bitwise_and)
+    cp(B("ofE", 0, 16), B("mi0"))
+    ts(B("e7"), B("enw"), 7, None, A.bitwise_and)
+    ts(B("wi", 16, 32), B("sdw"), 4095, None, A.bitwise_and)
+    ttg(B("gv0"), B("wi", 16, 32), B("jcl"), B("dm"), A.mult)
+    ts(B("ms"), B("psU", 0, 256), col("o"), None, A.is_equal)
+    for k in (4, 5):
+        act(B("win", 1024 * k, 1024 * k + 1024), B("win", 0, 1024))
+    L = quad("lb4f", "gm", 0, 256)
+    mm(B("psB", 0, 64), L, 0, 1)
+    ttg(B("gm"), B("bmr"), B("ofE", 0, 16), B("ms"), A.mult)
+    mm(B("psB", 0, 64), L, 1)
+    mm(B("psV", 0, 256), [(B("bkf"), B("gv0"))])
+    act(B("a0"), B("psV", 0, 256))
+    act(B("psZ"), B("kt"), bias=col("bb"))
+    ttg(B("ge"), B("enw"), B("jcl"), B("dm"), A.mult)
+    ts(B("wi", 32, 48), B("sdw"), 4, 4095, A.arith_shift_right, A.bitwise_and)
+    ts(B("wi", 48, 64), B("sdw"), 8, 4095, A.arith_shift_right, A.bitwise_and)
+    ttg(B("gv1"), B("wi", 32, 48), B("jcl"), B("dm"), A.mult)
+    Z = [(M3("fz", 0), B("ge")), (M3("fz", 1), B("gv1")), (M3("fz", 2), B("gv2")), (idb, B("ki"))]
+    mm(B("psI", 0, 256), Z, 0, 2)
+    cp(B("mi1"), unquad("psB", 16))
+    ts(B("mh0"), B("mi1"), 31, None, A.bitwise_and)
+    ts(B("mb0"), B("mi1"), 5, None, A.arith_shift_right)
+    tt(B("bw", 0, 16), B("mh0"), B("e7"), A.is_le)
+    tt(B("b2", 0, 16), B("mb0"), B("bw", 0, 16), A.add)
+    cp(B("bnE", 0, 16), B("b2", 0, 16))
+    ttg(B("gv2"), B("wi", 48, 64), B("jcl"), B("dm"), A.mult)
+    mm(B("psI", 0, 256), Z, 2, 3)
+    ts(B("bmh"), B("bmr"), 31, None, A.bitwise_and)
+    tt(B("psK"), B("psZ"), B("bmr"), A.add)
+    ts(B("t5"), B("bmh"), -5.0, None, A.mult)
+    tt(B("psZ"), B("psK"), B("t5"), A.add)
+    ts(B("ki"), B("pl"), oh(13), col("bA"), A.mult, A.add)
+    mm(B("psI", 0, 256), Z, 3)
+    act(B("hi"), B("psZ"))
+    act(B("h0"), B("psI", 0, 256), col("cM"))
+    for k in (6, 7):
+        act(B("win", 1024 * k, 1024 * k + 1024), B("win", 0, 1024))
     fill(B("csb", 4096, 4112), 0)
     fill(B("lsb", 4096, 4112), 0.0)
-    ts(B("pi", 1, 2), B("pi", 0, 1), 15, None, A.bitwise_and)
-    cp(col("p"), B("pi", 0, 1))
-    cp(col("o"), B("pi", 1, 2))
-    ts(col("bb"), col("o"), -16384.0, 32.0, A.mult, A.add)
-    tt(col("g16"), col("p"), col("o"), A.subtract)
-    ts(B("oh"), B("j16"), col("o"), None, A.is_equal)
-    ts(B("oz"), B("j16"), col("o"), 0.03125, A.is_equal, A.mult)
-    tt(B("dl"), B("oz", 0, 8), B("oz", 8, 16), A.add)
-    ts(col("o16"), col("o"), 16.0, None, A.mult)
-    tt(col("m1"), oh(9), oh(10), A.add)
-    tt(col("m2"), oh(11), oh(12), A.add)
-    ts(col("e3"), col("o"), 2.0, None, A.is_le)
-    ts(col("mA"), col("e3"), 0.125, oh(7), A.mult, A.add)
-    ts(col("t4"), col("e3"), -0.4375, oh(6), A.mult, A.add)
-    ts(col("bA"), oh(8), float(q), col("t4"), A.mult, A.add)
-    tt(col("t5"), oh(1), oh(2), A.add)
-    tt(col("t6"), oh(10), oh(12), A.add)
-    tt(col("cM"), col("t5"), col("t6"), A.add)
+    ts(B("bl", 0, 16), B("enw"), 0.125, -0.4375 - 8192.0 * q, A.mult, A.add)
     if q:
         fill(B("rm", 0, q * CT), 1.0)
         for t in range(3):
@@ -264,78 +351,38 @@ def rank_program(g, core, T, topo):
             fill(B("sw%d" % t, 0, CAP * q), 0.0)
         for d in range(1, q):
             fill(B("rm", d * CT, d * CT + 1), 0.0)
-    ts(B("bmh"), B("bmr"), 31, None, A.bitwise_and)
-    ts(B("psV"), B("bmh"), -5.0, col("bb"), A.mult, A.add)
-    tt(B("psK"), B("psV"), B("kt"), A.add)
-    tt(B("psZ"), B("psK"), B("bmr"), A.add)
-    act(B("hi"), B("psZ"))
-    ts(B("bk"), B("mg"), col("g16"), None, A.is_equal)
-    ts(B("idf"), B("mi"), col("p"), None, A.is_equal)
     tt(B("lo"), B("psZ"), B("hi"), A.subtract)
-    for k, b in enumerate(("psW", "psB")):
-        mm(B(b), [(M3("sel", k), B("hi")), (M3("sel", 2 + k), B("lo"))])
-    ts(B("prm"), B("ci"), col("o16"), None, A.add)
-    ts(B("bl", 0, 16), B("enw"), 0.125, -0.4375 - 8192.0 * q, A.mult, A.add)
-    ts(B("ofE", 0, 16), B("bl", 0, 16), 8191.0, 0.0, A.min, A.max)
-    cpg(B("rsp"), B("rsd"), B("prm"))
-    ts(B("a0"), B("rsp"), 4095, None, A.bitwise_and)
-    cp(B("bmp", 0, 512), B("psW"))
-    act(B("bmp", 512, 1024), B("psB"))
-    if q:
-        ts(B("idb"), B("mi"), col("p"), None, A.is_equal)
-        ts(B("nt"), B("mi"), col("p"), -1.0, A.is_le, A.mult)
-        tt(B("nt"), B("nt"), B("bk"), A.mult)
-        tt(B("nt"), B("nt"), B("idb"), A.add)
-    for s in range(8):
-        o = B("win", 1024 * s, 1024 * s + 1024)
-        d = B("dl", s, s + 1)
-        if s in (1, 4, 7):
-            act(o, B("bmp"), d)
-        else:
-            ts(o, B("bmp"), d, None, A.mult)
-    ts(B("lb"), B("lbi"), col("g16"), None, A.is_equal)
+    mm(B("psW"), [(M3("sel", 0), B("hi")), (M3("sel", 2), B("lo"))])
+    act(B("bmp", 0, 512), B("psW"), 0.03125)
 
-    def early():
-        if q:
-            for d in range(q):
-                ts(M3("nv", d), B("idb"), -2048.0 + CAP * d, None, A.mult)
-            for d in range(q):
-                tt(M3("nu", d), M3("nv", d), B("nt"), A.add)
+    def window():
+        mm(B("psP"), [(M3("sel", 1), B("hi")), (M3("sel", 3), B("lo"))])
+        act(B("bmp", 512, 1024), B("psP"), 0.03125)
+        dmas([("Y", T.win[s::8, 1024 * s:1024 * s + 1024], T.bmp[s::8, :]) for s in range(8)], [B("bmp"), B("win")], [B("win")])
 
-    def rows():
-        ts(B("a1"), B("rsp"), 4, 4095, A.arith_shift_right, A.bitwise_and)
-        ts(B("a2"), B("rsp"), 8, 4095, A.arith_shift_right, A.bitwise_and)
-        cpg(B("rawp"), B("raw"), B("prm"))
-
-    def later():
-        ts(B("f1"), B("a1"), col("m1"), None, A.mult)
-        ts(B("psU", 0, 256), B("rawp"), col("mA"), col("bA"), A.mult, A.add)
-        ts(B("f2"), B("a2"), col("m2"), None, A.mult)
-        tt(B("psP", 0, 256), B("psU", 0, 256), B("f1"), A.add)
-        tt(B("psI", 0, 256), B("psP", 0, 256), B("f2"), A.add)
-        act(B("h0"), B("psI", 0, 256), col("cM"))
-        for t in (1, 2):
-            ts(M3("bv", t), B("bk"), col("m%d" % t), None, A.mult)
-        if q:
-            for t in range(3):
-                ts(M3("nv", t), B("mo"), float(3 + t), None, A.is_equal)
+    def first1():
         tt(B("f3"), B("psI", 0, 256), B("h0"), A.subtract)
-        act(B("h1"), B("f3"), oh(2))
-        if q:
-            for t in range(3):
-                tt(M3("br", t), M3("nv", t), B("bk"), A.mult)
+        act(B("h1"), B("f3"), col("c2"))
+
+    def first2():
         tt(B("z", 0, 256), B("f3"), B("h1"), A.subtract)
+        for t in (1, 2):
+            ts(M3("bv", t), bk, col("m%d" % t), None, A.mult)
 
     def last():
         if NA:
-            ts(col("u1"), col("o"), 5.0, None, A.is_le)
-            ts(B("dm"), B("jm"), col("o"), None, A.is_equal)
-            ts(col("cb"), oh(6), -BIG, col("u1"), A.mult, A.add)
-            ts(B("r16"), B("jm"), 0.0, None, A.is_gt)
-            ts(B("be"), B("bk"), col("cb"), None, A.mult)
-            ts(col("u3"), oh(8), 256.0, oh(7), A.mult, A.add)
-            ts(col("cid"), oh(6), -2048.0, col("u3"), A.mult, A.add)
-            ts(B("lid"), B("lb"), col("cid"), None, A.mult)
+            ts(col("e9"), col("o"), 9.0, None, A.is_ge)
+            ts(B("nma"), B("jm", 0, 144), col("o"), LOW, A.not_equal, A.mult)
+            ts(B("r16"), B("jm", 0, 144), 0.0, 2 * LOW, A.is_equal, A.mult)
+            ts(col("e9"), col("o"), 11.0, col("e9"), A.is_le, A.mult)
+            tt(col("u1"), col("e3"), col("e9"), A.add)
+            ts(col("cb"), oh(12), -BIG, col("u1"), A.mult, A.add)
+            ts(B("be"), bk, col("cb"), None, A.mult)
+            ts(col("u3"), oh(14), 256.0, oh(13), A.mult, A.add)
+            ts(col("cid"), oh(12), -2048.0, col("u3"), A.mult, A.add)
+            ts(B("lid"), B("lb4"), col("cid"), None, A.mult)
+        ts(col("o16"), col("o"), 16.0, None, A.mult)
+        ts(B("prm"), B("ci"), col("o16"), None, A.add)
         if q:
             for s in range(q):
                 fill(B("ye%d" % s, 256 * q, 256 * q + 256), 0.0)
@@ -345,11 +392,6 @@ def rank_program(g, core, T, topo):
         mm(B("psV", 0, s1 - s0), [(M3("bv", t), B("z", s0, s1))])
         act(B("vr" + x, 0, s1 - s0), B("psV", 0, s1 - s0))
 
-    def diag(ps, n):
-        tt(B("dg", 0, n), B(ps, 0, n), B("dm", 0, n), A.mult)
-        scan(B("ds", 0, n), B("r16", 0, n), B("dg", 0, n))
-        return B("ds", 15, n, 16)
-
     def buckets(c0, c1):
         ts(B("ofE", 0, c1 - c0), B("bl", c0, c1), 8191.0, 0.0, A.min, A.max)
 
@@ -357,23 +399,24 @@ def rank_program(g, core, T, topo):
         n = c1 - c0
         yy = B("yy" + x, 0, 16 * n)
         if x == "E":
-            L = [(B("idf"), B("bl", c0, c1))] + wrapmm("lb", "yyE", 0, 16 * n)
-            mm(B("psW", 0, n), L, 0, 1)
+            L = quad("lb4", "yyE", 0, 16 * n)
+            mm(B("psW", 0, 4 * n), L, 0, 1)
             cpg(yy, B("win"), B("ofE", 0, n), "S")
-            mm(B("psW", 0, n), L, 1)
-            if mid:
-                mid()
-            ts(B("bnE", 0, n), B("psW", 0, n), 4096.0, 0.0, A.min, A.max)
+            mm(B("psW", 0, 4 * n), L, 1)
+            tt(B("bw", 0, n), unquad("psW", n), B("bl", c0, c1), A.add)
+            ts(B("bnE", 0, n), B("bw", 0, n), 4096.0, 0.0, A.min, A.max)
             return
+        s_ = 16 * n
+        L = [low(s_)] + ([(B("be"), B("z", 16 * c0, 16 * c1))] if q else []) + [(bk, yy)]
+        mm(B("psW", 0, s_), L, 0, len(L) - 1)
         cpg(yy, B("win"), B("ofA", 0, n))
         if mid:
             mid()
+        mm(B("psW", 0, s_), L, len(L) - 1)
         if q:
-            mm(B("psW", 0, 16 * n), [(B("be"), B("z", 16 * c0, 16 * c1)), (B("bk"), yy)])
-            ts(B("bnA", 0, n), diag("psW", 16 * n), OFF, 4096.0, A.add, A.min)
+            ts(B("bnA", 0, n), diag("psW", s_), OFF, 4096.0, A.add, A.min)
         else:
-            mm(B("psW", 0, 16 * n), [(B("bk"), yy)])
-            tt(B("bw", 0, n), diag("psW", 16 * n), B("bl", c0, c1), A.add)
+            tt(B("bw", 0, n), diag("psW", s_), B("bl", c0, c1), A.add)
             ts(B("bnA", 0, n), B("bw", 0, n), 4096.0, 0.0, A.min, A.max)
 
     def tally(x, c0, c1, first):
@@ -388,29 +431,33 @@ def rank_program(g, core, T, topo):
         S_ = 16 * n
         row, zr = B("xx" + x, 0, S_), B("z", s0, s1)
         ttg(B("in" + x, 0, S_), B("csb"), B("bn" + x, 0, n), B("a0") if t == 0 else B("vr" + x, 0, S_), A.is_le)
-        mm(B("psK", 0, S_), [(B("bk"), B("in" + x, 0, S_))])
-        L = [(B("idf"), B("bl", c0, c1))] + wrapmm("lb", "xxE", 0, S_)
+        mm(B("psK", 0, S_), [(bk, B("in" + x, 0, S_))])
+        if t == 0:
+            window()
         if x == "E":
-            mm(B("psB", 0, n), L, 0, 1)
-        elif q:
-            L = [(B("be"), zr), (B("bk"), row)]
+            L, w = quad("lb4", "xxE", 0, S_), 4 * n
+            mm(B("psB", 0, w), L, 0, 1)
+            k = 1
         else:
-            L = [(B("bk"), row)]
+            L, w = [low(S_)] + ([(B("be"), zr)] if q else []) + [(bk, row)], S_
+            k = len(L) - 1
+            mm(B("psB", 0, w), L, 0, k)
         tally(x, c0, c1, first)
         if t == 0:
-            later()
+            first1()
         ts(B("mk" + x, 0, S_), B("psK", 0, S_), col("o"), -0.125, A.is_equal, A.mult)
         ttg(row, B("lsb"), B("bn" + x, 0, n), B("mk" + x, 0, S_), A.mult)
+        mm(B("psB", 0, w), L, k)
+        if t == 0:
+            first2()
+        if q:
+            mm(B("psZ", 0, S_), [(idb, zr), (M3("br", t), row)])
+            act(zr, B("psZ", 0, S_))
         off = 0.0
         if x == "E":
-            mm(B("psB", 0, n), L, 1)
-            en = B("psB", 0, n)
+            tt(B("eb", 0, n), unquad("psB", n), B("bl", c0, c1), A.add)
+            en = B("eb", 0, n)
         else:
-            mm(B("psB", 0, S_), L)
-        if q:
-            mm(B("psZ", 0, S_), [(B("idb"), zr), (M3("br", t), row)])
-            act(zr, B("psZ", 0, S_))
-        if x == "A":
             en = diag("psB", S_)
             off = OFF
         if q == 0:
@@ -430,10 +477,10 @@ def rank_program(g, core, T, topo):
         for s in range(1, q):
             prev = B(ft, c0, c1) if s == 1 else B("af", (s - 1) * CT + c0, (s - 1) * CT + c1)
             tt(B(ft, s * CT + c0, s * CT + c1), B("af", s * CT + c0, s * CT + c1), prev, A.subtract)
+        L2 = [(idb, B("k48", 0, W)), (B("nu"), B(ft, 0, W)), (bk, B("xs", 0, W))]
+        mm(B("psP", 0, W), L2, 0, 1)
         scan(B("xs", 0, W), B("rm", 0, W), B(ft, 0, W))
-        for d in range(q):
-            blk = (d * CT, d * CT + CT)
-            mm(B("psP", *blk), [(B("bk"), B("xs", *blk)), (M3("nu", d), B(ft, *blk))])
+        mm(B("psP", 0, W), L2, 1)
         ts(B("dd", c0, c1), en, thr(q - 1), BIG, A.is_lt, A.mult)
         if x == "A":
             ts(B("b2", 0, n), en, off, None, A.add)
@@ -450,17 +497,18 @@ def rank_program(g, core, T, topo):
         return out + [[(d, 8)] for d in dests[:-2]]
 
     def fused(dests, src, dst, rsem):
-        wait("G", need("G", [src(d) for d in dests], []))
+        wait("G", need("G", [src(d, max(dests)) for d in dests], []))
         for call in calls(dests):
             e = topo.engines(core, T.cores[call[0][0]])
-            tr, pos = [], 0
+            tr, pos, top = [], 0, max(d for d, w in call)
             for d, w in call:
                 m = 0
                 for k in e[pos:pos + w]:
                     m |= 1 << k
                 pos += w
                 rid, pid, _ = topo.addr(T.cores[d])
-                tr.append(RemoteDMATransfer(dst_ids=[DstId(rid=rid, pnc=pid)], dma_engine_mask=m, remote_sem=T.sem[rsem], src=ap(src(d)), dst=ap(dst(d))))
+                tr.append(RemoteDMATransfer(dst_ids=[DstId(rid=rid, pnc=pid)], dma_engine_mask=m, remote_sem=T.sem[rsem],
+                                            src=ap(src(d, top)), dst=ap(dst(d, top))))
             g.remote_dma_fused(tr, local_sem=T.sem.snt)
             sent(pos)
 
@@ -470,13 +518,9 @@ def rank_program(g, core, T, topo):
     def zcol(s, t, r):
         return 16 * (RES + 3 * (N - 1 - s) * t) + CAP * (r - s - 1)
 
-    def idfin(n, tile, outbuf, off, c=0):
-        tt(B(tile, 0, n), B("psI", 0, n), B("trd", c, c + n), A.min)
-        ts(B(outbuf, off, off + n), B(tile, 0, n), 2048.0, None, A.add)
-
-    def lists(t, s):
-        k = 3 * (N - 1 - s)
-        return ({1: (0, k), 2: (k, 2 * k)} if s == 0 else {2: (0, 2 * k)}).get(t)
+    def places(c, n, out, off):
+        tt(B("ert", 0, n), unquad("psI", n), B("trd", c, c + n), A.min)
+        ts(B(out, off, off + n), B("ert", 0, n), 2048.0, None, A.add)
 
     up, down = list(range(q + 1, N)), list(range(q))
     for t in range(EV):
@@ -485,23 +529,24 @@ def rank_program(g, core, T, topo):
             if t:
                 buckets(0, ce)
                 vrep("E", t, 0, 16 * ce)
-            bins("E", 0, ce, early if t == 0 else None)
-            if t == 0:
-                rows()
+                bins("E", 0, ce)
             event("E", t, 0, ce, t == 0)
         elif NA:
             buckets(RES, ce)
             bins("E", RES, ce)
             tally("E", RES, ce, False)
             cp(B("er", 0, 32 * AC), B("tal", 256, 256 + 32 * AC))
-            fused(up, lambda d: B("er", 0, 32 * AC), lambda d: B("le%d" % q, 0, 32 * AC), "re%d" % q)
+            w = 16 * (AC + 3)
+            fused(up, lambda d, m: B("er", CAP * (d - q - 1), CAP * (d - q - 1) + w), lambda d, m: B("le%d" % q, 0, w), "re%d" % q)
         if t and NA:
             c0 = RES + AC * (t - 1)
             c1 = c0 + AC
             zr = B("z", 16 * c0, 16 * c1)
             n = 16 * AC
             landed("rx%d" % (t - 1), sum(width(list(range(r)), q) for r in range(q + 1, N)), [zr])
-            mm(B("psU", 0, n), [(B("be"), zr)])
+            U = [low(n), (B("be"), zr)]
+            mm(B("psU", 0, n), U, 0, 1)
+            mm(B("psU", 0, n), U, 1)
             if t < 3:
                 vrep("A", t, 16 * c0, 16 * c1)
             ts(B("ofA", 0, AC), diag("psU", n), OFF, 8191.0, A.add, A.min)
@@ -511,21 +556,21 @@ def rank_program(g, core, T, topo):
                 bins("A", c0, c1)
                 event("A", t, c0, c1, True)
             else:
-                L = wrapmm("lid", "z", 16 * c0, 16 * c1)
-                bins("A", c0, c1, lambda: mm(B("psI", 0, AC), L, 0, 8))
-                mm(B("psI", 0, AC), L, 8)
-                cpg(B("lr", 0, n), B("csb"), B("bnA", 0, AC))
-                idfin(AC, "lrt", "lr", n)
-                fused(up, lambda d: B("lr", 0, 17 * AC), lambda d: B("ll%d" % q, 0, 17 * AC), "rl%d" % q)
+                L = quad("lid", "z", 16 * c0, 16 * c1)
+                bins("A", c0, c1, lambda: mm(B("psI", 0, 4 * AC), L))
+                cpg(B("lr", AC, AC + n), B("csb"), B("bnA", 0, AC))
+                places(0, AC, "lr", 0)
+                fused(up, lambda d, m: B("lr", 0, AC + CAP * (m - q)), lambda d, m: B("ll%d" % q, 0, AC + CAP * (m - q)), "rl%d" % q)
         if t < 3 and q:
-            fused(down, lambda d: B("sw%d" % t, CAP * d, CAP * d + CAP), lambda d: B("z", zcol(d, t, q), zcol(d, t, q) + CAP), "rx%d" % t)
+            fused(down, lambda d, m: B("sw%d" % t, CAP * d, CAP * d + CAP), lambda d, m: B("z", zcol(d, t, q), zcol(d, t, q) + CAP), "rx%d" % t)
         if t == 0:
             last()
-        if NA and lists(t, q):
-            a, b = lists(t, q)
-            mm(B("psI", 0, b - a), wrapmm("lid", "z", 256 + 16 * a, 256 + 16 * b))
-            idfin(b - a, "ert", "il", a, a)
-            fused(up, lambda d: B("il", a, b), lambda d: B("li%d" % q, a, b), "ri%d" % q)
+        if NA and t == 2:
+            k = 2 * AC
+            mm(B("psI", 0, 4 * k), quad("lid", "z", 256, 256 + 16 * k))
+            places(0, k, "il", 0)
+            w = AC + 3
+            fused(up, lambda d, m: B("il", 3 * (d - q - 1), 3 * (d - q - 1) + w), lambda d, m: B("li%d" % q, 0, w), "ri%d" % q)
 
     buckets(0, RES)
     bins("E", 0, RES)
@@ -538,16 +583,16 @@ def rank_program(g, core, T, topo):
     else:
         cpg(B("ac"), B("tal", 0, 256), B("prm"))
         for s in range(q - 1, -1, -1):
-            n = 6 * (N - 1 - s)
+            n = 3 * (N - s)
             w = width(list(range(s + 1, N)), q)
-            landed("ri%d" % s, w * len([t for t in range(EV) if lists(t, s)]), [B("li%d" % s)])
+            landed("ri%d" % s, w, [B("li%d" % s)])
             landed("re%d" % s, w, [B("le%d" % s)])
             sca(B("ye%d" % s), B("li%d" % s, 0, n), B("le%d" % s, 0, 16 * n))
             tt(B("ac"), B("ac"), B("ye%d" % s, own, own + 256), A.add)
         for s in range(q - 1, -1, -1):
-            n = 3 * (N - 1 - s)
+            a, n = 3 * (N - 1 - s), 3 * (q - s)
             landed("rl%d" % s, width(list(range(s + 1, N)), q), [B("ll%d" % s)])
-            sca(B("yl"), B("ll%d" % s, 16 * n, 17 * n), B("ll%d" % s, 0, 16 * n))
+            sca(B("yl"), B("ll%d" % s, 0, n), B("ll%d" % s, a, a + 16 * n))
         for h in range(2):
             lo, hi = 128 * h, 128 * h + 128
             tt(B("yo", lo, hi), B("ac", lo, hi), B("yl", own + lo, own + hi), A.add)

@@ -5,40 +5,41 @@ N, CAP, EV, RES = 4, 48, 4, 16
 BIG = 131072.0
 LOW = -524288.0
 TRW = 1456
+ZF = "VVVSSSGG"
+ROUNDS = 4
+C = dict(cyc=1.0e-3, same=0.10, cross=0.17, dissue=0.06, dlat=0.6, drate=300e3, rissue=0.4, rstart=0.6, rhop=0.6,
+         rrate=60e3, first=1.4, gg=1.5, sg=3.5, look=0.5)
 
 SCRATCH = {}
 for _n, _w, _t in (
         ("bmr", 512, "int32"), ("bmh", 512, "int32"), ("kt", 512, "float32"), ("t5", 512, "float32"), ("hi", 512, "bfloat16"),
         ("lo", 512, "bfloat16"), ("bmp", 1024, "bfloat16"), ("win", 8192, "bfloat16"), ("one", 128, "bfloat16"),
-        ("s8", 128, "bfloat16"), ("s9", 128, "bfloat16"), ("sel", 512, "bfloat16"), ("csb", 4112, "int32"),
-        ("lsb", 4112, "bfloat16"), ("mg4", 512, "bfloat16"), ("bk4", 512, "bfloat16"), ("lb4", 512, "bfloat16"),
-        ("lb4f", 512, "float32"), ("lid", 512, "bfloat16"), ("bkf", 128, "float32"), ("fz", 384, "float32"),
-        ("nm", 112, "bfloat16"), ("rq", 112, "float32"), ("m4", 112, "float32"), ("dq", 112, "float32"),
+        ("zz", 1024, "bfloat16"), ("nb", 128, "bfloat16"),
+        ("s89", 256, "bfloat16"), ("sel", 512, "bfloat16"), ("csb", 4112, "int32"), ("lsb", 4112, "bfloat16"),
+        ("mg4", 128, "bfloat16"), ("bk4", 128, "bfloat16"), ("lb4", 512, "bfloat16"), ("lb4f", 512, "float32"),
+        ("lid", 512, "bfloat16"), ("bkf", 128, "float32"), ("fz", 256, "float32"), ("s5", 8, "float32"), ("dg", 512, "int32"),
+        ("nm", 112, "bfloat16"), ("rq", 112, "float32"), ("m4", 112, "float32"),
         ("nma", 144, "bfloat16"), ("jm", 256, "float32"), ("dm", 256, "float32"), ("r16", 144, "float32"),
-        ("ds", 144, "float32"), ("enw", 16, "int32"), ("sdw", 16, "int32"), ("wi", 64, "int32"), ("mi0", 16, "int32"),
-        ("mi1", 16, "int32"), ("mh0", 16, "int32"), ("mb0", 16, "int32"), ("e7", 16, "int32"), ("ge", 256, "float32"),
-        ("gv0", 256, "float32"), ("gv1", 256, "float32"), ("gv2", 256, "float32"), ("gs", 256, "bfloat16"),
+        ("enw", 16, "int32"), ("sdw", 16, "int32"), ("wi", 16, "int32"), ("iw", 80, "int32"),
+        ("ge", 256, "float32"), ("gv", 256, "float32"), ("gs", 256, "bfloat16"),
         ("gm", 256, "float32"), ("ms", 256, "bfloat16"), ("pl", 256, "bfloat16"), ("ki", 256, "bfloat16"),
-        ("a0", 256, "float32"), ("f3", 256, "float32"), ("h0", 256, "bfloat16"), ("h1", 256, "bfloat16"),
         ("pi", 4, "int32"), ("ci", 16, "int32"), ("jcl", 16, "uint16"), ("prm", 16, "uint16"), ("j16", 16, "float32"),
         ("oh", 16, "float32"), ("cc", 64, "float32"), ("mi", 128, "bfloat16"), ("idb", 128, "bfloat16"),
         ("nu", 128, "bfloat16"), ("k48", 64, "bfloat16"), ("nt", 128, "bfloat16"), ("bv", 384, "bfloat16"),
-        ("br", 384, "bfloat16"), ("be", 128, "bfloat16"), ("bw", 32, "float32"), ("b2", 32, "float32"),
-        ("eb", 32, "float32"), ("trn", 64, "float32"), ("trd", 32, "float32"), ("rm", 64, "float32"),
-        ("z", 704, "bfloat16"), ("tal", 704, "float32"), ("bl", 64, "float32"), ("le0", 192, "uint16"),
+        ("br", 384, "bfloat16"), ("be", 128, "bfloat16"), ("trn", 64, "float32"), ("trd", 32, "float32"),
+        ("rm", 64, "float32"), ("z", 704, "bfloat16"), ("tal", 704, "float32"), ("bl", 64, "float32"), ("le0", 192, "uint16"),
         ("le1", 144, "uint16"), ("le2", 96, "uint16"), ("li0", 12, "uint16"), ("li1", 10, "uint16"), ("li2", 6, "uint16"),
         ("ll0", 154, "uint16"), ("ll1", 102, "uint16"), ("ll2", 52, "uint16"), ("er", 288, "uint16"), ("il", 18, "uint16"),
-        ("lr", 154, "uint16"), ("ert", 32, "float32"), ("ye0", TRW, "float32"), ("ye1", TRW, "float32"),
+        ("lr", 154, "uint16"), ("ert", 64, "float32"), ("dqi", 112, "float32"), ("ye0", TRW, "float32"), ("ye1", TRW, "float32"),
         ("ye2", TRW, "float32"), ("yl", TRW, "float32"), ("ac", 256, "float32"), ("yo", 256, "float32"),
-        ("xs", 64, "bfloat16"), ("af", 64, "bfloat16"), ("dd", 64, "float32"), ("lf", 64, "float32"),
-        ("sw0", 768, "bfloat16"), ("sw1", 768, "bfloat16"), ("sw2", 768, "bfloat16"), ("ft0", 64, "bfloat16"),
-        ("ft1", 64, "bfloat16"), ("ft2", 64, "bfloat16")):
+        ("sw0", 768, "bfloat16"), ("sw1", 768, "bfloat16"), ("sw2", 768, "bfloat16"), ("ft", 192, "bfloat16")):
     SCRATCH[_n] = ("sbuf", [128, _w], _t)
-for _k in "EA":
-    for _n, _w, _t in (("of", 64, "uint16"), ("bn", 64, "uint16"), ("lt", 64, "uint16"), ("yy", 704, "bfloat16"),
-                       ("in", 512, "bfloat16"), ("mk", 512, "bfloat16"), ("xx", 512, "bfloat16"), ("vr", 512, "float32")):
+for _k in "EFA":
+    for _n, _w, _t in (("of", 32, "uint16"), ("bn", 32, "uint16"), ("lt", 32, "uint16"), ("yy", 288, "bfloat16"),
+                       ("in", 256, "bfloat16"), ("mk", 256, "bfloat16"), ("xx", 256, "bfloat16"), ("vr", 256, "float32"),
+                       ("tw", 448, "float32"), ("xf", 128, "bfloat16")):
         SCRATCH[_n + _k] = ("sbuf", [128, _w], _t)
-PS = ("psV", "psK", "psZ", "psW", "psB", "psU", "psP", "psI")
+PS = ("E0", "E1", "F0", "F1", "A0", "A1", "psZ", "psI")
 for _k in PS:
     SCRATCH[_k] = ("psum", [128, 512], "float32")
 
@@ -46,13 +47,14 @@ SEMAPHORES = (["cV", "cP", "cS", "cG", "snt", "rx0", "rx1", "rx2"] + [a + str(s)
               + ["d%d" % i for i in range(16)])
 
 
+def clean(regs):
+    return [(r[0], 0, 512) if r[0] in PS else tuple(r[:3]) for r in regs]
+
+
 def tracker(g, T):
     qs = {"V": g.vector, "P": g.tensor, "S": g.scalar, "Y": g.sync, "G": g}
     cnt, acc, nd = {}, {}, [0]
     know = {q: {} for q in qs}
-
-    def clean(regs):
-        return [(r[0], 0, 512) if r[0] in PS else tuple(r[:3]) for r in regs]
 
     def need(q, reads, writes):
         out = []
@@ -60,15 +62,10 @@ def tracker(g, T):
             for b, lo, hi in regs:
                 for e in acc.get(b, []):
                     if e[0] < hi and lo < e[1]:
-                        same = e[3] == q
                         if b in PS:
-                            if same and q == "P":
-                                continue
-                            if not same or e[2] == "w":
+                            if e[3] != q or (q != "P" and "w" in (kind, e[2])):
                                 out.append(e)
-                        elif e[2] == "w" or kind == "w":
-                            if same and e[2] == "r" and q in "VPS":
-                                continue
+                        elif "w" in (kind, e[2]):
                             out.append(e)
         return out
 
@@ -97,111 +94,258 @@ def tracker(g, T):
                     l[:] = [e for e in l if not (lo <= e[0] and e[1] <= hi)]
                 l.append((lo, hi, kind, q, sem, val, snap))
 
-    def op(q, fns, reads, writes):
-        wait(q, need(q, reads, writes))
-        for f in fns[:-1]:
-            f()
-        s = "c" + q
-        fns[-1]().then_inc(T.sem[s], 1)
-        cnt[s] = cnt.get(s, 0) + 1
-        note(q, reads, writes, s, cnt[s], dict(know[q]))
-
-    def dmas(lst, reads, writes):
-        s = "d%d" % nd[0]
-        nd[0] += 1
-        for e, o, i in lst:
-            wait(e, need(e, reads, []))
-            (g.sync if e == "Y" else g.scalar).dma_start(o, i).then_inc(T.sem[s], 16)
-        cnt[s] = 16 * len(lst)
-        note("D", reads, writes, s, cnt[s], {})
-
-    def landed(sem, val, regs):
-        note("R", [], regs, sem, val, {})
-        cnt[sem] = val
-
-    def sent(val):
-        cnt["snt"] = cnt.get("snt", 0) + val
+    def issue(o):
+        q, reads, writes = o["q0"], o["r"], o["w"]
+        if o["k"] == "op":
+            wait(q, need(q, reads, writes))
+            for f in o["f"][:-1]:
+                f()
+            s = "c" + q
+            o["f"][-1]().then_inc(T.sem[s], 1)
+            cnt[s] = cnt.get(s, 0) + 1
+            note(q, reads, writes, s, cnt[s], dict(know[q]))
+        elif o["k"] == "dma":
+            s = "d%d" % nd[0]
+            nd[0] += 1
+            wait(q, need(q, reads, writes))
+            for f in o["f"]:
+                f().then_inc(T.sem[s], 16)
+            cnt[s] = 16 * len(o["f"])
+            note("D", reads, writes, s, cnt[s], dict(know[q]))
+        elif o["k"] == "land":
+            note("R", [], writes, o["sem"], o["val"], {})
+            cnt[o["sem"]] = o["val"]
+        else:
+            wait(q, need(q, reads, []))
+            o["f"][0]()
+            cnt["snt"] = cnt.get("snt", 0) + o["val"]
 
     def finish():
         for s, v in cnt.items():
             g.wait_ge(T.sem[s], v)
 
-    return op, dmas, landed, sent, finish, wait, need
+    return issue, finish
 
 
-def rank_program(g, core, T, topo):
-    q = T.rank_of(core)
-    if q is None:
-        return
-    op, dmas, landed, sent, finish, wait, need = tracker(g, T)
+def links(ops):
+    acc = {}
+    for i, o in enumerate(ops):
+        d, q = {}, o["q"]
+        for kind, regs in (("r", clean(o["r"])), ("w", clean(o["w"]))):
+            for b, lo, hi in regs:
+                for e in acc.get(b, []):
+                    if e[0] < hi and lo < e[1] and e[4] != i:
+                        same = e[3] == q and q != "D"
+                        if b in PS:
+                            lat = (C["same"] if q != "P" and "w" in (kind, e[2]) else 0.0) if same else C["cross"]
+                        elif "w" in (kind, e[2]):
+                            lat = C["same"] if same else C["cross"]
+                        else:
+                            continue
+                        d[e[4]] = max(d.get(e[4], 0.0), lat)
+        for kind, regs in (("r", clean(o["r"])), ("w", clean(o["w"]))):
+            for b, lo, hi in regs:
+                l = acc.setdefault(b, [])
+                if kind == "w":
+                    l[:] = [e for e in l if not (lo <= e[0] and e[1] <= hi)]
+                l.append((lo, hi, kind, q, i))
+        o["d"] = d
+
+
+def schedule(progs):
+    ops, base = [], []
+    for p in progs:
+        links(p)
+        base.append(len(ops))
+        ops += p
+    n = len(ops)
+    rank = [r for r, p in enumerate(progs) for _ in p]
+    dep, sends = [], {}
+    for r, p in enumerate(progs):
+        for i, o in enumerate(p):
+            dep.append({base[r] + j: lat for j, lat in o["d"].items()})
+            if o["k"] == "send":
+                for d in o["to"]:
+                    sends.setdefault((d, o["sem"]), []).append((base[r] + i, C["rstart"] + o["by"] / C["rrate"] + C["rhop"]))
+    for i, o in enumerate(ops):
+        if o["k"] == "land":
+            for j, lat in sends[(rank[i], o["sem"])]:
+                dep[i][j] = lat
+    into = [list(d.items()) for d in dep]
+    out = [[] for _ in range(n)]
+    for i in range(n):
+        for j, lat in into[i]:
+            out[j].append((i, lat))
+    left, last, pri = [len(l) for l in out], [i for i in range(n) if not out[i]], [0.0] * n
+    for i in last:
+        pri[i] = ops[i]["t"] + max([pri[j] + lat for j, lat in out[i]] + [0.0])
+        for j, _ in into[i]:
+            left[j] -= 1
+            if left[j] == 0:
+                last.append(j)
+    best = None
+    for _ in range(ROUNDS):
+        end, seq, fin = arrange(ops, rank, into, out, pri)
+        if best is None or end < best[0]:
+            best = (end, seq)
+        pri = arrange(ops, rank, out, into, fin)[2]
+    return [[ops[i] for i in l] for l in best[1]]
+
+
+def arrange(ops, rank, into, out, pri):
+    n = len(ops)
+    deg, ready, fin = [len(l) for l in into], [0.0] * n, [0.0] * n
+    pool, free, dfree, first = {}, {}, [0.0] * N, set()
+    res = [[] for _ in range(N)]
+
+    def enter(j):
+        pool.setdefault((rank[j], ops[j]["q0"]), []).append(j)
+
+    def done(i, t):
+        st = [(i, t)]
+        while st:
+            i, t = st.pop()
+            fin[i] = t
+            for j, lat in out[i]:
+                ready[j] = max(ready[j], t + lat)
+                deg[j] -= 1
+                if deg[j] == 0:
+                    if ops[j]["k"] == "land":
+                        res[rank[j]].append(j)
+                        st.append((j, ready[j]))
+                    else:
+                        enter(j)
+
+    for i in range(n):
+        if not into[i]:
+            enter(i)
+    while True:
+        best = None
+        for key, l in pool.items():
+            if not l:
+                continue
+            f = free.get(key, 0.0)
+            t0 = max(f, min(ready[i] for i in l))
+            c = max((i for i in l if ready[i] <= t0), key=lambda i: (pri[i], -i))
+            lim = t0 + ops[c]["t"] * C["look"]
+            for i in l:
+                if t0 < ready[i] < lim and pri[i] > pri[c] + (ready[i] - t0):
+                    c, lim = i, ready[i]
+            s = max(f, ready[c])
+            if best is None or s < best[0]:
+                best = (s, key, c)
+        if best is None:
+            break
+        s, key, c = best
+        pool[key].remove(c)
+        o, r = ops[c], key[0]
+        e = s + o["t"]
+        if o["k"] == "send" and r not in first:
+            first.add(r)
+            e += C["first"]
+        free[key] = e
+        res[r].append(c)
+        if o["k"] == "dma":
+            dfree[r] = max(dfree[r], e + C["dlat"]) + o["by"] / C["drate"]
+            e = dfree[r] + C["dlat"]
+        done(c, e)
+    return max(fin), res, fin
+
+
+def program(g, q, T, topo):
+    ops, cols = [], {}
+    core = T.cores[q]
     V, P, S = g.vector, g.tensor, g.scalar
     NA = N - 1 - q
     AC = 3 * NA
     CT = RES + AC * 2
-    OFF = BIG - 8192.0 * q
-    cols = {}
+    OFF = BIG - 8192.0 * q - 0.4375
+    cy = C["cyc"]
+
+    def op(qq, fns, reads, writes, t, **kw):
+        o = dict(k="op", q=qq, q0=qq, f=fns, r=reads, w=writes, t=t)
+        o.update(kw)
+        ops.append(o)
 
     def B(n, lo=0, hi=None, step=1):
         return (n, lo, SCRATCH[n][1][1] if hi is None else hi, step)
 
     def ap(r):
+        if not isinstance(r, tuple):
+            return r
         return T[r[0]][:, r[1]:r[2]] if r[3] == 1 else T[r[0]][:, r[1]:r[2]:r[3]]
+
+    def wd(r):
+        return (r[2] - r[1] + r[3] - 1) // r[3]
+
+    def tv(n, f):
+        return cy * max(64, n * f)
+
+    def short(*rs):
+        return all(SCRATCH[r[0]][2] in ("bfloat16", "uint16") for r in rs)
 
     def ts(o, i, s1, s2, op0, op1=None):
         rd = [i] + [s for s in (s1, s2) if isinstance(s, tuple)]
-        a1 = ap(s1) if isinstance(s1, tuple) else s1
-        a2 = ap(s2) if isinstance(s2, tuple) else s2
+        t = tv(wd(o), 0.5 if short(o, i) else 1)
         if op1 is None:
-            op("V", [lambda: V.tensor_scalar(ap(o), ap(i), a1, None, op0)], rd, [o])
+            op("V", [lambda: V.tensor_scalar(ap(o), ap(i), ap(s1), None, op0)], rd, [o], t)
         else:
-            op("V", [lambda: V.tensor_scalar(ap(o), ap(i), a1, a2, op0, op1)], rd, [o])
+            op("V", [lambda: V.tensor_scalar(ap(o), ap(i), ap(s1), ap(s2), op0, op1)], rd, [o], t)
 
     def tt(o, a, b, f):
-        op("V", [lambda: V.tensor_tensor(ap(o), ap(a), ap(b), f)], [a, b], [o])
+        op("V", [lambda: V.tensor_tensor(ap(o), ap(a), ap(b), f)], [a, b], [o], tv(wd(o), 1 if a[0] in PS or b[0] in PS else 2))
 
     def ttg(o, w, l, b, f):
-        op("V", [lambda: V.tensor_tensor(ap(o), ap(w).indirect(ap(l)), ap(b), f)], [w, l, b], [o])
+        op("V", [lambda: V.tensor_tensor(ap(o), ap(w).indirect(ap(l)), ap(b), f)], [w, l, b], [o], 0.05 + cy * C["gg"] * wd(o))
 
     def cp(o, i):
-        op("V", [lambda: V.tensor_copy(ap(o), ap(i))], [i], [o])
+        op("V", [lambda: V.tensor_copy(ap(o), ap(i))], [i], [o], tv(wd(o), 0.5 if short(o, i) else 1))
 
     def cpg(o, w, l, eng="V"):
         if eng == "V":
-            op("V", [lambda: V.tensor_copy(ap(o), ap(w).indirect(ap(l)))], [w, l], [o])
+            op("V", [lambda: V.tensor_copy(ap(o), ap(w).indirect(ap(l)))], [w, l], [o], 0.05 + cy * C["gg"] * wd(o))
         else:
-            op("S", [lambda: S.activation(ap(o), ap(w).indirect(ap(l)), AF.Copy)], [w, l], [o])
+            op("S", [lambda: S.activation(ap(o), ap(w).indirect(ap(l)), AF.Copy)], [w, l], [o], 0.065 + cy * C["gg"] * wd(o))
 
     def sca(w, l, i):
-        op("V", [lambda: V.tensor_copy(ap(w).indirect(ap(l)), ap(i))], [l, i], [w])
+        op("V", [lambda: V.tensor_copy(ap(w).indirect(ap(l)), ap(i))], [l, i], [w], 0.05 + cy * C["sg"] * wd(i))
 
     def scan(o, m, i, op0=A.mult, op1=A.add):
-        op("V", [lambda: V.tensor_tensor_scan(ap(o), ap(m), ap(i), 0.0, op0, op1)], [m, i], [o])
+        op("V", [lambda: V.tensor_tensor_scan(ap(o), ap(m), ap(i), 0.0, op0, op1)], [m, i], [o], tv(wd(o), 1))
 
     def fill(o, c):
-        op("V", [lambda: V.memset(ap(o), c)], [], [o])
+        op("V", [lambda: V.memset(ap(o), c)], [], [o], tv(wd(o), 0.5 if short(o) else 1))
 
     def act(o, i, scale=1.0, bias=None):
+        t = 0.06 + cy * wd(o)
+        more = [x for x in (scale, bias) if isinstance(x, tuple)]
         if bias:
-            op("S", [lambda: S.activation(ap(o), ap(i), AF.Identity, bias=ap(bias))], [i, bias], [o])
-        elif isinstance(scale, float):
-            op("S", [lambda: S.activation(ap(o), ap(i), AF.Copy, scale=scale)], [i], [o])
+            op("S", [lambda: S.activation(ap(o), ap(i), AF.Identity, bias=ap(bias), scale=ap(scale))], [i] + more, [o], t)
+        elif more:
+            op("S", [lambda: S.activation(ap(o), ap(i), AF.Identity, scale=ap(scale))], [i] + more, [o], t)
         else:
-            op("S", [lambda: S.activation(ap(o), ap(i), AF.Identity, scale=ap(scale))], [i, scale], [o])
+            op("S", [lambda: S.activation(ap(o), ap(i), AF.Copy, scale=scale)], [i], [o], t)
 
     def iota(o, pat, base, ch):
-        if SCRATCH[o[0]][2] == "int32":
-            op("G", [lambda: g.iota(ap(o), pat, base, ch)], [], [o])
-        else:
-            op("G", [lambda: g.iota(ap(o), pat, base, ch, allow_small_or_imprecise_dtypes=True)], [], [o])
+        kw = {} if SCRATCH[o[0]][2] == "int32" else {"allow_small_or_imprecise_dtypes": True}
+        op("G", [lambda: g.iota(ap(o), pat, base, ch, **kw)], [], [o], 0.13 + 2 * cy * wd(o))
 
-    def aff(o, i, pat, cmp, base, ch):
-        op("G", [lambda: g.affine_select(ap(o), ap(i), pat, cmp, 0.0, base, ch)], [i], [o])
+    def aff(o, i, pat, cmp, base, ch, other=0.0):
+        op("G", [lambda: g.affine_select(ap(o), ap(i), pat, cmp, other, base, ch)], [i], [o], 0.17 + 2 * cy * wd(o))
 
     def mm(o, lst, a=0, b=None):
         n = len(lst)
         part = list(enumerate(lst))[a:b]
         fns = [lambda k=k, l=l, r=r: P.matmul(ap(o), ap(l), ap(r), k == 0, k == n - 1) for k, (l, r) in part]
-        op("P", fns, [x for _, p in part for x in p], [o])
+        t = sum(0.03 + cy * max(64, wd(r)) * (1 if short(r) else 4) for k, (l, r) in part)
+        op("P", fns, [x for _, p in part for x in p], [o], t)
+
+    def dma(qq, fns, reads, writes, by):
+        op(qq, fns, reads, writes, C["dissue"] * len(fns), k="dma", q="D", by=by)
+
+    def load(qq, dst, name):
+        dma(qq, [lambda: (g.sync if qq == "Y" else g.scalar).dma_start(T[dst[0]][:, dst[1]:dst[2]], T[name][:, :])], [], [dst],
+            128 * wd(dst) * (2 if short(dst) else 4))
 
     def col(name):
         if name not in cols:
@@ -215,39 +359,45 @@ def rank_program(g, core, T, topo):
     def M3(n, k):
         return B(n, 128 * k, 128 * k + 128)
 
-    bk, idb = B("bk4", 0, 128), B("idb")
+    bk, idb = B("bk4"), B("idb")
 
     def quad(lname, src, s0, s1):
         return ([(idb, B("nm", 0, (s1 - s0) // 4))]
                 + [(M3(lname, r), (src, s0 + r, s1, 4)) for r in range(4)])
 
-    def unquad(ps, n):
-        scan(B("dq", 0, 4 * n), B("rq", 0, 4 * n), B(ps, 0, 4 * n), A.add, A.max)
-        return B("dq", 3, 4 * n, 4)
+    def unquad(ps, n, o):
+        scan(B(o, 0, 4 * n), B("rq", 0, 4 * n), B(ps, 0, 4 * n), A.add, A.max)
+        return B(o, 3, 4 * n, 4)
 
     def low(n):
         return (idb, B("nma", 0, n))
 
-    def diag(ps, n):
-        scan(B("ds", 0, n), B("r16", 0, n), B(ps, 0, n), A.add, A.max)
-        return B("ds", 15, n, 16)
+    def diag(ps, n, o):
+        scan(B(o, 0, n), B("r16", 0, n), B(ps, 0, n), A.add, A.max)
+        return B(o, 15, n, 16)
 
-    dmas([("Y", T.enw[:, :], T.en[:, :])], [], [B("enw")])
-    dmas([("S", T.bmr[:, :], T.bm[:, :])], [], [B("bmr")])
-    dmas([("Y", T.sdw[:, :], T.sd[:, :])], [], [B("sdw")])
-    dmas([("Y", T.csb[:, 0:4096], T.cs[:, :])], [], [B("csb", 0, 4096)])
-    dmas([("Y", T.lsb[:, 0:4096], T.ls[:, :])], [], [B("lsb", 0, 4096)])
+    load("Y", B("enw"), "en")
+    load("S", B("bmr"), "bm")
+    load("Y", B("sdw"), "sd")
+    load("Y", B("csb", 0, 4096), "cs")
+    load("Y", B("lsb", 0, 4096), "ls")
     iota(B("pi", 0, 1), [[0, 1]], 0, 1)
     iota(B("j16"), [[1, 16]], 0, 0)
     iota(B("jm"), [[0, 16], [1, 16]], 0, 0)
     iota(B("ci"), [[1, 16]], 0, 0)
-    iota(B("mg4"), [[0, 4], [16, 8], [0, 16]], 0, 0)
+    iota(B("mg4"), [[16, 8], [0, 16]], 0, 0)
     iota(B("mi"), [[1, 128]], 0, 0)
     iota(B("m4"), [[0, 28], [1, 4]], 0, 0)
-    fill(B("win", 0, 1024), 0.0)
     fill(B("one"), 1.0)
-    for k in (1, 2, 3):
-        act(B("win", 1024 * k, 1024 * k + 1024), B("win", 0, 1024))
+    fill(B("zz"), 0.0)
+    for k, e in enumerate(ZF):
+        w = B("win", 1024 * k, 1024 * k + 1024)
+        if e == "V":
+            fill(w, 0.0)
+        elif e == "S":
+            act(w, B("zz"))
+        else:
+            iota(w, [[0, 1024]], 0, 0)
     ts(B("pi", 1, 2), B("pi", 0, 1), 15, None, A.bitwise_and)
     ts(B("pi", 2, 3), B("pi", 0, 1), 2, 3, A.arith_shift_right, A.bitwise_and)
     cp(col("p"), B("pi", 0, 1))
@@ -257,238 +407,221 @@ def rank_program(g, core, T, topo):
     ts(B("oh"), B("j16"), col("o"), None, A.is_equal)
     ts(B("dm"), B("jm"), col("o"), None, A.is_equal)
     cp(B("jcl"), B("ci"))
-    ts(col("e3"), col("o"), 2.0, None, A.is_le)
-    tt(col("t5"), oh(1), oh(2), A.add)
-    tt(col("m1"), oh(3), oh(4), A.add)
-    tt(col("m2"), oh(6), oh(7), A.add)
-    tt(col("t6"), oh(4), oh(5), A.add)
-    tt(col("t7"), oh(7), oh(8), A.add)
-    tt(col("t8"), oh(2), oh(5), A.add)
-    ts(col("t4"), col("e3"), -0.4375, oh(12), A.mult, A.add)
-    tt(col("t6"), col("t5"), col("t6"), A.add)
-    tt(col("c2"), col("t8"), oh(8), A.add)
-    tt(col("cM"), col("t6"), col("t7"), A.add)
-    ts(col("bA"), oh(14), float(q), col("t4"), A.mult, A.add)
-    ts(col("bb"), col("o"), -16384.0, 32.0, A.mult, A.add)
-    ts(B("bk4"), B("mg4"), col("g16"), None, A.is_equal)
+    ts(bk, B("mg4"), col("g16"), None, A.is_equal)
     ts(idb, B("mi"), col("p"), None, A.is_equal)
+    tt(B("s5", 0, 5), B("oh", 0, 5), B("oh", 5, 10), A.add)
+    sc = B("s5", 4, 5)
+    for k in (3, 2, 1, 0):
+        act(col("s%d" % k), sc, 0.0625, B("s5", k, k + 1))
+        sc = col("s%d" % k)
+    ts(col("h9"), col("o"), 9.0, -0.5, A.is_le, A.mult)
+    act(col("bi"), sc, 0.5, col("h9"))
+    for t in range(3):
+        act(col("n%d" % t), oh(6 + t), 16.0, oh(5 + t))
+        act(col("m%d" % t), oh(7 + t), 256.0, col("n%d" % t))
+        act(M3("bv", t), bk, col("m%d" % t))
+    act(col("bA"), oh(15), float(q), oh(13))
+    ts(col("bb"), col("o"), -16384.0, 32.0, A.mult, A.add)
     if q:
-        ts(B("nt"), B("mi"), col("p"), -1.0, A.is_lt, A.mult)
-        ts(B("nu"), idb, -2048.0, None, A.mult)
-        tt(B("nt"), B("nt"), bk, A.mult)
-        tt(B("nu"), B("nt"), B("nu"), A.add)
-    aff(B("lb4"), B("bk4"), [[-1, 4], [0, 32], [1, 4]], A.is_equal, 0, 0)
+        act(B("nb"), bk, -1.0)
+        aff(B("nt"), B("nb"), [[-1, 128]], A.is_gt, 0, 1)
+        aff(B("nu"), B("nt"), [[-1, 128]], A.not_equal, 0, 1, -2048.0)
+    act(B("lb4f"), B("zz", 0, 512))
+    act(B("lb4"), B("zz", 0, 512))
+    for r in range(4):
+        act(B("lb4f", 129 * r, 128 * r + 128, 4), B("bk4", r, 128, 4))
+        act(B("lb4", 129 * r, 128 * r + 128, 4), B("bk4", r, 128, 4))
     act(B("bkf"), bk)
-    act(M3("fz", 0), bk, 0.125)
-    act(B("fz", 128, 384), B("bk4", 0, 256))
-    act(B("lb4f"), B("lb4"))
-    aff(B("fz"), B("fz"), [[-3, 3], [0, 8], [1, 16]], A.is_ge, 0, 0)
-    aff(B("fz"), B("fz"), [[3, 3], [0, 8], [-1, 16]], A.is_ge, 2, 0)
+    aff(M3("fz", 0), B("bkf"), [[0, 8], [-1, 16]], A.is_ge, 4, 0)
+    aff(M3("fz", 1), B("bkf"), [[0, 8], [1, 16]], A.is_ge, -5, 0)
     iota(B("kt"), [[-32, 512]], 0, 0)
     iota(B("pl"), [[1, 16], [16, 16]], 0, 0)
-    aff(B("s8"), B("one"), [[0, 8], [-1, 16]], A.is_ge, 7, 0)
-    aff(B("s9"), B("one"), [[0, 8], [1, 16]], A.is_ge, -8, 0)
+    aff(M3("s89", 0), B("one"), [[0, 8], [-1, 16]], A.is_ge, 7, 0)
+    aff(M3("s89", 1), B("one"), [[0, 8], [1, 16]], A.is_ge, -8, 0)
     for k in range(2):
-        aff(M3("sel", k), B("s8"), [[-16, 8], [-2, 16]], A.is_equal, -k, 1)
-        aff(M3("sel", 2 + k), B("s9"), [[-16, 8], [-2, 16]], A.is_equal, 16 - k, 1)
+        aff(M3("sel", k), M3("s89", 0), [[-16, 8], [-2, 16]], A.is_equal, -k, 1)
+        aff(M3("sel", 2 + k), M3("s89", 1), [[-16, 8], [-2, 16]], A.is_equal, 16 - k, 1)
     if q:
         iota(B("trn", 0, CT), [[16, CT]], CAP * q - 2047, 1)
         iota(B("k48", 0, q * CT), [[CAP, q], [0, CT]], 0, 0)
-        aff(B("br"), B("bk4", 0, 384), [[-1, 3], [0, 8], [1, 16]], A.is_equal, -9, 0)
+        act(B("br"), B("zz", 0, 384))
+        for j in range(3):
+            act(B("br", 129 * j + 10, 128 * j + 128, 16), B("bk4", 10 + j, 128, 16))
     if NA:
         iota(B("trd"), [[16, 32]], -1024, 1)
     ts(B("nm"), B("m4"), col("o4"), LOW, A.not_equal, A.mult)
     ts(B("rq"), B("m4"), 0.0, 2 * LOW, A.is_equal, A.mult)
-    ts(B("wi", 0, 16), B("enw"), 12, 15, A.arith_shift_right, A.bitwise_and)
-    ttg(B("gs"), B("wi", 0, 16), B("jcl"), B("dm"), A.mult)
-    mm(B("psU", 0, 256), [(bk, B("gs"))])
-    ts(B("mi0"), B("enw"), 3, 511, A.arith_shift_right, A.bitwise_and)
-    cp(B("ofE", 0, 16), B("mi0"))
-    ts(B("e7"), B("enw"), 7, None, A.bitwise_and)
-    ts(B("wi", 16, 32), B("sdw"), 4095, None, A.bitwise_and)
-    ttg(B("gv0"), B("wi", 16, 32), B("jcl"), B("dm"), A.mult)
-    ts(B("ms"), B("psU", 0, 256), col("o"), None, A.is_equal)
-    for k in (4, 5):
-        act(B("win", 1024 * k, 1024 * k + 1024), B("win", 0, 1024))
+    mi0, mi1, mh0, mb0, e7 = [B("iw", 16 * k, 16 * k + 16) for k in range(5)]
+    ts(B("wi"), B("enw"), 12, 15, A.arith_shift_right, A.bitwise_and)
+    ttg(B("gs"), B("wi"), B("jcl"), B("dm"), A.mult)
+    mm(B("A0", 0, 256), [(bk, B("gs"))])
+    ts(mi0, B("enw"), 3, 511, A.arith_shift_right, A.bitwise_and)
+    cp(B("ofE", 0, 16), mi0)
+    ts(e7, B("enw"), 7, None, A.bitwise_and)
+    ts(B("ms"), B("A0", 0, 256), col("o"), None, A.is_equal)
     L = quad("lb4f", "gm", 0, 256)
-    mm(B("psB", 0, 64), L, 0, 1)
+    mm(B("E0", 0, 64), L, 0, 1)
     ttg(B("gm"), B("bmr"), B("ofE", 0, 16), B("ms"), A.mult)
-    mm(B("psB", 0, 64), L, 1)
-    mm(B("psV", 0, 256), [(B("bkf"), B("gv0"))])
-    act(B("a0"), B("psV", 0, 256))
-    act(B("psZ"), B("kt"), bias=col("bb"))
+    mm(B("E0", 0, 64), L, 1)
     ttg(B("ge"), B("enw"), B("jcl"), B("dm"), A.mult)
-    ts(B("wi", 32, 48), B("sdw"), 4, 4095, A.arith_shift_right, A.bitwise_and)
-    ts(B("wi", 48, 64), B("sdw"), 8, 4095, A.arith_shift_right, A.bitwise_and)
-    ttg(B("gv1"), B("wi", 32, 48), B("jcl"), B("dm"), A.mult)
-    Z = [(M3("fz", 0), B("ge")), (M3("fz", 1), B("gv1")), (M3("fz", 2), B("gv2")), (idb, B("ki"))]
-    mm(B("psI", 0, 256), Z, 0, 2)
-    cp(B("mi1"), unquad("psB", 16))
-    ts(B("mh0"), B("mi1"), 31, None, A.bitwise_and)
-    ts(B("mb0"), B("mi1"), 5, None, A.arith_shift_right)
-    tt(B("bw", 0, 16), B("mh0"), B("e7"), A.is_le)
-    tt(B("b2", 0, 16), B("mb0"), B("bw", 0, 16), A.add)
-    cp(B("bnE", 0, 16), B("b2", 0, 16))
-    ttg(B("gv2"), B("wi", 48, 64), B("jcl"), B("dm"), A.mult)
-    mm(B("psI", 0, 256), Z, 2, 3)
+    ttg(B("gv"), B("sdw"), B("jcl"), B("dm"), A.mult)
+    Z = [(M3("fz", 0), B("ge")), (M3("fz", 1), B("gv"))]
+    mm(B("F0", 0, 256), Z, 0, 1)
+    mm(B("F0", 0, 256), Z, 1, 2)
+    ts(B("dg", 0, 256), B("F0", 0, 256), sc, col("bi"), A.mult, A.add)
+    ts(B("dg", 256, 512), B("dg", 0, 256), 15, None, A.bitwise_and)
+    ts(B("ki"), B("pl"), oh(14), col("bA"), A.mult, A.add)
+    tt(B("z", 0, 256), B("dg", 256, 512), B("ki"), A.add)
+    cp(mi1, unquad("E0", 16, "twE"))
+    ts(mh0, mi1, 31, None, A.bitwise_and)
+    ts(mb0, mi1, 5, None, A.arith_shift_right)
+    tt(B("twE", 288, 304), mh0, e7, A.is_le)
+    tt(B("twE", 320, 336), mb0, B("twE", 288, 304), A.add)
+    cp(B("bnE", 0, 16), B("twE", 320, 336))
+    act(B("psZ"), B("kt"), bias=col("bb"))
     ts(B("bmh"), B("bmr"), 31, None, A.bitwise_and)
-    tt(B("psK"), B("psZ"), B("bmr"), A.add)
-    ts(B("t5"), B("bmh"), -5.0, None, A.mult)
-    tt(B("psZ"), B("psK"), B("t5"), A.add)
-    ts(B("ki"), B("pl"), oh(13), col("bA"), A.mult, A.add)
-    mm(B("psI", 0, 256), Z, 3)
+    tt(B("F1"), B("psZ"), B("bmr"), A.add)
+    act(B("t5"), B("bmh"), -5.0)
+    tt(B("psZ"), B("F1"), B("t5"), A.add)
     act(B("hi"), B("psZ"))
-    act(B("h0"), B("psI", 0, 256), col("cM"))
-    for k in (6, 7):
-        act(B("win", 1024 * k, 1024 * k + 1024), B("win", 0, 1024))
     fill(B("csb", 4096, 4112), 0)
     fill(B("lsb", 4096, 4112), 0.0)
     ts(B("bl", 0, 16), B("enw"), 0.125, -0.4375 - 8192.0 * q, A.mult, A.add)
     if q:
         fill(B("rm", 0, q * CT), 1.0)
+        fill(B("ft"), 0.0)
         for t in range(3):
-            fill(B("ft%d" % t, 0, q * CT), 0.0)
             fill(B("sw%d" % t, 0, CAP * q), 0.0)
         for d in range(1, q):
             fill(B("rm", d * CT, d * CT + 1), 0.0)
     tt(B("lo"), B("psZ"), B("hi"), A.subtract)
-    mm(B("psW"), [(M3("sel", 0), B("hi")), (M3("sel", 2), B("lo"))])
-    act(B("bmp", 0, 512), B("psW"), 0.03125)
+    mm(B("A1"), [(M3("sel", 0), B("hi")), (M3("sel", 2), B("lo"))])
+    act(B("bmp", 0, 512), B("A1"), 0.03125)
+    mm(B("psI"), [(M3("sel", 1), B("hi")), (M3("sel", 3), B("lo"))])
+    act(B("bmp", 512, 1024), B("psI"), 0.03125)
+    dma("Y", [lambda s=s: g.sync.dma_start(T.win[s::8, 1024 * s:1024 * s + 1024], T.bmp[s::8, :]) for s in range(8)],
+        [B("bmp"), B("win")], [B("win")], 262144)
+    if NA:
+        wt = oh(4)
+        for k in (3, 2, 1, 0):
+            act(col("w%d" % k), wt, 16.0, oh(k))
+            wt = col("w%d" % k)
+        ts(col("f9"), col("o"), 10.0, None, A.is_ge)
+        ts(B("nma"), B("jm", 0, 144), col("o"), LOW, A.not_equal, A.mult)
+        ts(B("r16"), B("jm", 0, 144), 0.0, 2 * LOW, A.is_equal, A.mult)
+        ts(col("e9"), col("o"), 12.0, col("f9"), A.is_le, A.mult)
+        act(col("u1"), wt, 0.125, col("e9"))
+        act(col("cb"), oh(13), -BIG, col("u1"))
+        act(B("be"), bk, col("cb"))
+        act(col("u3"), oh(15), 256.0, oh(14))
+        act(col("cid"), oh(13), -2048.0, col("u3"))
+        act(B("lid"), B("lb4"), col("cid"))
+    ts(col("o16"), col("o"), 16.0, None, A.mult)
+    ts(B("prm"), B("ci"), col("o16"), None, A.add)
+    if q:
+        for s in range(q):
+            act(B("ye%d" % s, 256 * q, 256 * q + 256), B("zz", 0, 256))
+        act(B("yl", 256 * q, 256 * q + 256), B("zz", 0, 256))
 
-    def window():
-        mm(B("psP"), [(M3("sel", 1), B("hi")), (M3("sel", 3), B("lo"))])
-        act(B("bmp", 512, 1024), B("psP"), 0.03125)
-        dmas([("Y", T.win[s::8, 1024 * s:1024 * s + 1024], T.bmp[s::8, :]) for s in range(8)], [B("bmp"), B("win")], [B("win")])
-
-    def first1():
-        tt(B("f3"), B("psI", 0, 256), B("h0"), A.subtract)
-        act(B("h1"), B("f3"), col("c2"))
-
-    def first2():
-        tt(B("z", 0, 256), B("f3"), B("h1"), A.subtract)
-        for t in (1, 2):
-            ts(M3("bv", t), bk, col("m%d" % t), None, A.mult)
-
-    def last():
-        if NA:
-            ts(col("e9"), col("o"), 9.0, None, A.is_ge)
-            ts(B("nma"), B("jm", 0, 144), col("o"), LOW, A.not_equal, A.mult)
-            ts(B("r16"), B("jm", 0, 144), 0.0, 2 * LOW, A.is_equal, A.mult)
-            ts(col("e9"), col("o"), 11.0, col("e9"), A.is_le, A.mult)
-            tt(col("u1"), col("e3"), col("e9"), A.add)
-            ts(col("cb"), oh(12), -BIG, col("u1"), A.mult, A.add)
-            ts(B("be"), bk, col("cb"), None, A.mult)
-            ts(col("u3"), oh(14), 256.0, oh(13), A.mult, A.add)
-            ts(col("cid"), oh(12), -2048.0, col("u3"), A.mult, A.add)
-            ts(B("lid"), B("lb4"), col("cid"), None, A.mult)
-        ts(col("o16"), col("o"), 16.0, None, A.mult)
-        ts(B("prm"), B("ci"), col("o16"), None, A.add)
-        if q:
-            for s in range(q):
-                fill(B("ye%d" % s, 256 * q, 256 * q + 256), 0.0)
-            fill(B("yl", 256 * q, 256 * q + 256), 0.0)
+    def tw(x, k, n):
+        return B("tw" + x, 288 + 32 * k, 288 + 32 * k + n)
 
     def vrep(x, t, s0, s1):
-        mm(B("psV", 0, s1 - s0), [(M3("bv", t), B("z", s0, s1))])
-        act(B("vr" + x, 0, s1 - s0), B("psV", 0, s1 - s0))
+        mm(B(x + "1", 0, s1 - s0), [(M3("bv", t), B("z", s0, s1))])
+        act(B("vr" + x, 0, s1 - s0), B(x + "1", 0, s1 - s0))
 
-    def buckets(c0, c1):
-        ts(B("ofE", 0, c1 - c0), B("bl", c0, c1), 8191.0, 0.0, A.min, A.max)
+    def buckets(x, c0, c1):
+        ts(B("of" + x, 0, c1 - c0), B("bl", c0, c1), 8191.0, 0.0, A.min, A.max)
 
-    def bins(x, c0, c1, mid=None):
+    def sums(x, row, c0, c1, fresh):
+        m = 16 * (c1 - c0)
+        if fresh:
+            return [low(m)] + ([(B("be"), B("z", 16 * c0, 16 * c1))] if q else []) + [(bk, row)], m, 1
+        if x == "E" or m > 144:
+            return quad("lb4", row[0], 0, m), m // 4, 4
+        return [low(m), (bk, row)], m, 1
+
+    def wrapped(x, n, w):
+        return unquad(x + "0", n, "tw" + x) if w < 16 * n else diag(x + "0", w, "tw" + x)
+
+    def bins(x, c0, c1, fresh=False):
         n = c1 - c0
-        yy = B("yy" + x, 0, 16 * n)
-        if x == "E":
-            L = quad("lb4", "yyE", 0, 16 * n)
-            mm(B("psW", 0, 4 * n), L, 0, 1)
-            cpg(yy, B("win"), B("ofE", 0, n), "S")
-            mm(B("psW", 0, 4 * n), L, 1)
-            tt(B("bw", 0, n), unquad("psW", n), B("bl", c0, c1), A.add)
-            ts(B("bnE", 0, n), B("bw", 0, n), 4096.0, 0.0, A.min, A.max)
-            return
-        s_ = 16 * n
-        L = [low(s_)] + ([(B("be"), B("z", 16 * c0, 16 * c1))] if q else []) + [(bk, yy)]
-        mm(B("psW", 0, s_), L, 0, len(L) - 1)
-        cpg(yy, B("win"), B("ofA", 0, n))
-        if mid:
-            mid()
-        mm(B("psW", 0, s_), L, len(L) - 1)
-        if q:
-            ts(B("bnA", 0, n), diag("psW", s_), OFF, 4096.0, A.add, A.min)
+        m = 16 * n
+        yy, bn = B("yy" + x, 0, m), B("bn" + x, 0, n)
+        L, w, late = sums(x, yy, c0, c1, fresh)
+        mm(B(x + "0", 0, w), L, 0, len(L) - late)
+        cpg(yy, B("win"), B("of" + x, 0, n), "S" if m > 64 and not fresh else "V")
+        mm(B(x + "0", 0, w), L, len(L) - late)
+        s = wrapped(x, n, w)
+        if fresh and q:
+            ts(bn, s, OFF, 4096.0, A.add, A.min)
         else:
-            tt(B("bw", 0, n), diag("psW", s_), B("bl", c0, c1), A.add)
-            ts(B("bnA", 0, n), B("bw", 0, n), 4096.0, 0.0, A.min, A.max)
+            tt(tw(x, 0, n), s, B("bl", c0, c1), A.add)
+            ts(bn, tw(x, 0, n), 4096.0, 0.0, A.min, A.max)
 
     def tally(x, c0, c1, first):
         o = B("tal", 16 * c0, 16 * c1)
         if first:
-            cpg(o, B("csb"), B("bn" + x, 0, c1 - c0))
+            cpg(o, B("csb"), B("bn" + x, 0, c1 - c0), "S")
         else:
             ttg(o, B("csb"), B("bn" + x, 0, c1 - c0), o, A.add)
 
-    def event(x, t, c0, c1, first):
+    def event(x, t, c0, c1, first, fresh=False):
         n, s0, s1 = c1 - c0, 16 * c0, 16 * c1
-        S_ = 16 * n
-        row, zr = B("xx" + x, 0, S_), B("z", s0, s1)
-        ttg(B("in" + x, 0, S_), B("csb"), B("bn" + x, 0, n), B("a0") if t == 0 else B("vr" + x, 0, S_), A.is_le)
-        mm(B("psK", 0, S_), [(bk, B("in" + x, 0, S_))])
-        if t == 0:
-            window()
-        if x == "E":
-            L, w = quad("lb4", "xxE", 0, S_), 4 * n
-            mm(B("psB", 0, w), L, 0, 1)
-            k = 1
-        else:
-            L, w = [low(S_)] + ([(B("be"), zr)] if q else []) + [(bk, row)], S_
-            k = len(L) - 1
-            mm(B("psB", 0, w), L, 0, k)
+        m = 16 * n
+        p0, p1 = x + "0", x + "1"
+        row, zr = B("xx" + x, 0, m), B("z", s0, s1)
+        ttg(B("in" + x, 0, m), B("csb"), B("bn" + x, 0, n), B("vr" + x, 0, m), A.is_le)
+        mm(B(p1, 0, m), [(bk, B("in" + x, 0, m))])
+        L, w, late = sums(x, row, c0, c1, fresh)
+        mm(B(p0, 0, w), L, 0, len(L) - late)
         tally(x, c0, c1, first)
-        if t == 0:
-            first1()
-        ts(B("mk" + x, 0, S_), B("psK", 0, S_), col("o"), -0.125, A.is_equal, A.mult)
-        ttg(row, B("lsb"), B("bn" + x, 0, n), B("mk" + x, 0, S_), A.mult)
-        mm(B("psB", 0, w), L, k)
-        if t == 0:
-            first2()
-        if q:
-            mm(B("psZ", 0, S_), [(idb, zr), (M3("br", t), row)])
-            act(zr, B("psZ", 0, S_))
-        off = 0.0
-        if x == "E":
-            tt(B("eb", 0, n), unquad("psB", n), B("bl", c0, c1), A.add)
-            en = B("eb", 0, n)
-        else:
-            en = diag("psB", S_)
-            off = OFF
+        ts(B("mk" + x, 0, m), B(p1, 0, m), col("o"), -0.125, A.is_equal, A.mult)
+        ttg(row, B("lsb"), B("bn" + x, 0, n), B("mk" + x, 0, m), A.mult)
+        mm(B(p0, 0, w), L, len(L) - late)
+        en, off = wrapped(x, n, w), OFF
+        if not fresh:
+            tt(tw(x, 1, n), en, B("bl", c0, c1), A.add)
+            en, off = tw(x, 1, n), 0.0
         if q == 0:
-            if x == "A":
-                tt(B("b2", 0, n), en, B("bl", c0, c1), A.add)
-                en = B("b2", 0, n)
+            if fresh:
+                tt(tw(x, 2, n), en, B("bl", c0, c1), A.add)
+                en = tw(x, 2, n)
             ts(B("bl", c0, c1), en, -0.4375, 0.0, A.max, A.add)
             return
-        ft = "ft%d" % t
-        W = q * CT
+        f0, W = 64 * t, q * CT
+        xs = B("xf" + x, 0, W)
+
+        def af(s):
+            return B("xf" + x, 64 + s * n, 64 + s * n + n)
 
         def thr(s):
             return 8192.0 * (s + 1 - q) - 0.5 - off
-        ts(B(ft, c0, c1), en, thr(0), None, A.is_lt)
+
+        def fcol(s):
+            return B("ft", f0 + s * CT + c0, f0 + s * CT + c1)
+        ts(fcol(0), en, thr(0), None, A.is_lt)
         for s in range(1, q):
-            ts(B("af", s * CT + c0, s * CT + c1), en, thr(s), None, A.is_lt)
+            ts(af(s), en, thr(s), None, A.is_lt)
         for s in range(1, q):
-            prev = B(ft, c0, c1) if s == 1 else B("af", (s - 1) * CT + c0, (s - 1) * CT + c1)
-            tt(B(ft, s * CT + c0, s * CT + c1), B("af", s * CT + c0, s * CT + c1), prev, A.subtract)
-        L2 = [(idb, B("k48", 0, W)), (B("nu"), B(ft, 0, W)), (bk, B("xs", 0, W))]
-        mm(B("psP", 0, W), L2, 0, 1)
-        scan(B("xs", 0, W), B("rm", 0, W), B(ft, 0, W))
-        mm(B("psP", 0, W), L2, 1)
-        ts(B("dd", c0, c1), en, thr(q - 1), BIG, A.is_lt, A.mult)
-        if x == "A":
-            ts(B("b2", 0, n), en, off, None, A.add)
-            en = B("b2", 0, n)
-        tt(B("bl", c0, c1), en, B("dd", c0, c1), A.add)
+            tt(fcol(s), af(s), fcol(0) if s == 1 else af(s - 1), A.subtract)
+        fW = B("ft", f0, f0 + W)
+        L2 = [(idb, B("k48", 0, W)), (B("nu"), fW), (bk, xs)]
+        mm(B(p0, 0, W), L2, 0, 1)
+        scan(xs, B("rm", 0, W), fW)
+        mm(B(p0, 0, W), L2, 1, 2)
+        mm(B(p0, 0, W), L2, 2)
+        ts(tw(x, 3, n), en, thr(q - 1), BIG, A.is_lt, A.mult)
+        if fresh:
+            ts(tw(x, 2, n), en, off, None, A.add)
+            en = tw(x, 2, n)
+        tt(B("bl", c0, c1), en, tw(x, 3, n), A.add)
+        lf = tw(x, 4, n)
         for d in range(q):
-            tt(B("lf", 0, n), B("psP", d * CT + c0, d * CT + c1), B("trn", c0, c1) if d == 0 else B("lf", 0, n), A.min)
-        ts(B("lt" + x, 0, n), B("lf", 0, n), 2047.0, None, A.add)
+            tt(lf, B(p0, d * CT + c0, d * CT + c1), B("trn", c0, c1) if d == 0 else lf, A.min)
+        ts(B("lt" + x, 0, n), lf, 2047.0, None, A.add)
+        mm(B("psZ", 0, m), [(idb, zr), (M3("br", t), row)])
+        act(zr, B("psZ", 0, m))
         sca(B("sw%d" % t, 0, CAP * q + 16 * CT + 128), B("lt" + x, 0, n), zr)
 
     def calls(dests):
@@ -497,44 +630,57 @@ def rank_program(g, core, T, topo):
         return out + [[(d, 8)] for d in dests[:-2]]
 
     def fused(dests, src, dst, rsem):
-        wait("G", need("G", [src(d, max(dests)) for d in dests], []))
         for call in calls(dests):
-            e = topo.engines(core, T.cores[call[0][0]])
-            tr, pos, top = [], 0, max(d for d, w in call)
-            for d, w in call:
-                m = 0
-                for k in e[pos:pos + w]:
-                    m |= 1 << k
-                pos += w
-                rid, pid, _ = topo.addr(T.cores[d])
-                tr.append(RemoteDMATransfer(dst_ids=[DstId(rid=rid, pnc=pid)], dma_engine_mask=m, remote_sem=T.sem[rsem],
-                                            src=ap(src(d, top)), dst=ap(dst(d, top))))
-            g.remote_dma_fused(tr, local_sem=T.sem.snt)
-            sent(pos)
+            top = max(d for d, w in call)
+            sd = [(d, w, src(d, top), dst(d, top)) for d, w in call]
+
+            def go(sd=sd):
+                e = topo.engines(core, T.cores[sd[0][0]])
+                tr, pos = [], 0
+                for d, w, a, b in sd:
+                    m = 0
+                    for k in e[pos:pos + w]:
+                        m |= 1 << k
+                    pos += w
+                    rid, pid, _ = topo.addr(T.cores[d])
+                    tr.append(RemoteDMATransfer(dst_ids=[DstId(rid=rid, pnc=pid)], dma_engine_mask=m, remote_sem=T.sem[rsem],
+                                                src=ap(a), dst=ap(b)))
+                g.remote_dma_fused(tr, local_sem=T.sem.snt)
+            op("G", [go], [x[2] for x in sd], [], C["rissue"], k="send", sem=rsem, to=[x[0] for x in sd],
+               by=256 * sum(wd(x[2]) for x in sd), val=sum(x[1] for x in sd))
 
     def width(dests, d):
         return [w for c in calls(dests) for x, w in c if x == d][0]
 
+    def landed(sem, val, regs):
+        op("R", [], [], regs, 0.0, k="land", sem=sem, val=val)
+
     def zcol(s, t, r):
         return 16 * (RES + 3 * (N - 1 - s) * t) + CAP * (r - s - 1)
 
-    def places(c, n, out, off):
-        tt(B("ert", 0, n), unquad("psI", n), B("trd", c, c + n), A.min)
-        ts(B(out, off, off + n), B("ert", 0, n), 2048.0, None, A.add)
+    def places(n, out, k, ps, tmp):
+        er = B("ert", 32 * k, 32 * k + n)
+        tt(er, unquad(ps, n, tmp), B("trd", 0, n), A.min)
+        ts(B(out, 0, n), er, 2048.0, None, A.add)
 
     up, down = list(range(q + 1, N)), list(range(q))
     for t in range(EV):
-        ce = RES + AC * max(0, t - 1)
         if t < 3:
             if t:
-                buckets(0, ce)
-                vrep("E", t, 0, 16 * ce)
-                bins("E", 0, ce)
-            event("E", t, 0, ce, t == 0)
-        elif NA:
-            buckets(RES, ce)
-            bins("E", RES, ce)
-            tally("E", RES, ce, False)
+                buckets("E", 0, RES)
+                bins("E", 0, RES)
+            vrep("E", t, 0, 256)
+            event("E", t, 0, RES, t == 0)
+        if t == 2 and NA:
+            buckets("F", RES, RES + AC)
+            vrep("F", t, 256, 256 + 16 * AC)
+            bins("F", RES, RES + AC)
+            event("F", t, RES, RES + AC, False)
+        if t == 3 and NA:
+            ce = RES + AC * 2
+            buckets("F", RES, ce)
+            bins("F", RES, ce)
+            tally("F", RES, ce, False)
             cp(B("er", 0, 32 * AC), B("tal", 256, 256 + 32 * AC))
             w = 16 * (AC + 3)
             fused(up, lambda d, m: B("er", CAP * (d - q - 1), CAP * (d - q - 1) + w), lambda d, m: B("le%d" % q, 0, w), "re%d" % q)
@@ -545,41 +691,43 @@ def rank_program(g, core, T, topo):
             n = 16 * AC
             landed("rx%d" % (t - 1), sum(width(list(range(r)), q) for r in range(q + 1, N)), [zr])
             U = [low(n), (B("be"), zr)]
-            mm(B("psU", 0, n), U, 0, 1)
-            mm(B("psU", 0, n), U, 1)
+            mm(B("A0", 0, n), U, 0, 1)
+            mm(B("A0", 0, n), U, 1)
             if t < 3:
                 vrep("A", t, 16 * c0, 16 * c1)
-            ts(B("ofA", 0, AC), diag("psU", n), OFF, 8191.0, A.add, A.min)
+            ts(B("ofA", 0, AC), diag("A0", n, "twA"), OFF, 8191.0, A.add, A.min)
             if q == 0:
-                ts(B("bl", c0, c1), B("ds", 15, n, 16), OFF, -0.4375, A.add, A.max)
+                ts(B("bl", c0, c1), B("twA", 15, n, 16), OFF, -0.4375, A.add, A.max)
+            bins("A", c0, c1, True)
             if t < 3:
-                bins("A", c0, c1)
-                event("A", t, c0, c1, True)
+                event("A", t, c0, c1, True, True)
             else:
-                L = quad("lid", "z", 16 * c0, 16 * c1)
-                bins("A", c0, c1, lambda: mm(B("psI", 0, 4 * AC), L))
+                mm(B("A1", 0, 4 * AC), quad("lid", "z", 16 * c0, 16 * c1))
                 cpg(B("lr", AC, AC + n), B("csb"), B("bnA", 0, AC))
-                places(0, AC, "lr", 0)
+                places(AC, "lr", 1, "A1", "twA")
                 fused(up, lambda d, m: B("lr", 0, AC + CAP * (m - q)), lambda d, m: B("ll%d" % q, 0, AC + CAP * (m - q)), "rl%d" % q)
         if t < 3 and q:
             fused(down, lambda d, m: B("sw%d" % t, CAP * d, CAP * d + CAP), lambda d, m: B("z", zcol(d, t, q), zcol(d, t, q) + CAP), "rx%d" % t)
-        if t == 0:
-            last()
         if NA and t == 2:
             k = 2 * AC
             mm(B("psI", 0, 4 * k), quad("lid", "z", 256, 256 + 16 * k))
-            places(0, k, "il", 0)
+            places(k, "il", 0, "psI", "dqi")
             w = AC + 3
             fused(up, lambda d, m: B("il", 3 * (d - q - 1), 3 * (d - q - 1) + w), lambda d, m: B("li%d" % q, 0, w), "ri%d" % q)
 
-    buckets(0, RES)
+    buckets("E", 0, RES)
     bins("E", 0, RES)
     tally("E", 0, RES, False)
     own = 256 * q
+
+    def leave(h):
+        lo, hi = 128 * h, 128 * h + 128
+        dma("YS"[h], [lambda: (g.scalar if h else g.sync).dma_start(T.y[:, lo:hi], T.yo[:, lo:hi])], [B("yo", lo, hi)], [], 65536)
+
     if q == 0:
         cpg(B("yo"), B("tal", 0, 256), B("prm"))
         for h in range(2):
-            dmas([("YS"[h], T.y[:, 128 * h:128 * h + 128], T.yo[:, 128 * h:128 * h + 128])], [B("yo")], [])
+            leave(h)
     else:
         cpg(B("ac"), B("tal", 0, 256), B("prm"))
         for s in range(q - 1, -1, -1):
@@ -596,5 +744,16 @@ def rank_program(g, core, T, topo):
         for h in range(2):
             lo, hi = 128 * h, 128 * h + 128
             tt(B("yo", lo, hi), B("ac", lo, hi), B("yl", own + lo, own + hi), A.add)
-            dmas([("YS"[h], T.y[:, lo:hi], T.yo[:, lo:hi])], [B("yo", lo, hi)], [])
+            leave(h)
+    return ops
+
+
+def rank_program(g, core, T, topo):
+    q = T.rank_of(core)
+    if q is None:
+        return
+    order = schedule([program(g, r, T, topo) for r in range(N)])
+    issue, finish = tracker(g, T)
+    for o in order[q]:
+        issue(o)
     finish()

@@ -6,9 +6,9 @@ BIG = 131072.0
 LOW = -524288.0
 TRW = 1456
 ZF = "VVVSSSGG"
-ROUNDS = 4
-C = dict(cyc=1.0e-3, same=0.10, cross=0.17, dissue=0.06, dlat=0.6, drate=300e3, rissue=0.4, rstart=0.6, rhop=0.6,
-         rrate=60e3, first=1.4, gg=1.5, sg=3.5, look=0.5)
+LOOKS, ROUNDS = (0.4, 0.5, 0.55, 0.6, 0.65, 0.7, 0.8), 6
+C = dict(cyc=1.0e-3, same=0.10, cross=0.17, dissue=0.06, dlat=0.6, drate=300e3, rissue=0.7, rstart=0.6, rhop=0.6,
+         rrate=60e3, first=1.4, gg=1.5, sg=3.5)
 
 SCRATCH = {}
 for _n, _w, _t in (
@@ -17,7 +17,8 @@ for _n, _w, _t in (
         ("zz", 1024, "bfloat16"), ("nb", 128, "bfloat16"),
         ("s89", 256, "bfloat16"), ("sel", 512, "bfloat16"), ("csb", 4112, "int32"), ("lsb", 4112, "bfloat16"),
         ("mg4", 128, "bfloat16"), ("bk4", 128, "bfloat16"), ("lb4", 512, "bfloat16"), ("lb4f", 512, "float32"),
-        ("lid", 512, "bfloat16"), ("bkf", 128, "float32"), ("fz", 256, "float32"), ("s5", 8, "float32"), ("dg", 512, "int32"),
+        ("lid", 512, "bfloat16"), ("lbe", 512, "bfloat16"), ("bkf", 128, "float32"), ("fz", 256, "float32"),
+        ("s5", 8, "float32"), ("dg", 512, "int32"),
         ("nm", 112, "bfloat16"), ("rq", 112, "float32"), ("m4", 112, "float32"),
         ("nma", 144, "bfloat16"), ("jm", 256, "float32"), ("dm", 256, "float32"), ("r16", 144, "float32"),
         ("enw", 16, "int32"), ("sdw", 16, "int32"), ("wi", 16, "int32"), ("iw", 80, "int32"),
@@ -25,19 +26,21 @@ for _n, _w, _t in (
         ("gm", 256, "float32"), ("ms", 256, "bfloat16"), ("pl", 256, "bfloat16"), ("ki", 256, "bfloat16"),
         ("pi", 4, "int32"), ("ci", 16, "int32"), ("jcl", 16, "uint16"), ("prm", 16, "uint16"), ("j16", 16, "float32"),
         ("oh", 16, "float32"), ("cc", 64, "float32"), ("mi", 128, "bfloat16"), ("idb", 128, "bfloat16"),
-        ("nu", 128, "bfloat16"), ("k48", 64, "bfloat16"), ("nt", 128, "bfloat16"), ("bv", 384, "bfloat16"),
-        ("br", 384, "bfloat16"), ("be", 128, "bfloat16"), ("trn", 64, "float32"), ("trd", 32, "float32"),
-        ("rm", 64, "float32"), ("z", 704, "bfloat16"), ("tal", 704, "float32"), ("bl", 64, "float32"), ("le0", 192, "uint16"),
+        ("nu", 128, "bfloat16"), ("dp", 128, "bfloat16"), ("k48", 96, "bfloat16"), ("kx", 96, "bfloat16"),
+        ("nt", 128, "bfloat16"), ("bv", 384, "bfloat16"), ("br", 384, "bfloat16"), ("be", 128, "bfloat16"),
+        ("trn", 32, "float32"), ("trd", 32, "float32"), ("rm", 96, "float32"), ("th", 216, "bfloat16"), ("ft", 216, "bfloat16"),
+        ("sg", 1024, "float32"), ("gl", 768, "bfloat16"), ("z", 704, "bfloat16"), ("tal", 704, "float32"),
+        ("bl", 64, "float32"), ("le0", 192, "uint16"),
         ("le1", 144, "uint16"), ("le2", 96, "uint16"), ("li0", 12, "uint16"), ("li1", 10, "uint16"), ("li2", 6, "uint16"),
         ("ll0", 154, "uint16"), ("ll1", 102, "uint16"), ("ll2", 52, "uint16"), ("er", 288, "uint16"), ("il", 18, "uint16"),
         ("lr", 154, "uint16"), ("ert", 64, "float32"), ("dqi", 112, "float32"), ("ye0", TRW, "float32"), ("ye1", TRW, "float32"),
         ("ye2", TRW, "float32"), ("yl", TRW, "float32"), ("ac", 256, "float32"), ("yo", 256, "float32"),
-        ("sw0", 768, "bfloat16"), ("sw1", 768, "bfloat16"), ("sw2", 768, "bfloat16"), ("ft", 192, "bfloat16")):
+        ("sw0", 768, "bfloat16"), ("sw1", 768, "bfloat16"), ("sw2", 768, "bfloat16"), ("mk", 256, "bfloat16")):
     SCRATCH[_n] = ("sbuf", [128, _w], _t)
 for _k in "EFA":
-    for _n, _w, _t in (("of", 32, "uint16"), ("bn", 32, "uint16"), ("lt", 32, "uint16"), ("yy", 288, "bfloat16"),
-                       ("in", 256, "bfloat16"), ("mk", 256, "bfloat16"), ("xx", 256, "bfloat16"), ("vr", 256, "float32"),
-                       ("tw", 448, "float32"), ("xf", 128, "bfloat16")):
+    for _n, _w, _t in (("of", 64, "uint16"), ("bn", 32, "uint16"), ("yy", 288, "bfloat16"),
+                       ("in", 256, "bfloat16"), ("xx", 256, "bfloat16"), ("vr", 256, "float32"),
+                       ("tw", 544, "float32"), ("xf", 128, "bfloat16")):
         SCRATCH[_n + _k] = ("sbuf", [128, _w], _t)
 PS = ("E0", "E1", "F0", "F1", "A0", "A1", "psZ", "psI")
 for _k in PS:
@@ -48,7 +51,15 @@ SEMAPHORES = (["cV", "cP", "cS", "cG", "snt", "rx0", "rx1", "rx2"] + [a + str(s)
 
 
 def clean(regs):
-    return [(r[0], 0, 512) if r[0] in PS else tuple(r[:3]) for r in regs]
+    return [(r[0], (0, 512, 1)) if r[0] in PS else (r[0], tuple(r[1:4])) for r in regs]
+
+
+def meet(a, b):
+    return a[0] < b[1] and b[0] < a[1] and (a[2] != b[2] or (a[0] - b[0]) % a[2] == 0)
+
+
+def within(a, b):
+    return b[0] <= a[0] and a[1] <= b[1] and (b[2] == 1 or (a[2] == b[2] and (a[0] - b[0]) % a[2] == 0))
 
 
 def tracker(g, T):
@@ -59,13 +70,13 @@ def tracker(g, T):
     def need(q, reads, writes):
         out = []
         for kind, regs in (("r", clean(reads)), ("w", clean(writes))):
-            for b, lo, hi in regs:
+            for b, c in regs:
                 for e in acc.get(b, []):
-                    if e[0] < hi and lo < e[1]:
+                    if meet(e[0], c):
                         if b in PS:
-                            if e[3] != q or (q != "P" and "w" in (kind, e[2])):
+                            if e[2] != q or (q != "P" and "w" in (kind, e[1])):
                                 out.append(e)
-                        elif "w" in (kind, e[2]):
+                        elif "w" in (kind, e[1]):
                             out.append(e)
         return out
 
@@ -73,26 +84,26 @@ def tracker(g, T):
         k = know[q]
         top, imp = {}, {}
         for e in deps:
-            top[e[4]] = max(top.get(e[4], 0), e[5])
-            for s, v in e[6].items():
-                if s != e[4]:
+            top[e[3]] = max(top.get(e[3], 0), e[4])
+            for s, v in e[5].items():
+                if s != e[3]:
                     imp[s] = max(imp.get(s, 0), v)
         for s, v in top.items():
             if k.get(s, 0) >= v or imp.get(s, 0) >= v:
                 continue
             qs[q].wait_ge(T.sem[s], v)
         for e in deps:
-            k[e[4]] = max(k.get(e[4], 0), e[5])
-            for s, v in e[6].items():
+            k[e[3]] = max(k.get(e[3], 0), e[4])
+            for s, v in e[5].items():
                 k[s] = max(k.get(s, 0), v)
 
     def note(q, reads, writes, sem, val, snap):
         for kind, regs in (("r", clean(reads)), ("w", clean(writes))):
-            for b, lo, hi in regs:
+            for b, c in regs:
                 l = acc.setdefault(b, [])
                 if kind == "w":
-                    l[:] = [e for e in l if not (lo <= e[0] and e[1] <= hi)]
-                l.append((lo, hi, kind, q, sem, val, snap))
+                    l[:] = [e for e in l if not within(e[0], c)]
+                l.append((c, kind, q, sem, val, snap))
 
     def issue(o):
         q, reads, writes = o["q0"], o["r"], o["w"]
@@ -132,23 +143,23 @@ def links(ops):
     for i, o in enumerate(ops):
         d, q = {}, o["q"]
         for kind, regs in (("r", clean(o["r"])), ("w", clean(o["w"]))):
-            for b, lo, hi in regs:
+            for b, c in regs:
                 for e in acc.get(b, []):
-                    if e[0] < hi and lo < e[1] and e[4] != i:
-                        same = e[3] == q and q != "D"
+                    if meet(e[0], c) and e[3] != i and not (o.get("com") == b and ops[e[3]].get("com") == b):
+                        same = e[2] == q and q != "D"
                         if b in PS:
-                            lat = (C["same"] if q != "P" and "w" in (kind, e[2]) else 0.0) if same else C["cross"]
-                        elif "w" in (kind, e[2]):
+                            lat = (C["same"] if q != "P" and "w" in (kind, e[1]) else 0.0) if same else C["cross"]
+                        elif "w" in (kind, e[1]):
                             lat = C["same"] if same else C["cross"]
                         else:
                             continue
-                        d[e[4]] = max(d.get(e[4], 0.0), lat)
+                        d[e[3]] = max(d.get(e[3], 0.0), lat)
         for kind, regs in (("r", clean(o["r"])), ("w", clean(o["w"]))):
-            for b, lo, hi in regs:
+            for b, c in regs:
                 l = acc.setdefault(b, [])
-                if kind == "w":
-                    l[:] = [e for e in l if not (lo <= e[0] and e[1] <= hi)]
-                l.append((lo, hi, kind, q, i))
+                if kind == "w" and o.get("com") != b:
+                    l[:] = [e for e in l if not within(e[0], c)]
+                l.append((c, kind, q, i))
         o["d"] = d
 
 
@@ -176,23 +187,25 @@ def schedule(progs):
     for i in range(n):
         for j, lat in into[i]:
             out[j].append((i, lat))
-    left, last, pri = [len(l) for l in out], [i for i in range(n) if not out[i]], [0.0] * n
+    left, last, way = [len(l) for l in out], [i for i in range(n) if not out[i]], [0.0] * n
     for i in last:
-        pri[i] = ops[i]["t"] + max([pri[j] + lat for j, lat in out[i]] + [0.0])
+        way[i] = ops[i]["t"] + max([way[j] + lat for j, lat in out[i]] + [0.0])
         for j, _ in into[i]:
             left[j] -= 1
             if left[j] == 0:
                 last.append(j)
     best = None
-    for _ in range(ROUNDS):
-        end, seq, fin = arrange(ops, rank, into, out, pri)
-        if best is None or end < best[0]:
-            best = (end, seq)
-        pri = arrange(ops, rank, out, into, fin)[2]
+    for look in LOOKS:
+        pri = way
+        for _ in range(ROUNDS):
+            end, seq, fin = arrange(ops, rank, into, out, pri, look)
+            if best is None or end < best[0]:
+                best = (end, seq)
+            pri = arrange(ops, rank, out, into, fin, look)[2]
     return [[ops[i] for i in l] for l in best[1]]
 
 
-def arrange(ops, rank, into, out, pri):
+def arrange(ops, rank, into, out, pri, look):
     n = len(ops)
     deg, ready, fin = [len(l) for l in into], [0.0] * n, [0.0] * n
     pool, free, dfree, first = {}, {}, [0.0] * N, set()
@@ -227,7 +240,7 @@ def arrange(ops, rank, into, out, pri):
             f = free.get(key, 0.0)
             t0 = max(f, min(ready[i] for i in l))
             c = max((i for i in l if ready[i] <= t0), key=lambda i: (pri[i], -i))
-            lim = t0 + ops[c]["t"] * C["look"]
+            lim = t0 + ops[c]["t"] * look
             for i in l:
                 if t0 < ready[i] < lim and pri[i] > pri[c] + (ready[i] - t0):
                     c, lim = i, ready[i]
@@ -259,7 +272,10 @@ def program(g, q, T, topo):
     NA = N - 1 - q
     AC = 3 * NA
     CT = RES + AC * 2
+    Q1 = q + 1
     OFF = BIG - 8192.0 * q - 0.4375
+    if q == 0:
+        OFF = -0.4375
     cy = C["cyc"]
 
     def op(qq, fns, reads, writes, t, **kw):
@@ -308,21 +324,21 @@ def program(g, q, T, topo):
             op("S", [lambda: S.activation(ap(o), ap(w).indirect(ap(l)), AF.Copy)], [w, l], [o], 0.065 + cy * C["gg"] * wd(o))
 
     def sca(w, l, i):
-        op("V", [lambda: V.tensor_copy(ap(w).indirect(ap(l)), ap(i))], [l, i], [w], 0.05 + cy * C["sg"] * wd(i))
+        op("V", [lambda: V.tensor_copy(ap(w).indirect(ap(l)), ap(i))], [l, i], [w], 0.05 + cy * C["sg"] * wd(i), com=w[0])
 
-    def scan(o, m, i, op0=A.mult, op1=A.add):
-        op("V", [lambda: V.tensor_tensor_scan(ap(o), ap(m), ap(i), 0.0, op0, op1)], [m, i], [o], tv(wd(o), 1))
+    def scan(o, m, i, op0=A.add, op1=A.max, f=1):
+        op("V", [lambda: V.tensor_tensor_scan(ap(o), ap(m), ap(i), 0.0, op0, op1)], [m, i], [o], tv(wd(o), f))
 
     def fill(o, c):
         op("V", [lambda: V.memset(ap(o), c)], [], [o], tv(wd(o), 0.5 if short(o) else 1))
 
-    def act(o, i, scale=1.0, bias=None):
+    def act(o, i, scale=1.0, bias=None, func=AF.Identity):
         t = 0.06 + cy * wd(o)
         more = [x for x in (scale, bias) if isinstance(x, tuple)]
         if bias:
-            op("S", [lambda: S.activation(ap(o), ap(i), AF.Identity, bias=ap(bias), scale=ap(scale))], [i] + more, [o], t)
+            op("S", [lambda: S.activation(ap(o), ap(i), func, bias=ap(bias), scale=ap(scale))], [i] + more, [o], t)
         elif more:
-            op("S", [lambda: S.activation(ap(o), ap(i), AF.Identity, scale=ap(scale))], [i] + more, [o], t)
+            op("S", [lambda: S.activation(ap(o), ap(i), func, scale=ap(scale))], [i] + more, [o], t)
         else:
             op("S", [lambda: S.activation(ap(o), ap(i), AF.Copy, scale=scale)], [i], [o], t)
 
@@ -366,14 +382,14 @@ def program(g, q, T, topo):
                 + [(M3(lname, r), (src, s0 + r, s1, 4)) for r in range(4)])
 
     def unquad(ps, n, o):
-        scan(B(o, 0, 4 * n), B("rq", 0, 4 * n), B(ps, 0, 4 * n), A.add, A.max)
+        scan(B(o, 0, 4 * n), B("rq", 0, 4 * n), B(ps, 0, 4 * n))
         return B(o, 3, 4 * n, 4)
 
     def low(n):
         return (idb, B("nma", 0, n))
 
     def diag(ps, n, o):
-        scan(B(o, 0, n), B("r16", 0, n), B(ps, 0, n), A.add, A.max)
+        scan(B(o, 0, n), B("r16", 0, n), B(ps, 0, n))
         return B(o, 15, n, 16)
 
     load("Y", B("enw"), "en")
@@ -426,6 +442,8 @@ def program(g, q, T, topo):
         act(B("nb"), bk, -1.0)
         aff(B("nt"), B("nb"), [[-1, 128]], A.is_gt, 0, 1)
         aff(B("nu"), B("nt"), [[-1, 128]], A.not_equal, 0, 1, -2048.0)
+        ts(col("p1"), col("p"), 1.0, None, A.add)
+        act(B("dp"), idb, col("p1"))
     act(B("lb4f"), B("zz", 0, 512))
     act(B("lb4"), B("zz", 0, 512))
     for r in range(4):
@@ -442,8 +460,9 @@ def program(g, q, T, topo):
         aff(M3("sel", k), M3("s89", 0), [[-16, 8], [-2, 16]], A.is_equal, -k, 1)
         aff(M3("sel", 2 + k), M3("s89", 1), [[-16, 8], [-2, 16]], A.is_equal, 16 - k, 1)
     if q:
-        iota(B("trn", 0, CT), [[16, CT]], CAP * q - 2047, 1)
-        iota(B("k48", 0, q * CT), [[CAP, q], [0, CT]], 0, 0)
+        iota(B("k48", 0, Q1 * CT), [[0, CT], [CAP, Q1]], 0, 0)
+        iota(B("trn", 0, CT), [[16, CT]], CAP * q - 2048, 0)
+        act(B("k48", q, Q1 * CT, Q1), B("trn", 0, CT))
         act(B("br"), B("zz", 0, 384))
         for j in range(3):
             act(B("br", 129 * j + 10, 128 * j + 128, 16), B("bk4", 10 + j, 128, 16))
@@ -486,14 +505,16 @@ def program(g, q, T, topo):
     act(B("hi"), B("psZ"))
     fill(B("csb", 4096, 4112), 0)
     fill(B("lsb", 4096, 4112), 0.0)
-    ts(B("bl", 0, 16), B("enw"), 0.125, -0.4375 - 8192.0 * q, A.mult, A.add)
     if q:
-        fill(B("rm", 0, q * CT), 1.0)
+        fill(B("rm", 0, Q1 * CT), 0.0)
+        fill(B("rm", 0, Q1 * CT, Q1), -2 * LOW)
+        fill(B("kx", 0, Q1 * CT), 0.0)
+        fill(B("kx", q, Q1 * CT, Q1), 1.0)
         fill(B("ft"), 0.0)
+        for x in "EFA" if NA else "E":
+            fill(B("xf" + x), 0.0)
         for t in range(3):
             fill(B("sw%d" % t, 0, CAP * q), 0.0)
-        for d in range(1, q):
-            fill(B("rm", d * CT, d * CT + 1), 0.0)
     tt(B("lo"), B("psZ"), B("hi"), A.subtract)
     mm(B("A1"), [(M3("sel", 0), B("hi")), (M3("sel", 2), B("lo"))])
     act(B("bmp", 0, 512), B("A1"), 0.03125)
@@ -501,156 +522,182 @@ def program(g, q, T, topo):
     act(B("bmp", 512, 1024), B("psI"), 0.03125)
     dma("Y", [lambda s=s: g.sync.dma_start(T.win[s::8, 1024 * s:1024 * s + 1024], T.bmp[s::8, :]) for s in range(8)],
         [B("bmp"), B("win")], [B("win")], 262144)
+    wt = oh(4)
+    for k in (3, 2, 1, 0):
+        act(col("w%d" % k), wt, 16.0, oh(k))
+        wt = col("w%d" % k)
+    ts(col("f9"), col("o"), 10.0, None, A.is_ge)
+    ts(col("e9"), col("o"), 12.0, col("f9"), A.is_le, A.mult)
+    act(col("u1"), wt, 0.125, col("e9"))
+    if q:
+        act(col("cb"), oh(13), -BIG, col("u1"))
+    act(B("lbe"), B("lb4"), col("cb" if q else "u1"))
     if NA:
-        wt = oh(4)
-        for k in (3, 2, 1, 0):
-            act(col("w%d" % k), wt, 16.0, oh(k))
-            wt = col("w%d" % k)
-        ts(col("f9"), col("o"), 10.0, None, A.is_ge)
         ts(B("nma"), B("jm", 0, 144), col("o"), LOW, A.not_equal, A.mult)
         ts(B("r16"), B("jm", 0, 144), 0.0, 2 * LOW, A.is_equal, A.mult)
-        ts(col("e9"), col("o"), 12.0, col("f9"), A.is_le, A.mult)
-        act(col("u1"), wt, 0.125, col("e9"))
-        act(col("cb"), oh(13), -BIG, col("u1"))
-        act(B("be"), bk, col("cb"))
+        act(B("be"), bk, col("cb" if q else "u1"))
         act(col("u3"), oh(15), 256.0, oh(14))
         act(col("cid"), oh(13), -2048.0, col("u3"))
         act(B("lid"), B("lb4"), col("cid"))
     ts(col("o16"), col("o"), 16.0, None, A.mult)
     ts(B("prm"), B("ci"), col("o16"), None, A.add)
     if q:
-        for s in range(q):
-            act(B("ye%d" % s, 256 * q, 256 * q + 256), B("zz", 0, 256))
-        act(B("yl", 256 * q, 256 * q + 256), B("zz", 0, 256))
+        for n in ["ye%d" % s for s in range(q)] + ["yl"]:
+            iota(B(n, 256 * q, 256 * q + 256), [[0, 256]], 0, 0)
 
     def tw(x, k, n):
         return B("tw" + x, 288 + 32 * k, 288 + 32 * k + n)
 
-    def vrep(x, t, s0, s1):
-        mm(B(x + "1", 0, s1 - s0), [(M3("bv", t), B("z", s0, s1))])
-        act(B("vr" + x, 0, s1 - s0), B(x + "1", 0, s1 - s0))
+    def sg(t):
+        return B("sg", 256 * t, 256 * t + 256)
 
-    def buckets(x, c0, c1):
-        ts(B("of" + x, 0, c1 - c0), B("bl", c0, c1), 8191.0, 0.0, A.min, A.max)
+    def vrep(x, t, s0, s1, copy):
+        o = B(x + "1", 256, 256 + s1 - s0)
+        mm(o, [(M3("bv", t), B("z", s0, s1))])
+        if copy:
+            act(B("vr" + x, 0, s1 - s0), o)
+
+    def buckets(x, src):
+        ts(B("of" + x, 0, wd(src)), src, 8191.0, 0.0, A.min, A.max)
 
     def sums(x, row, c0, c1, fresh):
         m = 16 * (c1 - c0)
         if fresh:
-            return [low(m)] + ([(B("be"), B("z", 16 * c0, 16 * c1))] if q else []) + [(bk, row)], m, 1
-        if x == "E" or m > 144:
+            return [low(m), (B("be"), B("z", 16 * c0, 16 * c1)), (bk, row)], m, 1
+        if m > 144:
             return quad("lb4", row[0], 0, m), m // 4, 4
         return [low(m), (bk, row)], m, 1
 
     def wrapped(x, n, w):
         return unquad(x + "0", n, "tw" + x) if w < 16 * n else diag(x + "0", w, "tw" + x)
 
-    def bins(x, c0, c1, fresh=False):
+    def bins(x, c0, c1):
         n = c1 - c0
         m = 16 * n
         yy, bn = B("yy" + x, 0, m), B("bn" + x, 0, n)
+        fresh = x == "A" and q
         L, w, late = sums(x, yy, c0, c1, fresh)
         mm(B(x + "0", 0, w), L, 0, len(L) - late)
-        cpg(yy, B("win"), B("of" + x, 0, n), "S" if m > 64 and not fresh else "V")
+        cpg(yy, B("win"), B("of" + x, 0, n), "S" if m > 64 and x != "A" else "V")
         mm(B(x + "0", 0, w), L, len(L) - late)
         s = wrapped(x, n, w)
-        if fresh and q:
+        if fresh:
             ts(bn, s, OFF, 4096.0, A.add, A.min)
         else:
             tt(tw(x, 0, n), s, B("bl", c0, c1), A.add)
             ts(bn, tw(x, 0, n), 4096.0, 0.0, A.min, A.max)
 
-    def tally(x, c0, c1, first):
-        o = B("tal", 16 * c0, 16 * c1)
-        if first:
-            cpg(o, B("csb"), B("bn" + x, 0, c1 - c0), "S")
+    def tally(x, t, c0, c1):
+        bn, o = B("bn" + x, 0, c1 - c0), B("tal", 16 * c0, 16 * c1)
+        if x == "E":
+            cpg(sg(t), B("csb"), bn, "S")
+        elif x == "A":
+            cpg(o, B("csb"), bn, "S")
         else:
-            ttg(o, B("csb"), B("bn" + x, 0, c1 - c0), o, A.add)
+            ttg(o, B("csb"), bn, o, A.add)
 
-    def event(x, t, c0, c1, first, fresh=False):
+    def event(x, t, c0, c1):
         n, s0, s1 = c1 - c0, 16 * c0, 16 * c1
         m = 16 * n
-        p0, p1 = x + "0", x + "1"
-        row, zr = B("xx" + x, 0, m), B("z", s0, s1)
-        ttg(B("in" + x, 0, m), B("csb"), B("bn" + x, 0, n), B("vr" + x, 0, m), A.is_le)
-        mm(B(p1, 0, m), [(bk, B("in" + x, 0, m))])
-        L, w, late = sums(x, row, c0, c1, fresh)
+        p0, p1, fresh = x + "0", x + "1", x == "A" or t == 0
+        row, zr, bn, hit = B("xx" + x, 0, m), B("z", s0, s1), B("bn" + x, 0, n), B("in" + x, 0, m)
+        ks, mp = B(p1, 0, m), B(p1, 256, 256 + m)
+        if x == "E" and t:
+            tally(x, t, c0, c1)
+            tt(hit, sg(t), mp, A.is_le)
+        else:
+            ttg(hit, B("csb"), bn, B("vr" + x, 0, m), A.is_le)
+        mm(ks, [(bk, hit)])
+        L, w, late = sums(x, row, c0, c1, x == "A")
+        if t == 0:
+            L[1:1] = [(M3("lbe", r), ("z", r, m, 4)) for r in range(4)]
         mm(B(p0, 0, w), L, 0, len(L) - late)
-        tally(x, c0, c1, first)
-        ts(B("mk" + x, 0, m), B(p1, 0, m), col("o"), -0.125, A.is_equal, A.mult)
-        ttg(row, B("lsb"), B("bn" + x, 0, n), B("mk" + x, 0, m), A.mult)
+        if t == 0:
+            tally(x, t, c0, c1)
+            ts(B("mk", 0, m), ks, col("o"), -0.125, A.is_equal, A.mult)
+            ttg(row, B("lsb"), bn, B("mk", 0, m), A.mult)
+        else:
+            k = 256 * "EFA".index(x)
+            gl = B("gl", k, k + m)
+            cpg(gl, B("lsb"), bn, "S")
+            if x != "E":
+                tally(x, t, c0, c1)
+            ts(mp, ks, col("o"), -0.125, A.is_equal, A.mult)
+            tt(row, gl, mp, A.mult)
         mm(B(p0, 0, w), L, len(L) - late)
         en, off = wrapped(x, n, w), OFF
+        if t == 0:
+            ts(B("ofE", 0, RES), en, OFF, 8191.0, A.add, A.min)
+        if q == 0 and fresh:
+            ts(B("bl", c0, c1), en, OFF, -0.4375, A.add, A.max)
+            return
         if not fresh:
             tt(tw(x, 1, n), en, B("bl", c0, c1), A.add)
             en, off = tw(x, 1, n), 0.0
         if q == 0:
-            if fresh:
-                tt(tw(x, 2, n), en, B("bl", c0, c1), A.add)
-                en = tw(x, 2, n)
             ts(B("bl", c0, c1), en, -0.4375, 0.0, A.max, A.add)
             return
-        f0, W = 64 * t, q * CT
-        xs = B("xf" + x, 0, W)
-
-        def af(s):
-            return B("xf" + x, 64 + s * n, 64 + s * n + n)
+        f0, a, b = 72 * t, c0 * Q1, c1 * Q1
 
         def thr(s):
             return 8192.0 * (s + 1 - q) - 0.5 - off
 
-        def fcol(s):
-            return B("ft", f0 + s * CT + c0, f0 + s * CT + c1)
-        ts(fcol(0), en, thr(0), None, A.is_lt)
+        def to(s):
+            return B("ft", f0 + a + s, f0 + b, Q1)
+
+        def under(s, lo, hi):
+            return B("th", f0 + s * CT + lo, f0 + s * CT + hi) if s else B("ft", f0 + lo * Q1, f0 + hi * Q1, Q1)
+        for s in range(q):
+            ts(under(s, c0, c1), en, thr(s), None, A.is_lt)
+        pl = B(p0, 0, b - a)
+        L2 = [(idb, B("k48", a, b)), (B("dp"), B("kx", a, b)), (B("nu"), B("ft", f0 + a, f0 + b)), (bk, B("xf" + x, a, b))]
+        mm(pl, L2, 0, 2)
+        for s in range(q):
+            scan(B("xf" + x, s, b, Q1), under(s, 0, c1), under(s - 1, 0, c1) if s else B("zz", 0, c1), A.add, A.subtract, 0.5)
         for s in range(1, q):
-            ts(af(s), en, thr(s), None, A.is_lt)
-        for s in range(1, q):
-            tt(fcol(s), af(s), fcol(0) if s == 1 else af(s - 1), A.subtract)
-        fW = B("ft", f0, f0 + W)
-        L2 = [(idb, B("k48", 0, W)), (B("nu"), fW), (bk, xs)]
-        mm(B(p0, 0, W), L2, 0, 1)
-        scan(xs, B("rm", 0, W), fW)
-        mm(B(p0, 0, W), L2, 1, 2)
-        mm(B(p0, 0, W), L2, 2)
-        ts(tw(x, 3, n), en, thr(q - 1), BIG, A.is_lt, A.mult)
+            tt(to(s), under(s, c0, c1), under(s - 1, c0, c1), A.subtract)
+        mm(pl, L2, 2, 3)
+        mm(pl, L2, 3)
+        act(tw(x, 3, n), en, -16 * BIG, 16 * BIG * thr(q - 1), AF.Relu)
         if fresh:
-            ts(tw(x, 2, n), en, off, None, A.add)
+            act(tw(x, 2, n), en, 1.0, off)
             en = tw(x, 2, n)
         tt(B("bl", c0, c1), en, tw(x, 3, n), A.add)
-        lf = tw(x, 4, n)
-        for d in range(q):
-            tt(lf, B(p0, d * CT + c0, d * CT + c1), B("trn", c0, c1) if d == 0 else lf, A.min)
-        ts(B("lt" + x, 0, n), lf, 2047.0, None, A.add)
-        mm(B("psZ", 0, m), [(idb, zr), (M3("br", t), row)])
-        act(zr, B("psZ", 0, m))
-        sca(B("sw%d" % t, 0, CAP * q + 16 * CT + 128), B("lt" + x, 0, n), zr)
+        scan(B("tw" + x, 448, 448 + b - a), B("rm", 0, b - a), pl, A.add, A.min)
+        ts(B("of" + x, 32, 32 + n), B("tw" + x, 448 + q, 448 + b - a, Q1), 2047.0, None, A.add)
+        k = 8 if m > 144 else n
+        for i in range(0, n, k):
+            o, h = B("psZ", 16 * i, 16 * (i + k)), B("z", s0 + 16 * i, s0 + 16 * (i + k))
+            L3 = [(idb, h), (M3("br", t), B("xx" + x, 16 * i, 16 * (i + k)))]
+            mm(o, L3, 0, 1)
+            mm(o, L3, 1, 2)
+            act(h, o)
+        for i in range(0, n, k):
+            sca(B("sw%d" % t, 0, CAP * q + 16 * CT + 128), B("of" + x, 32 + i, 32 + i + k), B("z", s0 + 16 * i, s0 + 16 * (i + k)))
 
-    def calls(dests):
-        two = dests[-2:]
-        out = [[(d, 8 // len(two)) for d in two]]
-        return out + [[(d, 8)] for d in dests[:-2]]
+    def split(s, kind):
+        d = list(range(s))[::-1] if kind == "rx" else list(range(s + 1, N))[::-1]
+        groups = {"rx": [[x] for x in d], "ri": [d]}.get(kind, [d[:2], d[2:]])
+        return [list(zip(x, {1: (8,), 2: (4, 4), 3: (4, 2, 2)}[len(x)])) for x in groups if x]
 
-    def fused(dests, src, dst, rsem):
-        for call in calls(dests):
-            top = max(d for d, w in call)
-            sd = [(d, w, src(d, top), dst(d, top)) for d, w in call]
+    def width(s, d, kind):
+        return [w for x in split(s, kind) for y, w in x if y == d][0]
+
+    def send(src, dst, rsem):
+        for call in split(q, rsem[:2]):
+            sd = [(d, w, src(d, call[0][0]), dst(d, call[0][0])) for d, w in call]
 
             def go(sd=sd):
                 e = topo.engines(core, T.cores[sd[0][0]])
                 tr, pos = [], 0
                 for d, w, a, b in sd:
-                    m = 0
-                    for k in e[pos:pos + w]:
-                        m |= 1 << k
-                    pos += w
                     rid, pid, _ = topo.addr(T.cores[d])
-                    tr.append(RemoteDMATransfer(dst_ids=[DstId(rid=rid, pnc=pid)], dma_engine_mask=m, remote_sem=T.sem[rsem],
-                                                src=ap(a), dst=ap(b)))
+                    tr.append(RemoteDMATransfer(dst_ids=[DstId(rid=rid, pnc=pid)], remote_sem=T.sem[rsem], src=ap(a), dst=ap(b),
+                                                dma_engine_mask=sum(1 << k for k in e[pos:pos + w])))
+                    pos += w
                 g.remote_dma_fused(tr, local_sem=T.sem.snt)
             op("G", [go], [x[2] for x in sd], [], C["rissue"], k="send", sem=rsem, to=[x[0] for x in sd],
                by=256 * sum(wd(x[2]) for x in sd), val=sum(x[1] for x in sd))
-
-    def width(dests, d):
-        return [w for c in calls(dests) for x, w in c if x == d][0]
 
     def landed(sem, val, regs):
         op("R", [], [], regs, 0.0, k="land", sem=sem, val=val)
@@ -663,87 +710,89 @@ def program(g, q, T, topo):
         tt(er, unquad(ps, n, tmp), B("trd", 0, n), A.min)
         ts(B(out, 0, n), er, 2048.0, None, A.add)
 
-    up, down = list(range(q + 1, N)), list(range(q))
     for t in range(EV):
         if t < 3:
+            if t == 2:
+                buckets("E", tw("E", 1, RES))
+            vrep("E", t, 0, 256, t == 0)
             if t:
-                buckets("E", 0, RES)
                 bins("E", 0, RES)
-            vrep("E", t, 0, 256)
-            event("E", t, 0, RES, t == 0)
+            event("E", t, 0, RES)
         if t == 2 and NA:
-            buckets("F", RES, RES + AC)
-            vrep("F", t, 256, 256 + 16 * AC)
+            buckets("F", B("bl", RES, RES + AC))
+            vrep("F", t, 256, 256 + 16 * AC, True)
             bins("F", RES, RES + AC)
-            event("F", t, RES, RES + AC, False)
+            event("F", t, RES, RES + AC)
         if t == 3 and NA:
-            ce = RES + AC * 2
-            buckets("F", RES, ce)
-            bins("F", RES, ce)
-            tally("F", RES, ce, False)
-            cp(B("er", 0, 32 * AC), B("tal", 256, 256 + 32 * AC))
+            for a in (RES, RES + AC):
+                buckets("F", tw("F", 1, AC) if a == RES else B("bl", a, a + AC))
+                bins("F", a, a + AC)
+                tally("F", t, a, a + AC)
+                cp(B("er", 16 * (a - RES), 16 * (a - RES + AC)), B("tal", 16 * a, 16 * (a + AC)))
             w = 16 * (AC + 3)
-            fused(up, lambda d, m: B("er", CAP * (d - q - 1), CAP * (d - q - 1) + w), lambda d, m: B("le%d" % q, 0, w), "re%d" % q)
+            send(lambda d, m: B("er", CAP * (d - q - 1), CAP * (d - q - 1) + w), lambda d, m: B("le%d" % q, 0, w), "re%d" % q)
         if t and NA:
             c0 = RES + AC * (t - 1)
             c1 = c0 + AC
             zr = B("z", 16 * c0, 16 * c1)
             n = 16 * AC
-            landed("rx%d" % (t - 1), sum(width(list(range(r)), q) for r in range(q + 1, N)), [zr])
+            landed("rx%d" % (t - 1), sum(width(r, q, "rx") for r in range(q + 1, N)), [zr])
             U = [low(n), (B("be"), zr)]
             mm(B("A0", 0, n), U, 0, 1)
             mm(B("A0", 0, n), U, 1)
             if t < 3:
-                vrep("A", t, 16 * c0, 16 * c1)
+                vrep("A", t, 16 * c0, 16 * c1, True)
             ts(B("ofA", 0, AC), diag("A0", n, "twA"), OFF, 8191.0, A.add, A.min)
             if q == 0:
                 ts(B("bl", c0, c1), B("twA", 15, n, 16), OFF, -0.4375, A.add, A.max)
-            bins("A", c0, c1, True)
+            bins("A", c0, c1)
             if t < 3:
-                event("A", t, c0, c1, True, True)
+                event("A", t, c0, c1)
             else:
                 mm(B("A1", 0, 4 * AC), quad("lid", "z", 16 * c0, 16 * c1))
                 cpg(B("lr", AC, AC + n), B("csb"), B("bnA", 0, AC))
-                places(AC, "lr", 1, "A1", "twA")
-                fused(up, lambda d, m: B("lr", 0, AC + CAP * (m - q)), lambda d, m: B("ll%d" % q, 0, AC + CAP * (m - q)), "rl%d" % q)
+                places(AC, "lr", 1, "A1", "dqi")
+                send(lambda d, m: B("lr", 0, AC + CAP * (m - q)), lambda d, m: B("ll%d" % q, 0, AC + CAP * (m - q)), "rl%d" % q)
         if t < 3 and q:
-            fused(down, lambda d, m: B("sw%d" % t, CAP * d, CAP * d + CAP), lambda d, m: B("z", zcol(d, t, q), zcol(d, t, q) + CAP), "rx%d" % t)
+            send(lambda d, m: B("sw%d" % t, CAP * d, CAP * d + CAP), lambda d, m: B("z", zcol(d, t, q), zcol(d, t, q) + CAP), "rx%d" % t)
         if NA and t == 2:
             k = 2 * AC
             mm(B("psI", 0, 4 * k), quad("lid", "z", 256, 256 + 16 * k))
             places(k, "il", 0, "psI", "dqi")
-            w = AC + 3
-            fused(up, lambda d, m: B("il", 3 * (d - q - 1), 3 * (d - q - 1) + w), lambda d, m: B("li%d" % q, 0, w), "ri%d" % q)
+            send(lambda d, m: B("il", 3 * (d - q - 1), 3 * (d - q - 1) + AC + 3), lambda d, m: B("li%d" % q, 0, AC + 3), "ri%d" % q)
 
-    buckets("E", 0, RES)
+    buckets("E", tw("E", 1, RES))
     bins("E", 0, RES)
-    tally("E", 0, RES, False)
+    tally("E", 3, 0, RES)
     own = 256 * q
 
     def leave(h):
         lo, hi = 128 * h, 128 * h + 128
         dma("YS"[h], [lambda: (g.scalar if h else g.sync).dma_start(T.y[:, lo:hi], T.yo[:, lo:hi])], [B("yo", lo, hi)], [], 65536)
 
+    out = B("ac" if q else "yo")
+    cpg(out, sg(0), B("prm"), "S")
+    for t in range(1, EV):
+        ttg(out, sg(t), B("prm"), out, A.add)
     if q == 0:
-        cpg(B("yo"), B("tal", 0, 256), B("prm"))
         for h in range(2):
             leave(h)
     else:
-        cpg(B("ac"), B("tal", 0, 256), B("prm"))
+        sm = B("psI", 0, 256)
+        act(sm, out)
         for s in range(q - 1, -1, -1):
             n = 3 * (N - s)
-            w = width(list(range(s + 1, N)), q)
-            landed("ri%d" % s, w, [B("li%d" % s)])
-            landed("re%d" % s, w, [B("le%d" % s)])
+            landed("ri%d" % s, width(s, q, "ri"), [B("li%d" % s)])
+            landed("re%d" % s, width(s, q, "re"), [B("le%d" % s)])
             sca(B("ye%d" % s), B("li%d" % s, 0, n), B("le%d" % s, 0, 16 * n))
-            tt(B("ac"), B("ac"), B("ye%d" % s, own, own + 256), A.add)
+            tt(sm, sm, B("ye%d" % s, own, own + 256), A.add)
         for s in range(q - 1, -1, -1):
             a, n = 3 * (N - 1 - s), 3 * (q - s)
-            landed("rl%d" % s, width(list(range(s + 1, N)), q), [B("ll%d" % s)])
+            landed("rl%d" % s, width(s, q, "rl"), [B("ll%d" % s)])
             sca(B("yl"), B("ll%d" % s, 0, n), B("ll%d" % s, a, a + 16 * n))
         for h in range(2):
             lo, hi = 128 * h, 128 * h + 128
-            tt(B("yo", lo, hi), B("ac", lo, hi), B("yl", own + lo, own + hi), A.add)
+            tt(B("yo", lo, hi), B("psI", lo, hi), B("yl", own + lo, own + hi), A.add)
             leave(h)
     return ops
 

from concourse.bass import DstId, RemoteDMATransfer
from concourse.mybir import AluOpType as A, ActivationFunctionType as AF

N, CAP, EV, RES = 4, 48, 4, 16
BIG = 131072.0
LOW = -524288.0
TRW = 1456
ZF = "VVVSSSGG"
LOOKS, ROUNDS = (0.4, 0.5, 0.55, 0.6, 0.65, 0.7, 0.8), 6
C = dict(cyc=1.0e-3, same=0.10, cross=0.17, dissue=0.06, dlat=0.6, drate=300e3, rissue=0.7, rstart=0.6, rhop=0.6,
         rrate=60e3, first=1.4, gg=1.5, sg=3.5)

SCRATCH = {}
for _n, _w, _t in (
        ("bmr", 512, "int32"), ("bmh", 512, "int32"), ("kt", 512, "float32"), ("t5", 512, "float32"), ("hi", 512, "bfloat16"),
        ("lo", 512, "bfloat16"), ("bmp", 1024, "bfloat16"), ("win", 8192, "bfloat16"), ("one", 128, "bfloat16"),
        ("zz", 1024, "bfloat16"), ("nb", 128, "bfloat16"),
        ("s89", 256, "bfloat16"), ("sel", 512, "bfloat16"), ("csb", 4112, "int32"), ("lsb", 4112, "bfloat16"),
        ("mg4", 128, "bfloat16"), ("bk4", 128, "bfloat16"), ("lb4", 512, "bfloat16"), ("lb4f", 512, "float32"),
        ("lid", 512, "bfloat16"), ("lbe", 512, "bfloat16"), ("bkf", 128, "float32"), ("fz", 256, "float32"),
        ("s5", 8, "float32"), ("dg", 512, "int32"),
        ("nm", 112, "bfloat16"), ("rq", 112, "float32"), ("m4", 112, "float32"),
        ("nma", 144, "bfloat16"), ("jm", 256, "float32"), ("dm", 256, "float32"), ("r16", 144, "float32"),
        ("enw", 16, "int32"), ("sdw", 16, "int32"), ("wi", 16, "int32"), ("iw", 80, "int32"),
        ("ge", 256, "float32"), ("gv", 256, "float32"), ("gs", 256, "bfloat16"),
        ("gm", 256, "float32"), ("ms", 256, "bfloat16"), ("pl", 256, "bfloat16"), ("ki", 256, "bfloat16"),
        ("pi", 4, "int32"), ("ci", 16, "int32"), ("jcl", 16, "uint16"), ("prm", 16, "uint16"), ("j16", 16, "float32"),
        ("oh", 16, "float32"), ("cc", 64, "float32"), ("mi", 128, "bfloat16"), ("idb", 128, "bfloat16"),
        ("nu", 128, "bfloat16"), ("dp", 128, "bfloat16"), ("k48", 96, "bfloat16"), ("kx", 96, "bfloat16"),
        ("nt", 128, "bfloat16"), ("bv", 384, "bfloat16"), ("br", 384, "bfloat16"), ("be", 128, "bfloat16"),
        ("trn", 32, "float32"), ("trd", 32, "float32"), ("rm", 96, "float32"), ("th", 216, "bfloat16"), ("ft", 216, "bfloat16"),
        ("sg", 1024, "float32"), ("gl", 768, "bfloat16"), ("z", 704, "bfloat16"), ("tal", 704, "float32"),
        ("bl", 64, "float32"), ("le0", 192, "uint16"),
        ("le1", 144, "uint16"), ("le2", 96, "uint16"), ("li0", 12, "uint16"), ("li1", 10, "uint16"), ("li2", 6, "uint16"),
        ("ll0", 154, "uint16"), ("ll1", 102, "uint16"), ("ll2", 52, "uint16"), ("er", 288, "uint16"), ("il", 18, "uint16"),
        ("lr", 154, "uint16"), ("ert", 64, "float32"), ("dqi", 112, "float32"), ("ye0", TRW, "float32"), ("ye1", TRW, "float32"),
        ("ye2", TRW, "float32"), ("yl", TRW, "float32"), ("ac", 256, "float32"), ("yo", 256, "float32"),
        ("sw0", 768, "bfloat16"), ("sw1", 768, "bfloat16"), ("sw2", 768, "bfloat16"), ("mk", 256, "bfloat16")):
    SCRATCH[_n] = ("sbuf", [128, _w], _t)
for _k in "EFA":
    for _n, _w, _t in (("of", 64, "uint16"), ("bn", 32, "uint16"), ("yy", 288, "bfloat16"),
                       ("in", 256, "bfloat16"), ("xx", 256, "bfloat16"), ("vr", 256, "float32"),
                       ("tw", 544, "float32"), ("xf", 128, "bfloat16")):
        SCRATCH[_n + _k] = ("sbuf", [128, _w], _t)
PS = ("E0", "E1", "F0", "F1", "A0", "A1", "psZ", "psI")
for _k in PS:
    SCRATCH[_k] = ("psum", [128, 512], "float32")

SEMAPHORES = (["cV", "cP", "cS", "cG", "snt", "rx0", "rx1", "rx2"] + [a + str(s) for a in ("ri", "re", "rl") for s in range(3)]
              + ["d%d" % i for i in range(16)])


def clean(regs):
    return [(r[0], (0, 512, 1)) if r[0] in PS else (r[0], tuple(r[1:4])) for r in regs]


def meet(a, b):
    return a[0] < b[1] and b[0] < a[1] and (a[2] != b[2] or (a[0] - b[0]) % a[2] == 0)


def within(a, b):
    return b[0] <= a[0] and a[1] <= b[1] and (b[2] == 1 or (a[2] == b[2] and (a[0] - b[0]) % a[2] == 0))


def tracker(g, T):
    qs = {"V": g.vector, "P": g.tensor, "S": g.scalar, "Y": g.sync, "G": g}
    cnt, acc, nd = {}, {}, [0]
    know = {q: {} for q in qs}

    def need(q, reads, writes):
        out = []
        for kind, regs in (("r", clean(reads)), ("w", clean(writes))):
            for b, c in regs:
                for e in acc.get(b, []):
                    if meet(e[0], c):
                        if b in PS:
                            if e[2] != q or (q != "P" and "w" in (kind, e[1])):
                                out.append(e)
                        elif "w" in (kind, e[1]):
                            out.append(e)
        return out

    def wait(q, deps):
        k = know[q]
        top, imp = {}, {}
        for e in deps:
            top[e[3]] = max(top.get(e[3], 0), e[4])
            for s, v in e[5].items():
                if s != e[3]:
                    imp[s] = max(imp.get(s, 0), v)
        for s, v in top.items():
            if k.get(s, 0) >= v or imp.get(s, 0) >= v:
                continue
            qs[q].wait_ge(T.sem[s], v)
        for e in deps:
            k[e[3]] = max(k.get(e[3], 0), e[4])
            for s, v in e[5].items():
                k[s] = max(k.get(s, 0), v)

    def note(q, reads, writes, sem, val, snap):
        for kind, regs in (("r", clean(reads)), ("w", clean(writes))):
            for b, c in regs:
                l = acc.setdefault(b, [])
                if kind == "w":
                    l[:] = [e for e in l if not within(e[0], c)]
                l.append((c, kind, q, sem, val, snap))

    def issue(o):
        q, reads, writes = o["q0"], o["r"], o["w"]
        if o["k"] == "op":
            wait(q, need(q, reads, writes))
            for f in o["f"][:-1]:
                f()
            s = "c" + q
            o["f"][-1]().then_inc(T.sem[s], 1)
            cnt[s] = cnt.get(s, 0) + 1
            note(q, reads, writes, s, cnt[s], dict(know[q]))
        elif o["k"] == "dma":
            s = "d%d" % nd[0]
            nd[0] += 1
            wait(q, need(q, reads, writes))
            for f in o["f"]:
                f().then_inc(T.sem[s], 16)
            cnt[s] = 16 * len(o["f"])
            note("D", reads, writes, s, cnt[s], dict(know[q]))
        elif o["k"] == "land":
            note("R", [], writes, o["sem"], o["val"], {})
            cnt[o["sem"]] = o["val"]
        else:
            wait(q, need(q, reads, []))
            o["f"][0]()
            cnt["snt"] = cnt.get("snt", 0) + o["val"]

    def finish():
        for s, v in cnt.items():
            g.wait_ge(T.sem[s], v)

    return issue, finish


def links(ops):
    acc = {}
    for i, o in enumerate(ops):
        d, q = {}, o["q"]
        for kind, regs in (("r", clean(o["r"])), ("w", clean(o["w"]))):
            for b, c in regs:
                for e in acc.get(b, []):
                    if meet(e[0], c) and e[3] != i and not (o.get("com") == b and ops[e[3]].get("com") == b):
                        same = e[2] == q and q != "D"
                        if b in PS:
                            lat = (C["same"] if q != "P" and "w" in (kind, e[1]) else 0.0) if same else C["cross"]
                        elif "w" in (kind, e[1]):
                            lat = C["same"] if same else C["cross"]
                        else:
                            continue
                        d[e[3]] = max(d.get(e[3], 0.0), lat)
        for kind, regs in (("r", clean(o["r"])), ("w", clean(o["w"]))):
            for b, c in regs:
                l = acc.setdefault(b, [])
                if kind == "w" and o.get("com") != b:
                    l[:] = [e for e in l if not within(e[0], c)]
                l.append((c, kind, q, i))
        o["d"] = d


def schedule(progs):
    ops, base = [], []
    for p in progs:
        links(p)
        base.append(len(ops))
        ops += p
    n = len(ops)
    rank = [r for r, p in enumerate(progs) for _ in p]
    dep, sends = [], {}
    for r, p in enumerate(progs):
        for i, o in enumerate(p):
            dep.append({base[r] + j: lat for j, lat in o["d"].items()})
            if o["k"] == "send":
                for d in o["to"]:
                    sends.setdefault((d, o["sem"]), []).append((base[r] + i, C["rstart"] + o["by"] / C["rrate"] + C["rhop"]))
    for i, o in enumerate(ops):
        if o["k"] == "land":
            for j, lat in sends[(rank[i], o["sem"])]:
                dep[i][j] = lat
    into = [list(d.items()) for d in dep]
    out = [[] for _ in range(n)]
    for i in range(n):
        for j, lat in into[i]:
            out[j].append((i, lat))
    left, last, way = [len(l) for l in out], [i for i in range(n) if not out[i]], [0.0] * n
    for i in last:
        way[i] = ops[i]["t"] + max([way[j] + lat for j, lat in out[i]] + [0.0])
        for j, _ in into[i]:
            left[j] -= 1
            if left[j] == 0:
                last.append(j)
    best = None
    for look in LOOKS:
        pri = way
        for _ in range(ROUNDS):
            end, seq, fin = arrange(ops, rank, into, out, pri, look)
            if best is None or end < best[0]:
                best = (end, seq)
            pri = arrange(ops, rank, out, into, fin, look)[2]
    return [[ops[i] for i in l] for l in best[1]]


def arrange(ops, rank, into, out, pri, look):
    n = len(ops)
    deg, ready, fin = [len(l) for l in into], [0.0] * n, [0.0] * n
    pool, free, dfree, first = {}, {}, [0.0] * N, set()
    res = [[] for _ in range(N)]

    def enter(j):
        pool.setdefault((rank[j], ops[j]["q0"]), []).append(j)

    def done(i, t):
        st = [(i, t)]
        while st:
            i, t = st.pop()
            fin[i] = t
            for j, lat in out[i]:
                ready[j] = max(ready[j], t + lat)
                deg[j] -= 1
                if deg[j] == 0:
                    if ops[j]["k"] == "land":
                        res[rank[j]].append(j)
                        st.append((j, ready[j]))
                    else:
                        enter(j)

    for i in range(n):
        if not into[i]:
            enter(i)
    while True:
        best = None
        for key, l in pool.items():
            if not l:
                continue
            f = free.get(key, 0.0)
            t0 = max(f, min(ready[i] for i in l))
            c = max((i for i in l if ready[i] <= t0), key=lambda i: (pri[i], -i))
            lim = t0 + ops[c]["t"] * look
            for i in l:
                if t0 < ready[i] < lim and pri[i] > pri[c] + (ready[i] - t0):
                    c, lim = i, ready[i]
            s = max(f, ready[c])
            if best is None or s < best[0]:
                best = (s, key, c)
        if best is None:
            break
        s, key, c = best
        pool[key].remove(c)
        o, r = ops[c], key[0]
        e = s + o["t"]
        if o["k"] == "send" and r not in first:
            first.add(r)
            e += C["first"]
        free[key] = e
        res[r].append(c)
        if o["k"] == "dma":
            dfree[r] = max(dfree[r], e + C["dlat"]) + o["by"] / C["drate"]
            e = dfree[r] + C["dlat"]
        done(c, e)
    return max(fin), res, fin


def program(g, q, T, topo):
    ops, cols = [], {}
    core = T.cores[q]
    V, P, S = g.vector, g.tensor, g.scalar
    NA = N - 1 - q
    AC = 3 * NA
    CT = RES + AC * 2
    Q1 = q + 1
    OFF = BIG - 8192.0 * q - 0.4375
    if q == 0:
        OFF = -0.4375
    cy = C["cyc"]

    def op(qq, fns, reads, writes, t, **kw):
        o = dict(k="op", q=qq, q0=qq, f=fns, r=reads, w=writes, t=t)
        o.update(kw)
        ops.append(o)

    def B(n, lo=0, hi=None, step=1):
        return (n, lo, SCRATCH[n][1][1] if hi is None else hi, step)

    def ap(r):
        if not isinstance(r, tuple):
            return r
        return T[r[0]][:, r[1]:r[2]] if r[3] == 1 else T[r[0]][:, r[1]:r[2]:r[3]]

    def wd(r):
        return (r[2] - r[1] + r[3] - 1) // r[3]

    def tv(n, f):
        return cy * max(64, n * f)

    def short(*rs):
        return all(SCRATCH[r[0]][2] in ("bfloat16", "uint16") for r in rs)

    def ts(o, i, s1, s2, op0, op1=None):
        rd = [i] + [s for s in (s1, s2) if isinstance(s, tuple)]
        t = tv(wd(o), 0.5 if short(o, i) else 1)
        if op1 is None:
            op("V", [lambda: V.tensor_scalar(ap(o), ap(i), ap(s1), None, op0)], rd, [o], t)
        else:
            op("V", [lambda: V.tensor_scalar(ap(o), ap(i), ap(s1), ap(s2), op0, op1)], rd, [o], t)

    def tt(o, a, b, f):
        op("V", [lambda: V.tensor_tensor(ap(o), ap(a), ap(b), f)], [a, b], [o], tv(wd(o), 1 if a[0] in PS or b[0] in PS else 2))

    def ttg(o, w, l, b, f):
        op("V", [lambda: V.tensor_tensor(ap(o), ap(w).indirect(ap(l)), ap(b), f)], [w, l, b], [o], 0.05 + cy * C["gg"] * wd(o))

    def cp(o, i):
        op("V", [lambda: V.tensor_copy(ap(o), ap(i))], [i], [o], tv(wd(o), 0.5 if short(o, i) else 1))

    def cpg(o, w, l, eng="V"):
        if eng == "V":
            op("V", [lambda: V.tensor_copy(ap(o), ap(w).indirect(ap(l)))], [w, l], [o], 0.05 + cy * C["gg"] * wd(o))
        else:
            op("S", [lambda: S.activation(ap(o), ap(w).indirect(ap(l)), AF.Copy)], [w, l], [o], 0.065 + cy * C["gg"] * wd(o))

    def sca(w, l, i):
        op("V", [lambda: V.tensor_copy(ap(w).indirect(ap(l)), ap(i))], [l, i], [w], 0.05 + cy * C["sg"] * wd(i), com=w[0])

    def scan(o, m, i, op0=A.add, op1=A.max, f=1):
        op("V", [lambda: V.tensor_tensor_scan(ap(o), ap(m), ap(i), 0.0, op0, op1)], [m, i], [o], tv(wd(o), f))

    def fill(o, c):
        op("V", [lambda: V.memset(ap(o), c)], [], [o], tv(wd(o), 0.5 if short(o) else 1))

    def act(o, i, scale=1.0, bias=None, func=AF.Identity):
        t = 0.06 + cy * wd(o)
        more = [x for x in (scale, bias) if isinstance(x, tuple)]
        if bias:
            op("S", [lambda: S.activation(ap(o), ap(i), func, bias=ap(bias), scale=ap(scale))], [i] + more, [o], t)
        elif more:
            op("S", [lambda: S.activation(ap(o), ap(i), func, scale=ap(scale))], [i] + more, [o], t)
        else:
            op("S", [lambda: S.activation(ap(o), ap(i), AF.Copy, scale=scale)], [i], [o], t)

    def iota(o, pat, base, ch):
        kw = {} if SCRATCH[o[0]][2] == "int32" else {"allow_small_or_imprecise_dtypes": True}
        op("G", [lambda: g.iota(ap(o), pat, base, ch, **kw)], [], [o], 0.13 + 2 * cy * wd(o))

    def aff(o, i, pat, cmp, base, ch, other=0.0):
        op("G", [lambda: g.affine_select(ap(o), ap(i), pat, cmp, other, base, ch)], [i], [o], 0.17 + 2 * cy * wd(o))

    def mm(o, lst, a=0, b=None):
        n = len(lst)
        part = list(enumerate(lst))[a:b]
        fns = [lambda k=k, l=l, r=r: P.matmul(ap(o), ap(l), ap(r), k == 0, k == n - 1) for k, (l, r) in part]
        t = sum(0.03 + cy * max(64, wd(r)) * (1 if short(r) else 4) for k, (l, r) in part)
        op("P", fns, [x for _, p in part for x in p], [o], t)

    def dma(qq, fns, reads, writes, by):
        op(qq, fns, reads, writes, C["dissue"] * len(fns), k="dma", q="D", by=by)

    def load(qq, dst, name):
        dma(qq, [lambda: (g.sync if qq == "Y" else g.scalar).dma_start(T[dst[0]][:, dst[1]:dst[2]], T[name][:, :])], [], [dst],
            128 * wd(dst) * (2 if short(dst) else 4))

    def col(name):
        if name not in cols:
            cols[name] = len(cols)
        k = cols[name]
        return B("cc", k, k + 1)

    def oh(k):
        return B("oh", k, k + 1)

    def M3(n, k):
        return B(n, 128 * k, 128 * k + 128)

    bk, idb = B("bk4"), B("idb")

    def quad(lname, src, s0, s1):
        return ([(idb, B("nm", 0, (s1 - s0) // 4))]
                + [(M3(lname, r), (src, s0 + r, s1, 4)) for r in range(4)])

    def unquad(ps, n, o):
        scan(B(o, 0, 4 * n), B("rq", 0, 4 * n), B(ps, 0, 4 * n))
        return B(o, 3, 4 * n, 4)

    def low(n):
        return (idb, B("nma", 0, n))

    def diag(ps, n, o):
        scan(B(o, 0, n), B("r16", 0, n), B(ps, 0, n))
        return B(o, 15, n, 16)

    load("Y", B("enw"), "en")
    load("S", B("bmr"), "bm")
    load("Y", B("sdw"), "sd")
    load("Y", B("csb", 0, 4096), "cs")
    load("Y", B("lsb", 0, 4096), "ls")
    iota(B("pi", 0, 1), [[0, 1]], 0, 1)
    iota(B("j16"), [[1, 16]], 0, 0)
    iota(B("jm"), [[0, 16], [1, 16]], 0, 0)
    iota(B("ci"), [[1, 16]], 0, 0)
    iota(B("mg4"), [[16, 8], [0, 16]], 0, 0)
    iota(B("mi"), [[1, 128]], 0, 0)
    iota(B("m4"), [[0, 28], [1, 4]], 0, 0)
    fill(B("one"), 1.0)
    fill(B("zz"), 0.0)
    for k, e in enumerate(ZF):
        w = B("win", 1024 * k, 1024 * k + 1024)
        if e == "V":
            fill(w, 0.0)
        elif e == "S":
            act(w, B("zz"))
        else:
            iota(w, [[0, 1024]], 0, 0)
    ts(B("pi", 1, 2), B("pi", 0, 1), 15, None, A.bitwise_and)
    ts(B("pi", 2, 3), B("pi", 0, 1), 2, 3, A.arith_shift_right, A.bitwise_and)
    cp(col("p"), B("pi", 0, 1))
    cp(col("o"), B("pi", 1, 2))
    cp(col("o4"), B("pi", 2, 3))
    tt(col("g16"), col("p"), col("o"), A.subtract)
    ts(B("oh"), B("j16"), col("o"), None, A.is_equal)
    ts(B("dm"), B("jm"), col("o"), None, A.is_equal)
    cp(B("jcl"), B("ci"))
    ts(bk, B("mg4"), col("g16"), None, A.is_equal)
    ts(idb, B("mi"), col("p"), None, A.is_equal)
    tt(B("s5", 0, 5), B("oh", 0, 5), B("oh", 5, 10), A.add)
    sc = B("s5", 4, 5)
    for k in (3, 2, 1, 0):
        act(col("s%d" % k), sc, 0.0625, B("s5", k, k + 1))
        sc = col("s%d" % k)
    ts(col("h9"), col("o"), 9.0, -0.5, A.is_le, A.mult)
    act(col("bi"), sc, 0.5, col("h9"))
    for t in range(3):
        act(col("n%d" % t), oh(6 + t), 16.0, oh(5 + t))
        act(col("m%d" % t), oh(7 + t), 256.0, col("n%d" % t))
        act(M3("bv", t), bk, col("m%d" % t))
    act(col("bA"), oh(15), float(q), oh(13))
    ts(col("bb"), col("o"), -16384.0, 32.0, A.mult, A.add)
    if q:
        act(B("nb"), bk, -1.0)
        aff(B("nt"), B("nb"), [[-1, 128]], A.is_gt, 0, 1)
        aff(B("nu"), B("nt"), [[-1, 128]], A.not_equal, 0, 1, -2048.0)
        ts(col("p1"), col("p"), 1.0, None, A.add)
        act(B("dp"), idb, col("p1"))
    act(B("lb4f"), B("zz", 0, 512))
    act(B("lb4"), B("zz", 0, 512))
    for r in range(4):
        act(B("lb4f", 129 * r, 128 * r + 128, 4), B("bk4", r, 128, 4))
        act(B("lb4", 129 * r, 128 * r + 128, 4), B("bk4", r, 128, 4))
    act(B("bkf"), bk)
    aff(M3("fz", 0), B("bkf"), [[0, 8], [-1, 16]], A.is_ge, 4, 0)
    aff(M3("fz", 1), B("bkf"), [[0, 8], [1, 16]], A.is_ge, -5, 0)
    iota(B("kt"), [[-32, 512]], 0, 0)
    iota(B("pl"), [[1, 16], [16, 16]], 0, 0)
    aff(M3("s89", 0), B("one"), [[0, 8], [-1, 16]], A.is_ge, 7, 0)
    aff(M3("s89", 1), B("one"), [[0, 8], [1, 16]], A.is_ge, -8, 0)
    for k in range(2):
        aff(M3("sel", k), M3("s89", 0), [[-16, 8], [-2, 16]], A.is_equal, -k, 1)
        aff(M3("sel", 2 + k), M3("s89", 1), [[-16, 8], [-2, 16]], A.is_equal, 16 - k, 1)
    if q:
        iota(B("k48", 0, Q1 * CT), [[0, CT], [CAP, Q1]], 0, 0)
        iota(B("trn", 0, CT), [[16, CT]], CAP * q - 2048, 0)
        act(B("k48", q, Q1 * CT, Q1), B("trn", 0, CT))
        act(B("br"), B("zz", 0, 384))
        for j in range(3):
            act(B("br", 129 * j + 10, 128 * j + 128, 16), B("bk4", 10 + j, 128, 16))
    if NA:
        iota(B("trd"), [[16, 32]], -1024, 1)
    ts(B("nm"), B("m4"), col("o4"), LOW, A.not_equal, A.mult)
    ts(B("rq"), B("m4"), 0.0, 2 * LOW, A.is_equal, A.mult)
    mi0, mi1, mh0, mb0, e7 = [B("iw", 16 * k, 16 * k + 16) for k in range(5)]
    ts(B("wi"), B("enw"), 12, 15, A.arith_shift_right, A.bitwise_and)
    ttg(B("gs"), B("wi"), B("jcl"), B("dm"), A.mult)
    mm(B("A0", 0, 256), [(bk, B("gs"))])
    ts(mi0, B("enw"), 3, 511, A.arith_shift_right, A.bitwise_and)
    cp(B("ofE", 0, 16), mi0)
    ts(e7, B("enw"), 7, None, A.bitwise_and)
    ts(B("ms"), B("A0", 0, 256), col("o"), None, A.is_equal)
    L = quad("lb4f", "gm", 0, 256)
    mm(B("E0", 0, 64), L, 0, 1)
    ttg(B("gm"), B("bmr"), B("ofE", 0, 16), B("ms"), A.mult)
    mm(B("E0", 0, 64), L, 1)
    ttg(B("ge"), B("enw"), B("jcl"), B("dm"), A.mult)
    ttg(B("gv"), B("sdw"), B("jcl"), B("dm"), A.mult)
    Z = [(M3("fz", 0), B("ge")), (M3("fz", 1), B("gv"))]
    mm(B("F0", 0, 256), Z, 0, 1)
    mm(B("F0", 0, 256), Z, 1, 2)
    ts(B("dg", 0, 256), B("F0", 0, 256), sc, col("bi"), A.mult, A.add)
    ts(B("dg", 256, 512), B("dg", 0, 256), 15, None, A.bitwise_and)
    ts(B("ki"), B("pl"), oh(14), col("bA"), A.mult, A.add)
    tt(B("z", 0, 256), B("dg", 256, 512), B("ki"), A.add)
    cp(mi1, unquad("E0", 16, "twE"))
    ts(mh0, mi1, 31, None, A.bitwise_and)
    ts(mb0, mi1, 5, None, A.arith_shift_right)
    tt(B("twE", 288, 304), mh0, e7, A.is_le)
    tt(B("twE", 320, 336), mb0, B("twE", 288, 304), A.add)
    cp(B("bnE", 0, 16), B("twE", 320, 336))
    act(B("psZ"), B("kt"), bias=col("bb"))
    ts(B("bmh"), B("bmr"), 31, None, A.bitwise_and)
    tt(B("F1"), B("psZ"), B("bmr"), A.add)
    act(B("t5"), B("bmh"), -5.0)
    tt(B("psZ"), B("F1"), B("t5"), A.add)
    act(B("hi"), B("psZ"))
    fill(B("csb", 4096, 4112), 0)
    fill(B("lsb", 4096, 4112), 0.0)
    if q:
        fill(B("rm", 0, Q1 * CT), 0.0)
        fill(B("rm", 0, Q1 * CT, Q1), -2 * LOW)
        fill(B("kx", 0, Q1 * CT), 0.0)
        fill(B("kx", q, Q1 * CT, Q1), 1.0)
        fill(B("ft"), 0.0)
        for x in "EFA" if NA else "E":
            fill(B("xf" + x), 0.0)
        for t in range(3):
            fill(B("sw%d" % t, 0, CAP * q), 0.0)
    tt(B("lo"), B("psZ"), B("hi"), A.subtract)
    mm(B("A1"), [(M3("sel", 0), B("hi")), (M3("sel", 2), B("lo"))])
    act(B("bmp", 0, 512), B("A1"), 0.03125)
    mm(B("psI"), [(M3("sel", 1), B("hi")), (M3("sel", 3), B("lo"))])
    act(B("bmp", 512, 1024), B("psI"), 0.03125)
    dma("Y", [lambda s=s: g.sync.dma_start(T.win[s::8, 1024 * s:1024 * s + 1024], T.bmp[s::8, :]) for s in range(8)],
        [B("bmp"), B("win")], [B("win")], 262144)
    wt = oh(4)
    for k in (3, 2, 1, 0):
        act(col("w%d" % k), wt, 16.0, oh(k))
        wt = col("w%d" % k)
    ts(col("f9"), col("o"), 10.0, None, A.is_ge)
    ts(col("e9"), col("o"), 12.0, col("f9"), A.is_le, A.mult)
    act(col("u1"), wt, 0.125, col("e9"))
    if q:
        act(col("cb"), oh(13), -BIG, col("u1"))
    act(B("lbe"), B("lb4"), col("cb" if q else "u1"))
    if NA:
        ts(B("nma"), B("jm", 0, 144), col("o"), LOW, A.not_equal, A.mult)
        ts(B("r16"), B("jm", 0, 144), 0.0, 2 * LOW, A.is_equal, A.mult)
        act(B("be"), bk, col("cb" if q else "u1"))
        act(col("u3"), oh(15), 256.0, oh(14))
        act(col("cid"), oh(13), -2048.0, col("u3"))
        act(B("lid"), B("lb4"), col("cid"))
    ts(col("o16"), col("o"), 16.0, None, A.mult)
    ts(B("prm"), B("ci"), col("o16"), None, A.add)
    if q:
        for n in ["ye%d" % s for s in range(q)] + ["yl"]:
            iota(B(n, 256 * q, 256 * q + 256), [[0, 256]], 0, 0)

    def tw(x, k, n):
        return B("tw" + x, 288 + 32 * k, 288 + 32 * k + n)

    def sg(t):
        return B("sg", 256 * t, 256 * t + 256)

    def vrep(x, t, s0, s1, copy):
        o = B(x + "1", 256, 256 + s1 - s0)
        mm(o, [(M3("bv", t), B("z", s0, s1))])
        if copy:
            act(B("vr" + x, 0, s1 - s0), o)

    def buckets(x, src):
        ts(B("of" + x, 0, wd(src)), src, 8191.0, 0.0, A.min, A.max)

    def sums(x, row, c0, c1, fresh):
        m = 16 * (c1 - c0)
        if fresh:
            return [low(m), (B("be"), B("z", 16 * c0, 16 * c1)), (bk, row)], m, 1
        if m > 144:
            return quad("lb4", row[0], 0, m), m // 4, 4
        return [low(m), (bk, row)], m, 1

    def wrapped(x, n, w):
        return unquad(x + "0", n, "tw" + x) if w < 16 * n else diag(x + "0", w, "tw" + x)

    def bins(x, c0, c1):
        n = c1 - c0
        m = 16 * n
        yy, bn = B("yy" + x, 0, m), B("bn" + x, 0, n)
        fresh = x == "A" and q
        L, w, late = sums(x, yy, c0, c1, fresh)
        mm(B(x + "0", 0, w), L, 0, len(L) - late)
        cpg(yy, B("win"), B("of" + x, 0, n), "S" if m > 64 and x != "A" else "V")
        mm(B(x + "0", 0, w), L, len(L) - late)
        s = wrapped(x, n, w)
        if fresh:
            ts(bn, s, OFF, 4096.0, A.add, A.min)
        else:
            tt(tw(x, 0, n), s, B("bl", c0, c1), A.add)
            ts(bn, tw(x, 0, n), 4096.0, 0.0, A.min, A.max)

    def tally(x, t, c0, c1):
        bn, o = B("bn" + x, 0, c1 - c0), B("tal", 16 * c0, 16 * c1)
        if x == "E":
            cpg(sg(t), B("csb"), bn, "S")
        elif x == "A":
            cpg(o, B("csb"), bn, "S")
        else:
            ttg(o, B("csb"), bn, o, A.add)

    def event(x, t, c0, c1):
        n, s0, s1 = c1 - c0, 16 * c0, 16 * c1
        m = 16 * n
        p0, p1, fresh = x + "0", x + "1", x == "A" or t == 0
        row, zr, bn, hit = B("xx" + x, 0, m), B("z", s0, s1), B("bn" + x, 0, n), B("in" + x, 0, m)
        ks, mp = B(p1, 0, m), B(p1, 256, 256 + m)
        if x == "E" and t:
            tally(x, t, c0, c1)
            tt(hit, sg(t), mp, A.is_le)
        else:
            ttg(hit, B("csb"), bn, B("vr" + x, 0, m), A.is_le)
        mm(ks, [(bk, hit)])
        L, w, late = sums(x, row, c0, c1, x == "A")
        if t == 0:
            L[1:1] = [(M3("lbe", r), ("z", r, m, 4)) for r in range(4)]
        mm(B(p0, 0, w), L, 0, len(L) - late)
        if t == 0:
            tally(x, t, c0, c1)
            ts(B("mk", 0, m), ks, col("o"), -0.125, A.is_equal, A.mult)
            ttg(row, B("lsb"), bn, B("mk", 0, m), A.mult)
        else:
            k = 256 * "EFA".index(x)
            gl = B("gl", k, k + m)
            cpg(gl, B("lsb"), bn, "S")
            if x != "E":
                tally(x, t, c0, c1)
            ts(mp, ks, col("o"), -0.125, A.is_equal, A.mult)
            tt(row, gl, mp, A.mult)
        mm(B(p0, 0, w), L, len(L) - late)
        en, off = wrapped(x, n, w), OFF
        if t == 0:
            ts(B("ofE", 0, RES), en, OFF, 8191.0, A.add, A.min)
        if q == 0 and fresh:
            ts(B("bl", c0, c1), en, OFF, -0.4375, A.add, A.max)
            return
        if not fresh:
            tt(tw(x, 1, n), en, B("bl", c0, c1), A.add)
            en, off = tw(x, 1, n), 0.0
        if q == 0:
            ts(B("bl", c0, c1), en, -0.4375, 0.0, A.max, A.add)
            return
        f0, a, b = 72 * t, c0 * Q1, c1 * Q1

        def thr(s):
            return 8192.0 * (s + 1 - q) - 0.5 - off

        def to(s):
            return B("ft", f0 + a + s, f0 + b, Q1)

        def under(s, lo, hi):
            return B("th", f0 + s * CT + lo, f0 + s * CT + hi) if s else B("ft", f0 + lo * Q1, f0 + hi * Q1, Q1)
        for s in range(q):
            ts(under(s, c0, c1), en, thr(s), None, A.is_lt)
        pl = B(p0, 0, b - a)
        L2 = [(idb, B("k48", a, b)), (B("dp"), B("kx", a, b)), (B("nu"), B("ft", f0 + a, f0 + b)), (bk, B("xf" + x, a, b))]
        mm(pl, L2, 0, 2)
        for s in range(q):
            scan(B("xf" + x, s, b, Q1), under(s, 0, c1), under(s - 1, 0, c1) if s else B("zz", 0, c1), A.add, A.subtract, 0.5)
        for s in range(1, q):
            tt(to(s), under(s, c0, c1), under(s - 1, c0, c1), A.subtract)
        mm(pl, L2, 2, 3)
        mm(pl, L2, 3)
        act(tw(x, 3, n), en, -16 * BIG, 16 * BIG * thr(q - 1), AF.Relu)
        if fresh:
            act(tw(x, 2, n), en, 1.0, off)
            en = tw(x, 2, n)
        tt(B("bl", c0, c1), en, tw(x, 3, n), A.add)
        scan(B("tw" + x, 448, 448 + b - a), B("rm", 0, b - a), pl, A.add, A.min)
        ts(B("of" + x, 32, 32 + n), B("tw" + x, 448 + q, 448 + b - a, Q1), 2047.0, None, A.add)
        k = 8 if m > 144 else n
        for i in range(0, n, k):
            o, h = B("psZ", 16 * i, 16 * (i + k)), B("z", s0 + 16 * i, s0 + 16 * (i + k))
            L3 = [(idb, h), (M3("br", t), B("xx" + x, 16 * i, 16 * (i + k)))]
            mm(o, L3, 0, 1)
            mm(o, L3, 1, 2)
            act(h, o)
        for i in range(0, n, k):
            sca(B("sw%d" % t, 0, CAP * q + 16 * CT + 128), B("of" + x, 32 + i, 32 + i + k), B("z", s0 + 16 * i, s0 + 16 * (i + k)))

    def split(s, kind):
        d = list(range(s))[::-1] if kind == "rx" else list(range(s + 1, N))[::-1]
        groups = {"rx": [[x] for x in d], "ri": [d]}.get(kind, [d[:2], d[2:]])
        return [list(zip(x, {1: (8,), 2: (4, 4), 3: (4, 2, 2)}[len(x)])) for x in groups if x]

    def width(s, d, kind):
        return [w for x in split(s, kind) for y, w in x if y == d][0]

    def send(src, dst, rsem):
        for call in split(q, rsem[:2]):
            sd = [(d, w, src(d, call[0][0]), dst(d, call[0][0])) for d, w in call]

            def go(sd=sd):
                e = topo.engines(core, T.cores[sd[0][0]])
                tr, pos = [], 0
                for d, w, a, b in sd:
                    rid, pid, _ = topo.addr(T.cores[d])
                    tr.append(RemoteDMATransfer(dst_ids=[DstId(rid=rid, pnc=pid)], remote_sem=T.sem[rsem], src=ap(a), dst=ap(b),
                                                dma_engine_mask=sum(1 << k for k in e[pos:pos + w])))
                    pos += w
                g.remote_dma_fused(tr, local_sem=T.sem.snt)
            op("G", [go], [x[2] for x in sd], [], C["rissue"], k="send", sem=rsem, to=[x[0] for x in sd],
               by=256 * sum(wd(x[2]) for x in sd), val=sum(x[1] for x in sd))

    def landed(sem, val, regs):
        op("R", [], [], regs, 0.0, k="land", sem=sem, val=val)

    def zcol(s, t, r):
        return 16 * (RES + 3 * (N - 1 - s) * t) + CAP * (r - s - 1)

    def places(n, out, k, ps, tmp):
        er = B("ert", 32 * k, 32 * k + n)
        tt(er, unquad(ps, n, tmp), B("trd", 0, n), A.min)
        ts(B(out, 0, n), er, 2048.0, None, A.add)

    for t in range(EV):
        if t < 3:
            if t == 2:
                buckets("E", tw("E", 1, RES))
            vrep("E", t, 0, 256, t == 0)
            if t:
                bins("E", 0, RES)
            event("E", t, 0, RES)
        if t == 2 and NA:
            buckets("F", B("bl", RES, RES + AC))
            vrep("F", t, 256, 256 + 16 * AC, True)
            bins("F", RES, RES + AC)
            event("F", t, RES, RES + AC)
        if t == 3 and NA:
            for a in (RES, RES + AC):
                buckets("F", tw("F", 1, AC) if a == RES else B("bl", a, a + AC))
                bins("F", a, a + AC)
                tally("F", t, a, a + AC)
                cp(B("er", 16 * (a - RES), 16 * (a - RES + AC)), B("tal", 16 * a, 16 * (a + AC)))
            w = 16 * (AC + 3)
            send(lambda d, m: B("er", CAP * (d - q - 1), CAP * (d - q - 1) + w), lambda d, m: B("le%d" % q, 0, w), "re%d" % q)
        if t and NA:
            c0 = RES + AC * (t - 1)
            c1 = c0 + AC
            zr = B("z", 16 * c0, 16 * c1)
            n = 16 * AC
            landed("rx%d" % (t - 1), sum(width(r, q, "rx") for r in range(q + 1, N)), [zr])
            U = [low(n), (B("be"), zr)]
            mm(B("A0", 0, n), U, 0, 1)
            mm(B("A0", 0, n), U, 1)
            if t < 3:
                vrep("A", t, 16 * c0, 16 * c1, True)
            ts(B("ofA", 0, AC), diag("A0", n, "twA"), OFF, 8191.0, A.add, A.min)
            if q == 0:
                ts(B("bl", c0, c1), B("twA", 15, n, 16), OFF, -0.4375, A.add, A.max)
            bins("A", c0, c1)
            if t < 3:
                event("A", t, c0, c1)
            else:
                mm(B("A1", 0, 4 * AC), quad("lid", "z", 16 * c0, 16 * c1))
                cpg(B("lr", AC, AC + n), B("csb"), B("bnA", 0, AC))
                places(AC, "lr", 1, "A1", "dqi")
                send(lambda d, m: B("lr", 0, AC + CAP * (m - q)), lambda d, m: B("ll%d" % q, 0, AC + CAP * (m - q)), "rl%d" % q)
        if t < 3 and q:
            send(lambda d, m: B("sw%d" % t, CAP * d, CAP * d + CAP), lambda d, m: B("z", zcol(d, t, q), zcol(d, t, q) + CAP), "rx%d" % t)
        if NA and t == 2:
            k = 2 * AC
            mm(B("psI", 0, 4 * k), quad("lid", "z", 256, 256 + 16 * k))
            places(k, "il", 0, "psI", "dqi")
            send(lambda d, m: B("il", 3 * (d - q - 1), 3 * (d - q - 1) + AC + 3), lambda d, m: B("li%d" % q, 0, AC + 3), "ri%d" % q)

    buckets("E", tw("E", 1, RES))
    bins("E", 0, RES)
    tally("E", 3, 0, RES)
    own = 256 * q

    def leave(h):
        lo, hi = 128 * h, 128 * h + 128
        dma("YS"[h], [lambda: (g.scalar if h else g.sync).dma_start(T.y[:, lo:hi], T.yo[:, lo:hi])], [B("yo", lo, hi)], [], 65536)

    out = B("ac" if q else "yo")
    cpg(out, sg(0), B("prm"), "S")
    for t in range(1, EV):
        ttg(out, sg(t), B("prm"), out, A.add)
    if q == 0:
        for h in range(2):
            leave(h)
    else:
        sm = B("psI", 0, 256)
        act(sm, out)
        for s in range(q - 1, -1, -1):
            n = 3 * (N - s)
            landed("ri%d" % s, width(s, q, "ri"), [B("li%d" % s)])
            landed("re%d" % s, width(s, q, "re"), [B("le%d" % s)])
            sca(B("ye%d" % s), B("li%d" % s, 0, n), B("le%d" % s, 0, 16 * n))
            tt(sm, sm, B("ye%d" % s, own, own + 256), A.add)
        for s in range(q - 1, -1, -1):
            a, n = 3 * (N - 1 - s), 3 * (q - s)
            landed("rl%d" % s, width(s, q, "rl"), [B("ll%d" % s)])
            sca(B("yl"), B("ll%d" % s, 0, n), B("ll%d" % s, a, a + 16 * n))
        for h in range(2):
            lo, hi = 128 * h, 128 * h + 128
            tt(B("yo", lo, hi), B("psI", lo, hi), B("yl", own + lo, own + hi), A.add)
            leave(h)
    return ops


def rank_program(g, core, T, topo):
    q = T.rank_of(core)
    if q is None:
        return
    order = schedule([program(g, r, T, topo) for r in range(N)])
    issue, finish = tracker(g, T)
    for o in order[q]:
        issue(o)
    finish()
